import numpy as np
import ml_dtypes


def mxq(x, axis, fmt="e4m3"):
    dtype, down = {"e4m3": (ml_dtypes.float8_e4m3fn, 7), "e5m2": (ml_dtypes.float8_e5m2, 14)}[fmt]
    v = np.moveaxis(np.asarray(x, np.float32).astype(ml_dtypes.bfloat16).astype(np.float64), axis, -1)
    blocks = v.reshape(v.shape[:-1] + (-1, 32))
    amax = np.abs(blocks).max(-1, keepdims=True)
    byte = np.maximum(np.where(amax > 0, np.frexp(amax)[1] - 1 + 127, 0) - down, 1)
    scale = np.exp2(byte - 127.0)
    codes = (blocks / scale).astype(np.float32).astype(dtype).astype(np.float64)
    return np.moveaxis((codes * scale).reshape(v.shape), -1, axis)


WIDE = False


def mx_kscale(k):
    if not WIDE:
        return np.ones(k)
    levels = np.array([10, -10, 5, -5, 0])
    if k % 512:
        return np.exp2(np.random.permutation(np.resize(levels, k // 32))).repeat(32)
    a = np.empty((k // 512, 16))
    for p in range(k // 512):
        a[p, :8] = np.random.permutation(np.resize(levels, 8))
        for g in range(8):
            far = levels[np.abs(levels - a[p, g]) >= 10]
            a[p, g + 8] = far[np.random.randint(len(far))]
    return np.exp2(a.ravel()).repeat(32)


def f64(x):
    return np.asarray(x).astype(np.float64)


def striped(idx):
    return np.tile(idx.reshape(-1, 16).T, (8, 1)).astype(np.uint16)


def unstriped(offs):
    return offs[:16].T.reshape(-1).astype(np.int64)


E2M1 = np.array([0.0, 0.5, 1.0, 1.5, 2.0, 3.0, 4.0, 6.0, -0.0, -0.5, -1.0, -1.5, -2.0, -3.0, -4.0, -6.0])


def pack_weight(w, fmt):
    k, n = w.shape
    w = f64(np.asarray(w, np.float32).astype(ml_dtypes.bfloat16)).reshape(k // 32, 32, n)
    amax = np.abs(w).max(1)
    if fmt == "e4m3":
        byte = np.frexp(amax)[1] - 1 + 127 - 7
    else:
        mant, ex = np.frexp(amax / 6.0)
        byte = np.where(mant > 0.5, ex, ex - 1) + 127
    byte = np.clip(np.where(amax > 0, byte, 1), 1, 254)
    scaled = (w * np.exp2(127.0 - byte)[:, None, :]).reshape(k, n).astype(np.float32)
    by_word = np.ascontiguousarray(scaled.reshape(k // 512, 128, 4, n).transpose(0, 1, 3, 2))
    if fmt == "e4m3":
        words = by_word.astype(ml_dtypes.float8_e4m3fn).view(np.uint8)
    else:
        c = by_word.astype(ml_dtypes.float4_e2m1fn).view(np.uint8) & 0xF
        words = (c[..., 0::2] | (c[..., 1::2] << 4)).reshape(k // 512, 128, 2 * n)
    return np.ascontiguousarray(words), np.ascontiguousarray(byte.astype(np.uint8).reshape(k // 512, 16, n))


def unpack_weight(words, scales, fmt):
    g, _, n = scales.shape
    words = np.ascontiguousarray(words).reshape(g, 128, n, -1)
    if fmt == "e4m3":
        vals = words.view(ml_dtypes.float8_e4m3fn).astype(np.float64)
    else:
        nib = np.empty((g, 128, n, 4), np.uint8)
        nib[..., 0::2] = words & 0xF
        nib[..., 1::2] = words >> 4
        vals = E2M1[nib]
    vals = vals * np.repeat(np.exp2(scales.astype(np.float64) - 127.0), 8, axis=1)[..., None]
    return vals.transpose(0, 1, 3, 2).reshape(g * 512, n)


def silu(v):
    return v / (1.0 + np.exp(-np.maximum(v, -700.0)))


K, T, E, C, N = 2560, 1280, 8, 128, 128
K8 = 1024


def by_expert(wq, xq):
    return np.concatenate([wq[e].T @ xq[:, e * C:(e + 1) * C] for e in range(E)], axis=1)


def setup_inputs():
    n = np.random.standard_normal
    s = mx_kscale(K)[:, None]
    w = n((E, K, N)) / np.sqrt(K) / s[None]
    w8 = [pack_weight(m[:K8], "e4m3") for m in w]
    w4 = [pack_weight(m[K8:], "e2m1") for m in w]
    return {
        "xT": (n((K, T)) * s).astype(np.float32),
        "w8_words": np.stack([m[0] for m in w8]),
        "w8_scales": np.stack([m[1] for m in w8]),
        "w4_words": np.stack([m[0] for m in w4]),
        "w4_scales": np.stack([m[1] for m in w4]),
        "b": (0.3 * n((N, E))).astype(np.float32),
        "gate": np.tile(np.random.uniform(0.2, 1.0, E * C), (N, 1)).astype(np.float32),
        "offs": striped(np.random.permutation(T)[:E * C]),
        "dst": striped(np.random.permutation(T)[:E * C]),
    }


def reference(xT, w8_words, w8_scales, w4_words, w4_scales, b, gate, offs, dst):
    idx = unstriped(offs)
    w = np.stack([np.concatenate([unpack_weight(w8_words[e], w8_scales[e], "e4m3"), unpack_weight(w4_words[e], w4_scales[e], "e2m1")]) for e in range(E)])
    xq = mxq(f64(xT)[:, idx], 0, "e4m3")
    y = by_expert(w, xq)
    y = silu(y + np.repeat(f64(b), C, axis=1))
    out = np.zeros((N, T))
    out[:, unstriped(dst)] = f64(gate) * y
    return out

@@ -1,0 +1,189 @@
+from contextlib import ExitStack
+
+import concourse.mybir as mybir
+
+K, T, E, C, N = 2560, 1280, 8, 128, 128
+S = E * C
+FLOPS = 2 * K * S * N
+
+F32 = mybir.dt.float32
+BF16 = mybir.dt.bfloat16
+I32 = mybir.dt.int32
+U32 = mybir.dt.uint32
+U16 = mybir.dt.uint16
+U8 = mybir.dt.uint8
+FP8X4 = mybir.dt.float8_e4m3fn_x4
+FP4X4 = mybir.dt.float4_e2m1fn_x4
+ACT = mybir.ActivationFunctionType
+MULT = mybir.AluOpType.mult
+
+P = 128
+PACK = 4
+K_PASS = P * PACK
+
+PASSES = (("e2m1", 0, 0, 0), ("e2m1", 1, 1, 0), ("e4m3", 0, 2, 4), ("e4m3", 1, 2, 8), ("e2m1", 2, 2, 0))
+QUANT = {0: ((0, 512), (512, 1024), (1024, 1280)), 1: ((0, 512), (512, 1024), (1024, 1280)), 2: ((0, 512), (512, 1024), (1024, 1280)), 3: ((0, 512), (512, 1024), (1024, 1280)), 4: ((0, 512), (512, 1024), (1024, 1280))}
+LOADS = {0: ((0, 512), (512, 1280)), 1: ((0, 512), (512, 1280)), 2: ((0, 1280),), 3: ((0, 1280),), 4: ((0, 1280),)}
+COPIES = {
+    0: (("S", 0, 512), ("V", 768, 1280), ("S", 512, 768)),
+    1: (("S", 0, 512), ("V", 1024, 1280), ("S", 512, 1024)),
+    2: (("V", 896, 1280), ("S", 0, 512), ("S", 512, 896)),
+    3: (("V", 896, 1280), ("S", 0, 512), ("S", 512, 896)),
+    4: (("V", 896, 1280), ("S", 0, 512), ("S", 512, 896)),
+}
+
+
+def tile_moe_two_lin_silu_kernel(
+    tc, xT, w8_words, w8_scales, w4_words, w4_scales, b, gate, offs, dst, out
+):
+    nc = tc.nc
+    last = len(PASSES) - 1
+    with ExitStack() as ctx:
+        keep = ctx.enter_context(tc.tile_pool(name="keep", bufs=1))
+        stage = ctx.enter_context(tc.tile_pool(name="stage", bufs=5))
+        psum = ctx.enter_context(tc.psum_pool(name="psum", bufs=1))
+
+        offs_sb = keep.tile([P, S // 16], U16, name="offs_sb")
+        dst_sb = keep.tile([P, S // 16], U16, name="dst_sb")
+        b_sb = keep.tile([P, E], F32, name="b_sb")
+        gate_sb = keep.tile([P, S], F32, name="gate_sb")
+        y_sb = keep.tile([P, S], F32, name="y_sb")
+        out_sb = keep.tile([P, T], F32, name="out_sb")
+        warm = keep.tile([P, 1], F32, name="warm")
+        raw = [keep.tile([P, PACK, T], F32, name=f"raw{i}") for i in range(len(PASSES))]
+        codes = [keep.tile([P, T], U32, name=f"codes{i}", align_bytes=64) for i in range(len(PASSES))]
+        planes = [keep.tile([P, T], U8, name=f"planes{i}", align_bytes=64) for i in range(3)]
+        slot_codes = [keep.tile([P, S], U32, name=f"slot_codes{i}", align_bytes=64) for i in range(len(PASSES))]
+        slot_planes = [keep.tile([P, S], U8, name=f"slot_planes{i}", align_bytes=64) for i in range(3)]
+        w8_sb = keep.tile([P, E * 2, 4 * N], U8, name="w8_sb", align_bytes=64)
+        w4_sb = keep.tile([P, E * 3, 2 * N], U8, name="w4_sb", align_bytes=64)
+        w8_plane = keep.tile([P, E * 2, N // 4], I32, name="w8_plane", align_bytes=64)
+        w4_plane = keep.tile([P, E * 3, N // 4], I32, name="w4_plane", align_bytes=64)
+        acc = [psum.tile([P, C], F32, name=f"acc{e}") for e in range(E)]
+
+        nc.vector.memset(w8_plane[:], 0)
+        nc.gpsimd.memset(w4_plane[:], 0)
+        for plane in planes:
+            nc.gpsimd.memset(plane[:].bitcast(I32), 0)
+        nc.vector.memset(out_sb[:], 0.0)
+        nc.vector.memset(warm[:], 0.0)
+        nc.scalar.activation(warm[:], warm[:], ACT.Silu)
+
+        def load_x(i, c0, c1):
+            fmt, a, sp, k0 = PASSES[i]
+            row = K_PASS * a + (0 if fmt == "e4m3" else 1024)
+            src = xT[row : row + K_PASS, :].rearrange("(p j) w -> p j w", j=PACK)
+            nc.sync.dma_start(out=raw[i][:, :, c0:c1], in_=src[:, :, c0:c1])
+
+        def load_w8(e0, e1, queue=None):
+            (queue or nc.sync).dma_start(
+                out=w8_sb[:, 2 * e0 : 2 * e1, :].bitcast(I32),
+                in_=w8_words[e0:e1].rearrange("e a p n r -> p (e a) (n r)").bitcast(I32),
+            )
+
+        def load_w4(e0, e1, queue=None):
+            (queue or nc.sync).dma_start(
+                out=w4_sb[:, 3 * e0 : 3 * e1, :].bitcast(I32),
+                in_=w4_words[e0:e1].rearrange("e a p n -> p (e a) n").bitcast(I32),
+            )
+
+        def load_scale_rows(tile, src):
+            rows = src.rearrange("e a q n -> q (e a) n").bitcast(I32)
+            for quad in range(4):
+                nc.sync.dma_start(out=tile[32 * quad : 32 * quad + 4], in_=rows[4 * quad : 4 * quad + 4])
+
+        def load_lists():
+            nc.sync.dma_start(offs_sb[:], offs)
+            nc.sync.dma_start(dst_sb[:], dst)
+
+        def load_gate(queue=None):
+            (queue or nc.sync).dma_start(out=gate_sb[:], in_=gate)
+
+        def load_b(queue):
+            queue.dma_start(out=b_sb[:], in_=b)
+
+        def load_pass(i):
+            for c0, c1 in LOADS[i]:
+                load_x(i, c0, c1)
+
+        load_pass(0)
+        load_lists()
+        load_b(nc.sync)
+        for i in range(1, len(PASSES)):
+            load_pass(i)
+        load_scale_rows(w4_plane, w4_scales)
+        load_w4(0, E)
+        load_scale_rows(w8_plane, w8_scales)
+        load_w8(0, E)
+        load_gate()
+
+        def interleave(engine, i, grouped, c0, c1):
+            dst_view = grouped[:, c0:c1, :].rearrange("p (c i) t -> p c t i", i=4)
+            src_view = raw[i][:, :, c0:c1].rearrange("p t (c i) -> p c t i", i=4)
+            if True:
+                dst_view, src_view = grouped[:, c0:c1, :], raw[i][:, :, c0:c1].rearrange("p j w -> p w j")
+            if engine == "S":
+                nc.scalar.activation(dst_view, src_view, ACT.Copy)
+            else:
+                nc.vector.tensor_copy(dst_view, src_view)
+
+        def quantize(i, grouped, c0, c1):
+            fmt, a, sp, k0 = PASSES[i]
+            nc.vector.quantize_mx(
+                out=codes[i][:, c0:c1].bitcast(FP8X4),
+                scales=planes[sp][k0:P, c0:c1],
+                in_=grouped[:, c0:c1, :].rearrange("p w j -> p (w j)"),
+            )
+
+        def gather_codes(i, s0, s1):
+            nc.vector.tensor_copy(slot_codes[i][:, s0:s1], codes[i][:].indirect(offs_sb[:, s0 // 16 : s1 // 16]))
+
+        def gather_planes(sp, s0, s1):
+            nc.vector.tensor_copy(slot_planes[sp][:, s0:s1], planes[sp][:].indirect(offs_sb[:, s0 // 16 : s1 // 16]))
+
+        def multiply(i, e):
+            fmt, a, sp, k0 = PASSES[i]
+            cols = slice(e * C, (e + 1) * C)
+            if fmt == "e4m3":
+                w, plane = w8_sb[:, 2 * e + a, :].bitcast(FP8X4), w8_plane[:, 2 * e + a, :]
+            else:
+                w, plane = w4_sb[:, 3 * e + a, :].bitcast(FP4X4), w4_plane[:, 3 * e + a, :]
+            nc.tensor.matmul_mx(
+                out=acc[e][:],
+                lhsT=w,
+                lhsT_scale=plane.bitcast(U8),
+                rhs=slot_codes[i][:, cols].bitcast(FP8X4),
+                rhs_scale=slot_planes[sp][k0:P, cols],
+                start=(i == 0),
+                stop=(i == last),
+            )
+
+        for i in range(len(PASSES)):
+            grouped = stage.tile([P, T, PACK], BF16, name="grouped", align_bytes=64)
+            for engine, c0, c1 in COPIES[i]:
+                interleave(engine, i, grouped, c0, c1)
+            for c0, c1 in QUANT[i]:
+                quantize(i, grouped, c0, c1)
+            if i < last:
+                gather_codes(i, 0, 512)
+                gather_codes(i, 512, 1024)
+            if i in (0, 1):
+                for s0 in (0, 512):
+                    gather_planes(i, s0, s0 + 512)
+            if i == 1:
+                for e in range(E):
+                    multiply(0, e)
+                    multiply(1, e)
+
+        for s in range(2):
+            gather_codes(last, s * 512, s * 512 + 512)
+            gather_planes(2, s * 512, s * 512 + 512)
+        for s in range(4):
+            for e in (2 * s, 2 * s + 1):
+                for i in range(2, last + 1):
+                    multiply(i, e)
+                nc.scalar.activation(y_sb[:, e * C : (e + 1) * C], acc[e][:], ACT.Silu, bias=b_sb[:, e : e + 1])
+        for s in range(2):
+            cols = slice(s * 512, s * 512 + 512)
+            nc.vector.tensor_tensor(out_sb[:].indirect(dst_sb[:, s * 32 : s * 32 + 32]), y_sb[:, cols], gate_sb[:, cols], MULT)
+        nc.sync.dma_start(out=out, in_=out_sb[:])

@@ -20,16 +20,17 @@ MULT = mybir.AluOpType.mult
 P = 128
 PACK = 4
 K_PASS = P * PACK
+SPARE = 256
 
-PASSES = (("e2m1", 0, 0, 0), ("e2m1", 1, 1, 0), ("e4m3", 0, 2, 4), ("e4m3", 1, 2, 8), ("e2m1", 2, 2, 0))
-QUANT = {0: ((0, 512), (512, 1024), (1024, 1280)), 1: ((0, 512), (512, 1024), (1024, 1280)), 2: ((0, 512), (512, 1024), (1024, 1280)), 3: ((0, 512), (512, 1024), (1024, 1280)), 4: ((0, 512), (512, 1024), (1024, 1280))}
-LOADS = {0: ((0, 512), (512, 1280)), 1: ((0, 512), (512, 1280)), 2: ((0, 1280),), 3: ((0, 1280),), 4: ((0, 1280),)}
+PASSES = (("e2m1", 0, 0, 0), ("e2m1", 1, 0, 4), ("e4m3", 0, 1, 4), ("e4m3", 1, 1, 8), ("e2m1", 2, 1, 0))
+QUANT = {0: ((0, 256), (256, 768), (768, 1280)), 1: ((0, 256), (256, 768), (768, 1280)), 2: ((0, 512), (512, 1024), (1024, 1280)), 3: ((0, 512), (512, 1024), (1024, 1280)), 4: ((0, 512), (512, 1024), (1024, 1280))}
+LOADS = {0: ((0, 256), (256, 768), (768, 1280)), 1: ((0, 256), (256, 768), (768, 1280)), 2: ((0, 640), (640, 1280)), 3: ((0, 640), (640, 1280)), 4: ((0, 512), (512, 1024), (1024, 1280))}
 COPIES = {
-    0: (("S", 0, 512), ("V", 768, 1280), ("S", 512, 768)),
-    1: (("S", 0, 512), ("V", 1024, 1280), ("S", 512, 1024)),
-    2: (("V", 896, 1280), ("S", 0, 512), ("S", 512, 896)),
-    3: (("V", 896, 1280), ("S", 0, 512), ("S", 512, 896)),
-    4: (("V", 896, 1280), ("S", 0, 512), ("S", 512, 896)),
+    0: (("S", 0, 256), ("V", 256, 768), ("S", 768, 1024), ("V", 1024, 1280)),
+    1: (("S", 0, 256), ("S", 256, 768), ("S", 768, 1152), ("V", 1152, 1280)),
+    2: (("S", 0, 640), ("S", 640, 1280)),
+    3: (("S", 0, 640), ("S", 640, 1088), ("V", 1088, 1280)),
+    4: (("S", 0, 512), ("S", 512, 1024), ("S", 1024, 1088), ("V", 1088, 1280)),
 }
 
 
@@ -41,22 +42,32 @@ def tile_moe_two_lin_silu_kernel(
     with ExitStack() as ctx:
         keep = ctx.enter_context(tc.tile_pool(name="keep", bufs=1))
         stage = ctx.enter_context(tc.tile_pool(name="stage", bufs=5))
+        reuse = ctx.enter_context(tc.tile_pool(name="reuse", bufs=1))
         psum = ctx.enter_context(tc.psum_pool(name="psum", bufs=1))
 
         offs_sb = keep.tile([P, S // 16], U16, name="offs_sb")
         dst_sb = keep.tile([P, S // 16], U16, name="dst_sb")
         b_sb = keep.tile([P, E], F32, name="b_sb")
-        gate_sb = keep.tile([P, S], F32, name="gate_sb")
         y_sb = keep.tile([P, S], F32, name="y_sb")
         out_sb = keep.tile([P, T], F32, name="out_sb")
         warm = keep.tile([P, 1], F32, name="warm")
-        raw = [keep.tile([P, PACK, T], F32, name=f"raw{i}") for i in range(len(PASSES))]
-        codes = [keep.tile([P, T], U32, name=f"codes{i}", align_bytes=64) for i in range(len(PASSES))]
-        planes = [keep.tile([P, T], U8, name=f"planes{i}", align_bytes=64) for i in range(3)]
+        raw = {}
+        for i in range(len(PASSES)):
+            for c0, c1 in LOADS[i]:
+                if i == 2:
+                    raw[i, c0] = reuse.tile([P, PACK, c1 - c0], F32, name=f"raw{i}_{c0}", offset=16 * c0)
+                else:
+                    raw[i, c0] = keep.tile([P, PACK, c1 - c0], F32, name=f"raw{i}_{c0}")
+        all_codes = keep.tile([P, len(PASSES) * T + SPARE], U32, name="all_codes", align_bytes=64)
+        codes = [all_codes[:, (last - i) * T : (last - i + 1) * T] for i in range(len(PASSES))]
+        windows = [all_codes[:, (last - i) * T : (last - i + 1) * T + SPARE] for i in range(len(PASSES))]
+        planes = [keep.tile([P, T + SPARE], U8, name=f"planes{i}", align_bytes=64) for i in range(2)]
         slot_codes = [keep.tile([P, S], U32, name=f"slot_codes{i}", align_bytes=64) for i in range(len(PASSES))]
-        slot_planes = [keep.tile([P, S], U8, name=f"slot_planes{i}", align_bytes=64) for i in range(3)]
-        w8_sb = keep.tile([P, E * 2, 4 * N], U8, name="w8_sb", align_bytes=64)
-        w4_sb = keep.tile([P, E * 3, 2 * N], U8, name="w4_sb", align_bytes=64)
+        slot_planes = [keep.tile([P, S], U8, name=f"slot_planes{i}", align_bytes=64) for i in range(2)]
+        moved = keep.tile([P, S], U8, name="moved", align_bytes=64)
+        w8_sb = reuse.tile([P, E * 2, 4 * N], U8, name="w8_sb", align_bytes=64, offset=0)
+        w4_sb = reuse.tile([P, E * 3, 2 * N], U8, name="w4_sb", align_bytes=64, offset=8192)
+        gate_sb = reuse.tile([P, S], F32, name="gate_sb", offset=14336)
         w8_plane = keep.tile([P, E * 2, N // 4], I32, name="w8_plane", align_bytes=64)
         w4_plane = keep.tile([P, E * 3, N // 4], I32, name="w4_plane", align_bytes=64)
         acc = [psum.tile([P, C], F32, name=f"acc{e}") for e in range(E)]
@@ -65,7 +76,9 @@ def tile_moe_two_lin_silu_kernel(
         nc.gpsimd.memset(w4_plane[:], 0)
         for plane in planes:
             nc.gpsimd.memset(plane[:].bitcast(I32), 0)
+        nc.gpsimd.memset(moved[:].bitcast(I32), 0)
         nc.vector.memset(out_sb[:], 0.0)
+        nc.vector.memset(all_codes[:, len(PASSES) * T :].bitcast(I32), 0)
         nc.vector.memset(warm[:], 0.0)
         nc.scalar.activation(warm[:], warm[:], ACT.Silu)
 
@@ -73,7 +86,7 @@ def tile_moe_two_lin_silu_kernel(
             fmt, a, sp, k0 = PASSES[i]
             row = K_PASS * a + (0 if fmt == "e4m3" else 1024)
             src = xT[row : row + K_PASS, :].rearrange("(p j) w -> p j w", j=PACK)
-            nc.sync.dma_start(out=raw[i][:, :, c0:c1], in_=src[:, :, c0:c1])
+            nc.sync.dma_start(out=raw[i, c0][:], in_=src[:, :, c0:c1])
 
         def load_w8(e0, e1, queue=None):
             (queue or nc.sync).dma_start(
@@ -87,17 +100,17 @@ def tile_moe_two_lin_silu_kernel(
                 in_=w4_words[e0:e1].rearrange("e a p n -> p (e a) n").bitcast(I32),
             )
 
-        def load_scale_rows(tile, src):
+        def load_scale_rows(tile, src, quads):
             rows = src.rearrange("e a q n -> q (e a) n").bitcast(I32)
-            for quad in range(4):
+            for quad in quads:
                 nc.sync.dma_start(out=tile[32 * quad : 32 * quad + 4], in_=rows[4 * quad : 4 * quad + 4])
 
         def load_lists():
             nc.sync.dma_start(offs_sb[:], offs)
             nc.sync.dma_start(dst_sb[:], dst)
 
-        def load_gate(queue=None):
-            (queue or nc.sync).dma_start(out=gate_sb[:], in_=gate)
+        def load_gate(e0, e1):
+            nc.sync.dma_start(out=gate_sb[:, e0 * C : e1 * C], in_=gate[:, e0 * C : e1 * C])
 
         def load_b(queue):
             queue.dma_start(out=b_sb[:], in_=b)
@@ -109,19 +122,17 @@ def tile_moe_two_lin_silu_kernel(
         load_pass(0)
         load_lists()
         load_b(nc.sync)
-        for i in range(1, len(PASSES)):
-            load_pass(i)
-        load_scale_rows(w4_plane, w4_scales)
-        load_w4(0, E)
-        load_scale_rows(w8_plane, w8_scales)
-        load_w8(0, E)
-        load_gate()
+        load_pass(1)
+        load_pass(2)
+        load_pass(3)
+        load_pass(4)
+        load_scale_rows(w4_plane, w4_scales, range(4))
+        load_scale_rows(w8_plane, w8_scales, range(4))
 
         def interleave(engine, i, grouped, c0, c1):
-            dst_view = grouped[:, c0:c1, :].rearrange("p (c i) t -> p c t i", i=4)
-            src_view = raw[i][:, :, c0:c1].rearrange("p t (c i) -> p c t i", i=4)
-            if True:
-                dst_view, src_view = grouped[:, c0:c1, :], raw[i][:, :, c0:c1].rearrange("p j w -> p w j")
+            dst_view = grouped[:, c0:c1, :].rearrange("p (c i) t -> p c t i", i=2)
+            l0 = max(a for a, z in LOADS[i] if a <= c0)
+            src_view = raw[i, l0][:, :, c0 - l0 : c1 - l0].rearrange("p t (c i) -> p c t i", i=2)
             if engine == "S":
                 nc.scalar.activation(dst_view, src_view, ACT.Copy)
             else:
@@ -136,7 +147,7 @@ def tile_moe_two_lin_silu_kernel(
             )
 
         def gather_codes(i, s0, s1):
-            nc.vector.tensor_copy(slot_codes[i][:, s0:s1], codes[i][:].indirect(offs_sb[:, s0 // 16 : s1 // 16]))
+            nc.vector.tensor_copy(slot_codes[i][:, s0:s1], windows[i].indirect(offs_sb[:, s0 // 16 : s1 // 16]))
 
         def gather_planes(sp, s0, s1):
             nc.vector.tensor_copy(slot_planes[sp][:, s0:s1], planes[sp][:].indirect(offs_sb[:, s0 // 16 : s1 // 16]))
@@ -153,7 +164,7 @@ def tile_moe_two_lin_silu_kernel(
                 lhsT=w,
                 lhsT_scale=plane.bitcast(U8),
                 rhs=slot_codes[i][:, cols].bitcast(FP8X4),
-                rhs_scale=slot_planes[sp][k0:P, cols],
+                rhs_scale=moved[:, cols] if i == 1 else slot_planes[sp][k0:P, cols],
                 start=(i == 0),
                 stop=(i == last),
             )
@@ -165,25 +176,29 @@ def tile_moe_two_lin_silu_kernel(
             for c0, c1 in QUANT[i]:
                 quantize(i, grouped, c0, c1)
             if i < last:
-                gather_codes(i, 0, 512)
-                gather_codes(i, 512, 1024)
-            if i in (0, 1):
-                for s0 in (0, 512):
-                    gather_planes(i, s0, s0 + 512)
+                gather_codes(i, 0, S)
+            if i == 2:
+                for g in range(4):
+                    load_w4(2 * g, 2 * g + 2)
+                    load_w8(2 * g, 2 * g + 2)
+                    if g % 2 == 0:
+                        load_gate(2 * g, 2 * g + 4)
             if i == 1:
-                for e in range(E):
-                    multiply(0, e)
-                    multiply(1, e)
+                gather_planes(0, 0, S)
+                for quad in range(4):
+                    nc.sync.dma_start(
+                        out=moved[32 * quad : 32 * quad + 4, :].bitcast(I32),
+                        in_=slot_planes[0][32 * quad + 4 : 32 * quad + 8, :].bitcast(I32),
+                    )
 
         for s in range(2):
             gather_codes(last, s * 512, s * 512 + 512)
-            gather_planes(2, s * 512, s * 512 + 512)
+            gather_planes(1, s * 512, s * 512 + 512)
         for s in range(4):
             for e in (2 * s, 2 * s + 1):
-                for i in range(2, last + 1):
+                for i in range(last + 1):
                     multiply(i, e)
                 nc.scalar.activation(y_sb[:, e * C : (e + 1) * C], acc[e][:], ACT.Silu, bias=b_sb[:, e : e + 1])
-        for s in range(2):
-            cols = slice(s * 512, s * 512 + 512)
-            nc.vector.tensor_tensor(out_sb[:].indirect(dst_sb[:, s * 32 : s * 32 + 32]), y_sb[:, cols], gate_sb[:, cols], MULT)
+            cols = slice(s * 256, s * 256 + 256)
+            nc.vector.tensor_tensor(out_sb[:].indirect(dst_sb[:, s * 16 : s * 16 + 16]), y_sb[:, cols], gate_sb[:, cols], MULT)
         nc.sync.dma_start(out=out, in_=out_sb[:])

@@ -1,6 +1,7 @@
 from contextlib import ExitStack
 
 import concourse.mybir as mybir
+from concourse.masks import make_identity
 
 K, T, E, C, N = 2560, 1280, 8, 128, 128
 S = E * C
@@ -23,14 +24,14 @@ K_PASS = P * PACK
 SPARE = 256
 
 PASSES = (("e2m1", 0, 0, 0), ("e2m1", 1, 0, 4), ("e4m3", 0, 1, 4), ("e4m3", 1, 1, 8), ("e2m1", 2, 1, 0))
-QUANT = {0: ((0, 256), (256, 768), (768, 1280)), 1: ((0, 256), (256, 768), (768, 1280)), 2: ((0, 512), (512, 1024), (1024, 1280)), 3: ((0, 512), (512, 1024), (1024, 1280)), 4: ((0, 512), (512, 1024), (1024, 1280))}
-LOADS = {0: ((0, 256), (256, 768), (768, 1280)), 1: ((0, 256), (256, 768), (768, 1280)), 2: ((0, 640), (640, 1280)), 3: ((0, 640), (640, 1280)), 4: ((0, 512), (512, 1024), (1024, 1280))}
+QUANT = {i: ((0, 512), (512, 1024), (1024, 1280)) for i in range(5)}
+LOADS = {0: ((0, 1280),), 1: ((0, 1280),), 2: ((0, 640), (640, 1280)), 3: ((0, 640), (640, 1280)), 4: ((0, 640), (640, 1280))}
 COPIES = {
-    0: (("S", 0, 256), ("V", 256, 768), ("S", 768, 1024), ("V", 1024, 1280)),
-    1: (("S", 0, 256), ("S", 256, 768), ("S", 768, 1152), ("V", 1152, 1280)),
-    2: (("S", 0, 640), ("S", 640, 1280)),
-    3: (("S", 0, 640), ("S", 640, 1088), ("V", 1088, 1280)),
-    4: (("S", 0, 512), ("S", 512, 1024), ("S", 1024, 1088), ("V", 1088, 1280)),
+    0: (("S", 0, 512), ("V", 640, 1280), ("S", 512, 640)),
+    1: (("S", 0, 512), ("V", 640, 1280), ("S", 512, 640)),
+    2: (("S", 0, 512), ("S", 512, 640), ("S", 640, 1024), ("V", 1152, 1280), ("S", 1024, 1152)),
+    3: (("S", 0, 512), ("S", 512, 640), ("V", 1024, 1280), ("S", 640, 1024)),
+    4: (("S", 0, 512), ("S", 512, 640), ("V", 960, 1280), ("S", 640, 960)),
 }
 
 
@@ -54,8 +55,8 @@ def tile_moe_two_lin_silu_kernel(
         raw = {}
         for i in range(len(PASSES)):
             for c0, c1 in LOADS[i]:
-                if i == 2:
-                    raw[i, c0] = reuse.tile([P, PACK, c1 - c0], F32, name=f"raw{i}_{c0}", offset=16 * c0)
+                if (i, c0) in ((2, 640), (3, 0)):
+                    raw[i, c0] = reuse.tile([P, PACK, c1 - c0], F32, name=f"raw{i}_{c0}", offset=10240 * (i - 2))
                 else:
                     raw[i, c0] = keep.tile([P, PACK, c1 - c0], F32, name=f"raw{i}_{c0}")
         all_codes = keep.tile([P, len(PASSES) * T + SPARE], U32, name="all_codes", align_bytes=64)
@@ -65,13 +66,15 @@ def tile_moe_two_lin_silu_kernel(
         slot_codes = [keep.tile([P, S], U32, name=f"slot_codes{i}", align_bytes=64) for i in range(len(PASSES))]
         slot_planes = [keep.tile([P, S], U8, name=f"slot_planes{i}", align_bytes=64) for i in range(2)]
         moved = keep.tile([P, S], U8, name="moved", align_bytes=64)
-        w8_sb = reuse.tile([P, E * 2, 4 * N], U8, name="w8_sb", align_bytes=64, offset=0)
-        w4_sb = reuse.tile([P, E * 3, 2 * N], U8, name="w4_sb", align_bytes=64, offset=8192)
-        gate_sb = reuse.tile([P, S], F32, name="gate_sb", offset=14336)
+        w8_sb = [reuse.tile([P, 4, 4 * N], U8, name=f"w8_sb{g}", align_bytes=64, offset=10240 * (g // 2) + 3584 * (g % 2)) for g in range(4)]
+        w4_sb = [reuse.tile([P, 6, 2 * N], U8, name=f"w4_sb{g}", align_bytes=64, offset=10240 * (g // 2) + 3584 * (g % 2) + 2048) for g in range(4)]
+        gate_sb = keep.tile([P, S], F32, name="gate_sb")
+        ident = keep.tile([P, P], F32, name="ident")
+        gate_cols = keep.tile([P, E], F32, name="gate_cols")
         w8_plane = keep.tile([P, E * 2, N // 4], I32, name="w8_plane", align_bytes=64)
         w4_plane = keep.tile([P, E * 3, N // 4], I32, name="w4_plane", align_bytes=64)
-        acc = [psum.tile([P, C], F32, name=f"acc{e}") for e in range(E)]
 
+        make_identity(nc, ident[:])
         nc.vector.memset(w8_plane[:], 0)
         nc.gpsimd.memset(w4_plane[:], 0)
         for plane in planes:
@@ -90,13 +93,13 @@ def tile_moe_two_lin_silu_kernel(
 
         def load_w8(e0, e1, queue=None):
             (queue or nc.sync).dma_start(
-                out=w8_sb[:, 2 * e0 : 2 * e1, :].bitcast(I32),
+                out=w8_sb[e0 // 2][:].bitcast(I32),
                 in_=w8_words[e0:e1].rearrange("e a p n r -> p (e a) (n r)").bitcast(I32),
             )
 
         def load_w4(e0, e1, queue=None):
             (queue or nc.sync).dma_start(
-                out=w4_sb[:, 3 * e0 : 3 * e1, :].bitcast(I32),
+                out=w4_sb[e0 // 2][:].bitcast(I32),
                 in_=w4_words[e0:e1].rearrange("e a p n -> p (e a) n").bitcast(I32),
             )
 
@@ -109,8 +112,17 @@ def tile_moe_two_lin_silu_kernel(
             nc.sync.dma_start(offs_sb[:], offs)
             nc.sync.dma_start(dst_sb[:], dst)
 
-        def load_gate(e0, e1):
-            nc.sync.dma_start(out=gate_sb[:, e0 * C : e1 * C], in_=gate[:, e0 * C : e1 * C])
+        def spread_gate():
+            nc.sync.dma_start(out=gate_cols[:], in_=gate[0:1, :].rearrange("o (p i) -> (o p) i", i=8))
+            for half in range(2):
+                spread = psum.tile([P, 4, P], F32, name="spread", tag=f"bank{half}")
+                for q in range(4):
+                    i = 4 * half + q
+                    nc.tensor.transpose(spread[:, q, :], gate_cols[:, i : i + 1].to_broadcast([P, P]), ident[:])
+                nc.vector.tensor_copy(
+                    gate_sb[:].rearrange("m (p i) -> m p i", i=8)[:, :, 4 * half : 4 * half + 4],
+                    spread[:].rearrange("m q p -> m p q"),
+                )
 
         def load_b(queue):
             queue.dma_start(out=b_sb[:], in_=b)
@@ -119,6 +131,8 @@ def tile_moe_two_lin_silu_kernel(
             for c0, c1 in LOADS[i]:
                 load_x(i, c0, c1)
 
+        spread_gate()
+        acc = [psum.tile([P, C], F32, name=f"acc{e}", tag=f"bank{e}") for e in range(E)]
         load_pass(0)
         load_lists()
         load_b(nc.sync)
@@ -156,9 +170,9 @@ def tile_moe_two_lin_silu_kernel(
             fmt, a, sp, k0 = PASSES[i]
             cols = slice(e * C, (e + 1) * C)
             if fmt == "e4m3":
-                w, plane = w8_sb[:, 2 * e + a, :].bitcast(FP8X4), w8_plane[:, 2 * e + a, :]
+                w, plane = w8_sb[e // 2][:, 2 * (e % 2) + a, :].bitcast(FP8X4), w8_plane[:, 2 * e + a, :]
             else:
-                w, plane = w4_sb[:, 3 * e + a, :].bitcast(FP4X4), w4_plane[:, 3 * e + a, :]
+                w, plane = w4_sb[e // 2][:, 3 * (e % 2) + a, :].bitcast(FP4X4), w4_plane[:, 3 * e + a, :]
             nc.tensor.matmul_mx(
                 out=acc[e][:],
                 lhsT=w,
@@ -166,7 +180,7 @@ def tile_moe_two_lin_silu_kernel(
                 rhs=slot_codes[i][:, cols].bitcast(FP8X4),
                 rhs_scale=moved[:, cols] if i == 1 else slot_planes[sp][k0:P, cols],
                 start=(i == 0),
-                stop=(i == last),
+                stop=(i == 3),
             )
 
         for i in range(len(PASSES)):
@@ -177,12 +191,10 @@ def tile_moe_two_lin_silu_kernel(
                 quantize(i, grouped, c0, c1)
             if i < last:
                 gather_codes(i, 0, S)
-            if i == 2:
-                for g in range(4):
+            if i in (2, 3):
+                for g in (2 * i - 4, 2 * i - 3):
                     load_w4(2 * g, 2 * g + 2)
                     load_w8(2 * g, 2 * g + 2)
-                    if g % 2 == 0:
-                        load_gate(2 * g, 2 * g + 4)
             if i == 1:
                 gather_planes(0, 0, S)
                 for quad in range(4):
@@ -196,7 +208,10 @@ def tile_moe_two_lin_silu_kernel(
             gather_planes(1, s * 512, s * 512 + 512)
         for s in range(4):
             for e in (2 * s, 2 * s + 1):
-                for i in range(last + 1):
+                for i in (0, 1, 4):
+                    multiply(i, e)
+            for e in (2 * s, 2 * s + 1):
+                for i in (2, 3):
                     multiply(i, e)
                 nc.scalar.activation(y_sb[:, e * C : (e + 1) * C], acc[e][:], ACT.Silu, bias=b_sb[:, e : e + 1])
             cols = slice(s * 256, s * 256 + 256)

@@ -25,13 +25,13 @@ SPARE = 256
 
 PASSES = (("e2m1", 0, 0, 0), ("e2m1", 1, 0, 4), ("e4m3", 0, 1, 4), ("e4m3", 1, 1, 8), ("e2m1", 2, 1, 0))
 QUANT = {i: ((0, 512), (512, 1024), (1024, 1280)) for i in range(5)}
-LOADS = {0: ((0, 1280),), 1: ((0, 1280),), 2: ((0, 640), (640, 1280)), 3: ((0, 640), (640, 1280)), 4: ((0, 640), (640, 1280))}
+LOADS = {0: ((0, 1280),), 1: ((0, 640), (640, 1280)), 2: ((0, 640), (640, 1280)), 3: ((0, 640), (640, 1280)), 4: ((0, 512), (512, 1024), (1024, 1280))}
 COPIES = {
     0: (("S", 0, 512), ("V", 640, 1280), ("S", 512, 640)),
-    1: (("S", 0, 512), ("V", 640, 1280), ("S", 512, 640)),
-    2: (("S", 0, 512), ("S", 512, 640), ("S", 640, 1024), ("V", 1152, 1280), ("S", 1024, 1152)),
+    1: (("S", 0, 512), ("S", 512, 640), ("S", 640, 1024), ("V", 1152, 1280), ("S", 1024, 1152)),
+    2: (("S", 0, 512), ("S", 512, 640), ("S", 640, 1024), ("S", 1024, 1280)),
     3: (("S", 0, 512), ("S", 512, 640), ("V", 1024, 1280), ("S", 640, 1024)),
-    4: (("S", 0, 512), ("S", 512, 640), ("V", 960, 1280), ("S", 640, 960)),
+    4: (("S", 0, 512), ("V", 896, 1024), ("S", 512, 896), ("V", 1152, 1280), ("S", 1024, 1152)),
 }
 
 
@@ -150,7 +150,7 @@ def tile_moe_two_lin_silu_kernel(
             if engine == "S":
                 nc.scalar.activation(dst_view, src_view, ACT.Copy)
             else:
-                nc.vector.tensor_copy(dst_view, src_view)
+                nc.vector.tensor_copy(grouped[:, c0:c1, :], raw[i, l0][:, :, c0 - l0 : c1 - l0].rearrange("p t c -> p c t"))
 
         def quantize(i, grouped, c0, c1):
             fmt, a, sp, k0 = PASSES[i]

@@ -27,11 +27,11 @@ PASSES = (("e2m1", 0, 0, 0), ("e2m1", 1, 0, 4), ("e4m3", 0, 1, 4), ("e4m3", 1, 1
 QUANT = {i: ((0, 512), (512, 1024), (1024, 1280)) for i in range(5)}
 LOADS = {0: ((0, 1280),), 1: ((0, 640), (640, 1280)), 2: ((0, 640), (640, 1280)), 3: ((0, 640), (640, 1280)), 4: ((0, 512), (512, 1024), (1024, 1280))}
 COPIES = {
-    0: (("S", 0, 512), ("V", 640, 1280), ("S", 512, 640)),
-    1: (("S", 0, 512), ("S", 512, 640), ("S", 640, 1024), ("V", 1152, 1280), ("S", 1024, 1152)),
-    2: (("S", 0, 512), ("S", 512, 640), ("S", 640, 1024), ("S", 1024, 1280)),
+    0: (("S", 0, 512), ("V", 512, 1280)),
+    1: (("S", 0, 512), ("S", 512, 640), ("V", 1024, 1280), ("S", 640, 1024)),
+    2: (("S", 0, 512), ("S", 512, 640), ("S", 640, 1024), ("V", 1152, 1280), ("S", 1024, 1152)),
     3: (("S", 0, 512), ("S", 512, 640), ("V", 1024, 1280), ("S", 640, 1024)),
-    4: (("S", 0, 512), ("V", 896, 1024), ("S", 512, 896), ("V", 1152, 1280), ("S", 1024, 1152)),
+    4: (("V", 384, 512), ("S", 0, 384), ("V", 896, 1024), ("S", 512, 896), ("V", 1152, 1280), ("S", 1024, 1152)),
 }
 
 
@@ -106,7 +106,7 @@ def tile_moe_two_lin_silu_kernel(
         def load_scale_rows(tile, src, quads):
             rows = src.rearrange("e a q n -> q (e a) n").bitcast(I32)
             for quad in quads:
-                nc.sync.dma_start(out=tile[32 * quad : 32 * quad + 4], in_=rows[4 * quad : 4 * quad + 4])
+                nc.sync.dma_start(out=tile[quad:P:32], in_=rows[quad:16:4])
 
         def load_lists():
             nc.sync.dma_start(offs_sb[:], offs)
@@ -199,8 +199,8 @@ def tile_moe_two_lin_silu_kernel(
                 gather_planes(0, 0, S)
                 for quad in range(4):
                     nc.sync.dma_start(
-                        out=moved[32 * quad : 32 * quad + 4, :].bitcast(I32),
-                        in_=slot_planes[0][32 * quad + 4 : 32 * quad + 8, :].bitcast(I32),
+                        out=moved[quad:P:32, :].bitcast(I32),
+                        in_=slot_planes[0][4 + quad : P : 32, :].bitcast(I32),
                     )
 
         for s in range(2):

@@ -4,6 +4,7 @@ import concourse.mybir as mybir
 from concourse.masks import make_identity
 
 K, T, E, C, N = 2560, 1280, 8, 128, 128
+K8 = 1024
 S = E * C
 FLOPS = 2 * K * S * N
 
@@ -21,28 +22,32 @@ MULT = mybir.AluOpType.mult
 P = 128
 PACK = 4
 K_PASS = P * PACK
+A8, A4 = 2, 3
+PAIRS = E // 2
 SPARE = 256
 
 PASSES = (("e2m1", 0, 0, 0), ("e2m1", 1, 0, 4), ("e4m3", 0, 1, 4), ("e4m3", 1, 1, 8), ("e2m1", 2, 1, 0))
-QUANT = {i: ((0, 512), (512, 1024), (1024, 1280)) for i in range(5)}
-LOADS = {0: ((0, 1280),), 1: ((0, 640), (640, 1280)), 2: ((0, 640), (640, 1280)), 3: ((0, 640), (640, 1280)), 4: ((0, 512), (512, 1024), (1024, 1280))}
-COPIES = {
-    0: (("S", 0, 512), ("V", 512, 1280)),
-    1: (("S", 0, 512), ("S", 512, 640), ("V", 1024, 1280), ("S", 640, 1024)),
-    2: (("S", 0, 512), ("S", 512, 640), ("S", 640, 1024), ("V", 1152, 1280), ("S", 1024, 1152)),
-    3: (("S", 0, 512), ("S", 512, 640), ("V", 1024, 1280), ("S", 640, 1024)),
-    4: (("V", 384, 512), ("S", 0, 384), ("V", 896, 1024), ("S", 512, 896), ("V", 1152, 1280), ("S", 1024, 1152)),
-}
+MOVED, LAST = 1, 4
+E2M1_PASSES, E4M3_PASSES = (0, 1, 4), (2, 3)
+
+QUANT = ((0, 512), (512, 1024), (1024, T))
+HALVES = ((0, T // 2), (T // 2, T))
+LOADS = (((0, T),), HALVES, HALVES, HALVES, QUANT)
+
+VECTOR_SHARE = ((768,), (0, 256), (0, 0), (0, 256), (0, 128, 128))
+
+REUSED = ((2, T // 2), (3, 0))
+LOAD_BYTES = PACK * (T // 2) * 4
+W8_BYTES, W4_BYTES = 2 * A8 * 4 * N, 2 * A4 * 2 * N
 
 
 def tile_moe_two_lin_silu_kernel(
     tc, xT, w8_words, w8_scales, w4_words, w4_scales, b, gate, offs, dst, out
 ):
     nc = tc.nc
-    last = len(PASSES) - 1
     with ExitStack() as ctx:
         keep = ctx.enter_context(tc.tile_pool(name="keep", bufs=1))
-        stage = ctx.enter_context(tc.tile_pool(name="stage", bufs=5))
+        stage = ctx.enter_context(tc.tile_pool(name="stage", bufs=len(PASSES)))
         reuse = ctx.enter_context(tc.tile_pool(name="reuse", bufs=1))
         psum = ctx.enter_context(tc.psum_pool(name="psum", bufs=1))
 
@@ -51,169 +56,172 @@ def tile_moe_two_lin_silu_kernel(
         b_sb = keep.tile([P, E], F32, name="b_sb")
         y_sb = keep.tile([P, S], F32, name="y_sb")
         out_sb = keep.tile([P, T], F32, name="out_sb")
-        warm = keep.tile([P, 1], F32, name="warm")
         raw = {}
         for i in range(len(PASSES)):
             for c0, c1 in LOADS[i]:
-                if (i, c0) in ((2, 640), (3, 0)):
-                    raw[i, c0] = reuse.tile([P, PACK, c1 - c0], F32, name=f"raw{i}_{c0}", offset=10240 * (i - 2))
+                if (i, c0) in REUSED:
+                    offset = LOAD_BYTES * REUSED.index((i, c0))
+                    raw[i, c0] = reuse.tile([P, PACK, c1 - c0], F32, name=f"raw{i}_{c0}", offset=offset)
                 else:
                     raw[i, c0] = keep.tile([P, PACK, c1 - c0], F32, name=f"raw{i}_{c0}")
         all_codes = keep.tile([P, len(PASSES) * T + SPARE], U32, name="all_codes", align_bytes=64)
-        codes = [all_codes[:, (last - i) * T : (last - i + 1) * T] for i in range(len(PASSES))]
-        windows = [all_codes[:, (last - i) * T : (last - i + 1) * T + SPARE] for i in range(len(PASSES))]
+        codes = [all_codes[:, (LAST - i) * T : (LAST - i + 1) * T] for i in range(len(PASSES))]
+        windows = [all_codes[:, (LAST - i) * T : (LAST - i + 1) * T + SPARE] for i in range(len(PASSES))]
         planes = [keep.tile([P, T + SPARE], U8, name=f"planes{i}", align_bytes=64) for i in range(2)]
         slot_codes = [keep.tile([P, S], U32, name=f"slot_codes{i}", align_bytes=64) for i in range(len(PASSES))]
         slot_planes = [keep.tile([P, S], U8, name=f"slot_planes{i}", align_bytes=64) for i in range(2)]
-        moved = keep.tile([P, S], U8, name="moved", align_bytes=64)
-        w8_sb = [reuse.tile([P, 4, 4 * N], U8, name=f"w8_sb{g}", align_bytes=64, offset=10240 * (g // 2) + 3584 * (g % 2)) for g in range(4)]
-        w4_sb = [reuse.tile([P, 6, 2 * N], U8, name=f"w4_sb{g}", align_bytes=64, offset=10240 * (g // 2) + 3584 * (g % 2) + 2048) for g in range(4)]
+        moved_plane = keep.tile([P, S], U8, name="moved_plane", align_bytes=64)
+        pair_offset = [LOAD_BYTES * (g // 2) + (W8_BYTES + W4_BYTES) * (g % 2) for g in range(PAIRS)]
+        w8_sb = [
+            reuse.tile([P, 2 * A8, 4 * N], U8, name=f"w8_sb{g}", align_bytes=64, offset=pair_offset[g])
+            for g in range(PAIRS)
+        ]
+        w4_sb = [
+            reuse.tile([P, 2 * A4, 2 * N], U8, name=f"w4_sb{g}", align_bytes=64, offset=pair_offset[g] + W8_BYTES)
+            for g in range(PAIRS)
+        ]
         gate_sb = keep.tile([P, S], F32, name="gate_sb")
         ident = keep.tile([P, P], F32, name="ident")
-        gate_cols = keep.tile([P, E], F32, name="gate_cols")
-        w8_plane = keep.tile([P, E * 2, N // 4], I32, name="w8_plane", align_bytes=64)
-        w4_plane = keep.tile([P, E * 3, N // 4], I32, name="w4_plane", align_bytes=64)
+        gate_row = keep.tile([P, S // P], F32, name="gate_row")
+        w8_plane = keep.tile([P, E * A8, N // 4], I32, name="w8_plane", align_bytes=64)
+        w4_plane = keep.tile([P, E * A4, N // 4], I32, name="w4_plane", align_bytes=64)
 
         make_identity(nc, ident[:])
         nc.vector.memset(w8_plane[:], 0)
         nc.gpsimd.memset(w4_plane[:], 0)
         for plane in planes:
             nc.gpsimd.memset(plane[:].bitcast(I32), 0)
-        nc.gpsimd.memset(moved[:].bitcast(I32), 0)
+        nc.gpsimd.memset(moved_plane[:].bitcast(I32), 0)
         nc.vector.memset(out_sb[:], 0.0)
         nc.vector.memset(all_codes[:, len(PASSES) * T :].bitcast(I32), 0)
-        nc.vector.memset(warm[:], 0.0)
-        nc.scalar.activation(warm[:], warm[:], ACT.Silu)
-
-        def load_x(i, c0, c1):
-            fmt, a, sp, k0 = PASSES[i]
-            row = K_PASS * a + (0 if fmt == "e4m3" else 1024)
-            src = xT[row : row + K_PASS, :].rearrange("(p j) w -> p j w", j=PACK)
-            nc.sync.dma_start(out=raw[i, c0][:], in_=src[:, :, c0:c1])
-
-        def load_w8(e0, e1, queue=None):
-            (queue or nc.sync).dma_start(
-                out=w8_sb[e0 // 2][:].bitcast(I32),
-                in_=w8_words[e0:e1].rearrange("e a p n r -> p (e a) (n r)").bitcast(I32),
-            )
-
-        def load_w4(e0, e1, queue=None):
-            (queue or nc.sync).dma_start(
-                out=w4_sb[e0 // 2][:].bitcast(I32),
-                in_=w4_words[e0:e1].rearrange("e a p n -> p (e a) n").bitcast(I32),
-            )
-
-        def load_scale_rows(tile, src, quads):
-            rows = src.rearrange("e a q n -> q (e a) n").bitcast(I32)
-            for quad in quads:
-                nc.sync.dma_start(out=tile[quad:P:32], in_=rows[quad:16:4])
-
-        def load_lists():
-            nc.sync.dma_start(offs_sb[:], offs)
-            nc.sync.dma_start(dst_sb[:], dst)
 
         def spread_gate():
-            nc.sync.dma_start(out=gate_cols[:], in_=gate[0:1, :].rearrange("o (p i) -> (o p) i", i=8))
+            nc.sync.dma_start(out=gate_row[:], in_=gate[0:1, :].rearrange("o (p i) -> (o p) i", i=S // P))
             for half in range(2):
                 spread = psum.tile([P, 4, P], F32, name="spread", tag=f"bank{half}")
                 for q in range(4):
                     i = 4 * half + q
-                    nc.tensor.transpose(spread[:, q, :], gate_cols[:, i : i + 1].to_broadcast([P, P]), ident[:])
+                    nc.tensor.transpose(spread[:, q, :], gate_row[:, i : i + 1].to_broadcast([P, P]), ident[:])
                 nc.vector.tensor_copy(
-                    gate_sb[:].rearrange("m (p i) -> m p i", i=8)[:, :, 4 * half : 4 * half + 4],
+                    gate_sb[:].rearrange("m (p i) -> m p i", i=S // P)[:, :, 4 * half : 4 * half + 4],
                     spread[:].rearrange("m q p -> m p q"),
                 )
 
-        def load_b(queue):
-            queue.dma_start(out=b_sb[:], in_=b)
-
         def load_pass(i):
+            fmt, a, tile_no, first = PASSES[i]
+            row = K_PASS * a + (0 if fmt == "e4m3" else K8)
+            src = xT[row : row + K_PASS, :].rearrange("(p t) c -> p t c", t=PACK)
             for c0, c1 in LOADS[i]:
-                load_x(i, c0, c1)
+                nc.sync.dma_start(out=raw[i, c0][:], in_=src[:, :, c0:c1])
 
-        spread_gate()
-        acc = [psum.tile([P, C], F32, name=f"acc{e}", tag=f"bank{e}") for e in range(E)]
-        load_pass(0)
-        load_lists()
-        load_b(nc.sync)
-        load_pass(1)
-        load_pass(2)
-        load_pass(3)
-        load_pass(4)
-        load_scale_rows(w4_plane, w4_scales, range(4))
-        load_scale_rows(w8_plane, w8_scales, range(4))
+        def load_scale_rows(plane, scales):
+            rows = scales.rearrange("e a q n -> q (e a) n").bitcast(I32)
+            for r in range(4):
+                nc.sync.dma_start(out=plane[32 * r : 32 * r + 4], in_=rows[4 * r : 4 * r + 4])
 
-        def interleave(engine, i, grouped, c0, c1):
-            dst_view = grouped[:, c0:c1, :].rearrange("p (c i) t -> p c t i", i=2)
-            l0 = max(a for a, z in LOADS[i] if a <= c0)
-            src_view = raw[i, l0][:, :, c0 - l0 : c1 - l0].rearrange("p t (c i) -> p c t i", i=2)
-            if engine == "S":
-                nc.scalar.activation(dst_view, src_view, ACT.Copy)
-            else:
-                nc.vector.tensor_copy(grouped[:, c0:c1, :], raw[i, l0][:, :, c0 - l0 : c1 - l0].rearrange("p t c -> p c t"))
-
-        def quantize(i, grouped, c0, c1):
-            fmt, a, sp, k0 = PASSES[i]
-            nc.vector.quantize_mx(
-                out=codes[i][:, c0:c1].bitcast(FP8X4),
-                scales=planes[sp][k0:P, c0:c1],
-                in_=grouped[:, c0:c1, :].rearrange("p w j -> p (w j)"),
+        def load_weights(g):
+            nc.sync.dma_start(
+                out=w4_sb[g][:].bitcast(I32),
+                in_=w4_words[2 * g : 2 * g + 2].rearrange("e a p n -> p (e a) n").bitcast(I32),
             )
+            nc.sync.dma_start(
+                out=w8_sb[g][:].bitcast(I32),
+                in_=w8_words[2 * g : 2 * g + 2].rearrange("e a p n r -> p (e a) (n r)").bitcast(I32),
+            )
+
+        def pair_views(i, grouped, l0, c0, c1):
+            return (
+                grouped[:, c0:c1, :].rearrange("p (c i) t -> p c t i", i=2),
+                raw[i, l0][:, :, c0 - l0 : c1 - l0].rearrange("p t (c i) -> p c t i", i=2),
+            )
+
+        def interleave(i, grouped):
+            for (l0, l1), share in zip(LOADS[i], VECTOR_SHARE[i]):
+                split = l1 - share
+                if share:
+                    nc.vector.tensor_copy(*pair_views(i, grouped, l0, split, l1))
+                cuts = [l0] + [c1 for c0, c1 in QUANT if l0 < c1 < split] + [split]
+                for c0, c1 in zip(cuts, cuts[1:]):
+                    nc.scalar.activation(*pair_views(i, grouped, l0, c0, c1), ACT.Copy)
+
+        def quantize(i, grouped):
+            fmt, a, tile_no, first = PASSES[i]
+            for c0, c1 in QUANT:
+                nc.vector.quantize_mx(
+                    out=codes[i][:, c0:c1].bitcast(FP8X4),
+                    scales=planes[tile_no][first:P, c0:c1],
+                    in_=grouped[:, c0:c1, :].rearrange("p c t -> p (c t)"),
+                )
 
         def gather_codes(i, s0, s1):
             nc.vector.tensor_copy(slot_codes[i][:, s0:s1], windows[i].indirect(offs_sb[:, s0 // 16 : s1 // 16]))
 
-        def gather_planes(sp, s0, s1):
-            nc.vector.tensor_copy(slot_planes[sp][:, s0:s1], planes[sp][:].indirect(offs_sb[:, s0 // 16 : s1 // 16]))
+        def gather_planes(tile_no, s0, s1):
+            window = planes[tile_no][:].indirect(offs_sb[:, s0 // 16 : s1 // 16])
+            nc.vector.tensor_copy(slot_planes[tile_no][:, s0:s1], window)
+
+        def move_plane():
+            fmt, a, tile_no, first = PASSES[MOVED]
+            for r in range(4):
+                nc.sync.dma_start(
+                    out=moved_plane[32 * r : 32 * r + 4, :].bitcast(I32),
+                    in_=slot_planes[tile_no][32 * r + first : 32 * r + first + 4, :].bitcast(I32),
+                )
 
         def multiply(i, e):
-            fmt, a, sp, k0 = PASSES[i]
+            fmt, a, tile_no, first = PASSES[i]
             cols = slice(e * C, (e + 1) * C)
             if fmt == "e4m3":
-                w, plane = w8_sb[e // 2][:, 2 * (e % 2) + a, :].bitcast(FP8X4), w8_plane[:, 2 * e + a, :]
+                words, plane = w8_sb[e // 2][:, A8 * (e % 2) + a, :].bitcast(FP8X4), w8_plane[:, A8 * e + a, :]
             else:
-                w, plane = w4_sb[e // 2][:, 3 * (e % 2) + a, :].bitcast(FP4X4), w4_plane[:, 3 * e + a, :]
+                words, plane = w4_sb[e // 2][:, A4 * (e % 2) + a, :].bitcast(FP4X4), w4_plane[:, A4 * e + a, :]
             nc.tensor.matmul_mx(
                 out=acc[e][:],
-                lhsT=w,
+                lhsT=words,
                 lhsT_scale=plane.bitcast(U8),
                 rhs=slot_codes[i][:, cols].bitcast(FP8X4),
-                rhs_scale=moved[:, cols] if i == 1 else slot_planes[sp][k0:P, cols],
-                start=(i == 0),
-                stop=(i == 3),
+                rhs_scale=moved_plane[:, cols] if i == MOVED else slot_planes[tile_no][first:P, cols],
+                start=(i == E2M1_PASSES[0]),
+                stop=(i == E4M3_PASSES[-1]),
             )
+
+        spread_gate()
+        acc = [psum.tile([P, C], F32, name=f"acc{e}", tag=f"bank{e}") for e in range(E)]
+        load_pass(0)
+        nc.sync.dma_start(offs_sb[:], offs)
+        nc.sync.dma_start(dst_sb[:], dst)
+        nc.sync.dma_start(out=b_sb[:], in_=b)
+        for i in range(1, len(PASSES)):
+            load_pass(i)
+        load_scale_rows(w4_plane, w4_scales)
+        load_scale_rows(w8_plane, w8_scales)
 
         for i in range(len(PASSES)):
             grouped = stage.tile([P, T, PACK], BF16, name="grouped", align_bytes=64)
-            for engine, c0, c1 in COPIES[i]:
-                interleave(engine, i, grouped, c0, c1)
-            for c0, c1 in QUANT[i]:
-                quantize(i, grouped, c0, c1)
-            if i < last:
+            interleave(i, grouped)
+            quantize(i, grouped)
+            if i < LAST:
                 gather_codes(i, 0, S)
-            if i in (2, 3):
-                for g in (2 * i - 4, 2 * i - 3):
-                    load_w4(2 * g, 2 * g + 2)
-                    load_w8(2 * g, 2 * g + 2)
-            if i == 1:
-                gather_planes(0, 0, S)
-                for quad in range(4):
-                    nc.sync.dma_start(
-                        out=moved[quad:P:32, :].bitcast(I32),
-                        in_=slot_planes[0][4 + quad : P : 32, :].bitcast(I32),
-                    )
+            for h, (reused_pass, c0) in enumerate(REUSED):
+                if i == reused_pass:
+                    load_weights(2 * h)
+                    load_weights(2 * h + 1)
+            if i == MOVED:
+                gather_planes(PASSES[MOVED][2], 0, S)
+                move_plane()
 
-        for s in range(2):
-            gather_codes(last, s * 512, s * 512 + 512)
-            gather_planes(1, s * 512, s * 512 + 512)
-        for s in range(4):
-            for e in (2 * s, 2 * s + 1):
-                for i in (0, 1, 4):
+        for s0 in (0, S // 2):
+            gather_codes(LAST, s0, s0 + S // 2)
+            gather_planes(PASSES[LAST][2], s0, s0 + S // 2)
+        for g in range(PAIRS):
+            for e in (2 * g, 2 * g + 1):
+                for i in E2M1_PASSES:
                     multiply(i, e)
-            for e in (2 * s, 2 * s + 1):
-                for i in (2, 3):
+            for e in (2 * g, 2 * g + 1):
+                for i in E4M3_PASSES:
                     multiply(i, e)
                 nc.scalar.activation(y_sb[:, e * C : (e + 1) * C], acc[e][:], ACT.Silu, bias=b_sb[:, e : e + 1])
-            cols = slice(s * 256, s * 256 + 256)
-            nc.vector.tensor_tensor(out_sb[:].indirect(dst_sb[:, s * 16 : s * 16 + 16]), y_sb[:, cols], gate_sb[:, cols], MULT)
+            cols = slice(2 * g * C, 2 * (g + 1) * C)
+            places = out_sb[:].indirect(dst_sb[:, cols.start // 16 : cols.stop // 16])
+            nc.vector.tensor_tensor(places, y_sb[:, cols], gate_sb[:, cols], MULT)
         nc.sync.dma_start(out=out, in_=out_sb[:])

@@ -36,9 +36,9 @@ LOADS = (((0, T),), HALVES, HALVES, HALVES, QUANT)
 
 VECTOR_SHARE = ((768,), (0, 256), (0, 0), (0, 256), (0, 128, 128))
 
-REUSED = ((2, T // 2), (3, 0))
-LOAD_BYTES = PACK * (T // 2) * 4
-W8_BYTES, W4_BYTES = 2 * A8 * 4 * N, 2 * A4 * 2 * N
+W8_FIRST = 8
+W4_LOADS = ((0, 2), (2, 4), (4, 8))
+W8_LOADS = ((0, 4), (4, 6), (6, 8))
 
 
 def tile_moe_two_lin_silu_kernel(
@@ -47,8 +47,7 @@ def tile_moe_two_lin_silu_kernel(
     nc = tc.nc
     with ExitStack() as ctx:
         keep = ctx.enter_context(tc.tile_pool(name="keep", bufs=1))
-        stage = ctx.enter_context(tc.tile_pool(name="stage", bufs=len(PASSES)))
-        reuse = ctx.enter_context(tc.tile_pool(name="reuse", bufs=1))
+        stage = ctx.enter_context(tc.tile_pool(name="stage", bufs=4))
         psum = ctx.enter_context(tc.psum_pool(name="psum", bufs=1))
 
         offs_sb = keep.tile([P, S // 16], U16, name="offs_sb")
@@ -59,11 +58,7 @@ def tile_moe_two_lin_silu_kernel(
         raw = {}
         for i in range(len(PASSES)):
             for c0, c1 in LOADS[i]:
-                if (i, c0) in REUSED:
-                    offset = LOAD_BYTES * REUSED.index((i, c0))
-                    raw[i, c0] = reuse.tile([P, PACK, c1 - c0], F32, name=f"raw{i}_{c0}", offset=offset)
-                else:
-                    raw[i, c0] = keep.tile([P, PACK, c1 - c0], F32, name=f"raw{i}_{c0}")
+                raw[i, c0] = keep.tile([P, PACK, c1 - c0], F32, name=f"raw{i}_{c0}")
         all_codes = keep.tile([P, len(PASSES) * T + SPARE], U32, name="all_codes", align_bytes=64)
         codes = [all_codes[:, (LAST - i) * T : (LAST - i + 1) * T] for i in range(len(PASSES))]
         windows = [all_codes[:, (LAST - i) * T : (LAST - i + 1) * T + SPARE] for i in range(len(PASSES))]
@@ -71,15 +66,8 @@ def tile_moe_two_lin_silu_kernel(
         slot_codes = [keep.tile([P, S], U32, name=f"slot_codes{i}", align_bytes=64) for i in range(len(PASSES))]
         slot_planes = [keep.tile([P, S], U8, name=f"slot_planes{i}", align_bytes=64) for i in range(2)]
         moved_plane = keep.tile([P, S], U8, name="moved_plane", align_bytes=64)
-        pair_offset = [LOAD_BYTES * (g // 2) + (W8_BYTES + W4_BYTES) * (g % 2) for g in range(PAIRS)]
-        w8_sb = [
-            reuse.tile([P, 2 * A8, 4 * N], U8, name=f"w8_sb{g}", align_bytes=64, offset=pair_offset[g])
-            for g in range(PAIRS)
-        ]
-        w4_sb = [
-            reuse.tile([P, 2 * A4, 2 * N], U8, name=f"w4_sb{g}", align_bytes=64, offset=pair_offset[g] + W8_BYTES)
-            for g in range(PAIRS)
-        ]
+        w8_sb = [keep.tile([P, (e1 - e0) * A8, 4 * N], U8, name=f"w8_sb{e0}", align_bytes=64) for e0, e1 in W8_LOADS]
+        w4_sb = [keep.tile([P, (e1 - e0) * A4, 2 * N], U8, name=f"w4_sb{e0}", align_bytes=64) for e0, e1 in W4_LOADS]
         gate_sb = keep.tile([P, S], F32, name="gate_sb")
         ident = keep.tile([P, P], F32, name="ident")
         gate_row = keep.tile([P, S // P], F32, name="gate_row")
@@ -114,20 +102,24 @@ def tile_moe_two_lin_silu_kernel(
             for c0, c1 in LOADS[i]:
                 nc.sync.dma_start(out=raw[i, c0][:], in_=src[:, :, c0:c1])
 
-        def load_scale_rows(plane, scales):
+        def load_scale_rows(plane, scales, first):
             rows = scales.rearrange("e a q n -> q (e a) n").bitcast(I32)
             for r in range(4):
-                nc.sync.dma_start(out=plane[32 * r : 32 * r + 4], in_=rows[4 * r : 4 * r + 4])
+                nc.sync.dma_start(out=plane[first + r : P : 32], in_=rows[r:16:4])
 
-        def load_weights(g):
-            nc.sync.dma_start(
-                out=w4_sb[g][:].bitcast(I32),
-                in_=w4_words[2 * g : 2 * g + 2].rearrange("e a p n -> p (e a) n").bitcast(I32),
-            )
-            nc.sync.dma_start(
-                out=w8_sb[g][:].bitcast(I32),
-                in_=w8_words[2 * g : 2 * g + 2].rearrange("e a p n r -> p (e a) (n r)").bitcast(I32),
-            )
+        def load_w4(j):
+            e0, e1 = W4_LOADS[j]
+            rows = w4_words[e0:e1].rearrange("e a p n -> p (e a) n")
+            nc.sync.dma_start(out=w4_sb[j][:].bitcast(I32), in_=rows.bitcast(I32))
+
+        def load_w8(j):
+            e0, e1 = W8_LOADS[j]
+            rows = w8_words[e0:e1].rearrange("e a p n r -> p (e a) (n r)")
+            nc.sync.dma_start(out=w8_sb[j][:].bitcast(I32), in_=rows.bitcast(I32))
+
+        def words_of(tiles, loads, passes, e, a):
+            j = [e0 <= e < e1 for e0, e1 in loads].index(True)
+            return tiles[j][:, passes * (e - loads[j][0]) + a, :]
 
         def pair_views(i, grouped, l0, c0, c1):
             return (
@@ -163,7 +155,7 @@ def tile_moe_two_lin_silu_kernel(
         def move_plane():
             fmt, a, tile_no, first = PASSES[MOVED]
             for r in range(4):
-                nc.sync.dma_start(
+                nc.gpsimd.dma_start(
                     out=moved_plane[32 * r : 32 * r + 4, :].bitcast(I32),
                     in_=slot_planes[tile_no][32 * r + first : 32 * r + first + 4, :].bitcast(I32),
                 )
@@ -172,9 +164,9 @@ def tile_moe_two_lin_silu_kernel(
             fmt, a, tile_no, first = PASSES[i]
             cols = slice(e * C, (e + 1) * C)
             if fmt == "e4m3":
-                words, plane = w8_sb[e // 2][:, A8 * (e % 2) + a, :].bitcast(FP8X4), w8_plane[:, A8 * e + a, :]
+                words, plane = words_of(w8_sb, W8_LOADS, A8, e, a).bitcast(FP8X4), w8_plane[W8_FIRST:P, A8 * e + a, :]
             else:
-                words, plane = w4_sb[e // 2][:, A4 * (e % 2) + a, :].bitcast(FP4X4), w4_plane[:, A4 * e + a, :]
+                words, plane = words_of(w4_sb, W4_LOADS, A4, e, a).bitcast(FP4X4), w4_plane[:, A4 * e + a, :]
             nc.tensor.matmul_mx(
                 out=acc[e][:],
                 lhsT=words,
@@ -193,22 +185,24 @@ def tile_moe_two_lin_silu_kernel(
         nc.sync.dma_start(out=b_sb[:], in_=b)
         for i in range(1, len(PASSES)):
             load_pass(i)
-        load_scale_rows(w4_plane, w4_scales)
-        load_scale_rows(w8_plane, w8_scales)
+        load_w4(0)
+        load_scale_rows(w4_plane, w4_scales, 0)
+        load_w8(0)
+        load_scale_rows(w8_plane, w8_scales, W8_FIRST)
+        load_w4(1)
+        load_w4(2)
+        load_w8(1)
+        load_w8(2)
 
         for i in range(len(PASSES)):
             grouped = stage.tile([P, T, PACK], BF16, name="grouped", align_bytes=64)
             interleave(i, grouped)
             quantize(i, grouped)
-            if i < LAST:
-                gather_codes(i, 0, S)
-            for h, (reused_pass, c0) in enumerate(REUSED):
-                if i == reused_pass:
-                    load_weights(2 * h)
-                    load_weights(2 * h + 1)
             if i == MOVED:
                 gather_planes(PASSES[MOVED][2], 0, S)
                 move_plane()
+            if i < LAST:
+                gather_codes(i, 0, S)
 
         for s0 in (0, S // 2):
             gather_codes(LAST, s0, s0 + S // 2)

@@ -32,13 +32,13 @@ E2M1_PASSES, E4M3_PASSES = (0, 1, 4), (2, 3)
 
 QUANT = ((0, 512), (512, 1024), (1024, T))
 HALVES = ((0, T // 2), (T // 2, T))
-LOADS = (((0, T),), HALVES, HALVES, HALVES, QUANT)
+LOADS = (((0, T),), ((0, T),), HALVES, HALVES, QUANT)
 
-VECTOR_SHARE = ((768,), (0, 256), (0, 0), (0, 256), (0, 128, 128))
+VECTOR_SHARE = ((640,), (576,), (0, 0), (0, 128), (0, 128, 128))
 
 W8_FIRST = 8
-W4_LOADS = ((0, 2), (2, 4), (4, 8))
-W8_LOADS = ((0, 4), (4, 6), (6, 8))
+W4_LOADS = ((0, 2), (2, 4), (4, 6), (6, 8))
+W8_LOADS = W4_LOADS
 
 
 def tile_moe_two_lin_silu_kernel(
@@ -84,13 +84,12 @@ def tile_moe_two_lin_silu_kernel(
         nc.vector.memset(all_codes[:, len(PASSES) * T :].bitcast(I32), 0)
 
         def spread_gate():
-            nc.sync.dma_start(out=gate_row[:], in_=gate[0:1, :].rearrange("o (p i) -> (o p) i", i=S // P))
             for half in range(2):
-                spread = psum.tile([P, 4, P], F32, name="spread", tag=f"bank{half}")
+                spread = psum.tile([P, 4, P], F32, name="spread", tag=f"bank{E - 2 + half}")
                 for q in range(4):
                     i = 4 * half + q
                     nc.tensor.transpose(spread[:, q, :], gate_row[:, i : i + 1].to_broadcast([P, P]), ident[:])
-                nc.vector.tensor_copy(
+                nc.scalar.copy(
                     gate_sb[:].rearrange("m (p i) -> m p i", i=S // P)[:, :, 4 * half : 4 * half + 4],
                     spread[:].rearrange("m q p -> m p q"),
                 )
@@ -123,8 +122,8 @@ def tile_moe_two_lin_silu_kernel(
 
         def pair_views(i, grouped, l0, c0, c1):
             return (
-                grouped[:, c0:c1, :].rearrange("p (c i) t -> p c t i", i=2),
-                raw[i, l0][:, :, c0 - l0 : c1 - l0].rearrange("p t (c i) -> p c t i", i=2),
+                grouped[:, c0:c1, :].rearrange("p (c i) t -> p c t i", i=4),
+                raw[i, l0][:, :, c0 - l0 : c1 - l0].rearrange("p t (c i) -> p c t i", i=4),
             )
 
         def interleave(i, grouped):
@@ -177,22 +176,20 @@ def tile_moe_two_lin_silu_kernel(
                 stop=(i == E4M3_PASSES[-1]),
             )
 
-        spread_gate()
-        acc = [psum.tile([P, C], F32, name=f"acc{e}", tag=f"bank{e}") for e in range(E)]
         load_pass(0)
         nc.sync.dma_start(offs_sb[:], offs)
-        nc.sync.dma_start(dst_sb[:], dst)
-        nc.sync.dma_start(out=b_sb[:], in_=b)
         for i in range(1, len(PASSES)):
             load_pass(i)
+        nc.sync.dma_start(out=gate_row[:], in_=gate[0:1, :].rearrange("o (p i) -> (o p) i", i=S // P))
         load_w4(0)
         load_scale_rows(w4_plane, w4_scales, 0)
         load_w8(0)
         load_scale_rows(w8_plane, w8_scales, W8_FIRST)
-        load_w4(1)
-        load_w4(2)
-        load_w8(1)
-        load_w8(2)
+        nc.sync.dma_start(out=b_sb[:], in_=b)
+        nc.sync.dma_start(dst_sb[:], dst)
+        for g in range(1, PAIRS):
+            load_w4(g)
+            load_w8(g)
 
         for i in range(len(PASSES)):
             grouped = stage.tile([P, T, PACK], BF16, name="grouped", align_bytes=64)
@@ -204,6 +201,8 @@ def tile_moe_two_lin_silu_kernel(
             if i < LAST:
                 gather_codes(i, 0, S)
 
+        spread_gate()
+        acc = [psum.tile([P, C], F32, name=f"acc{e}", tag=f"bank{e}") for e in range(E)]
         for s0 in (0, S // 2):
             gather_codes(LAST, s0, s0 + S // 2)
             gather_planes(PASSES[LAST][2], s0, s0 + S // 2)

@@ -36,9 +36,8 @@ LOADS = (((0, T),), ((0, T),), HALVES, HALVES, QUANT)
 
 VECTOR_SHARE = ((640,), (576,), (0, 0), (0, 128), (0, 128, 128))
 
-W8_FIRST = 8
-W4_LOADS = ((0, 2), (2, 4), (4, 6), (6, 8))
-W8_LOADS = W4_LOADS
+SCATTERS = ((0, 2), (2, 5), (5, 8))
+W4_BYTES, W8_BYTES = 2 * A4 * 2 * N, 2 * A8 * 4 * N
 
 
 def tile_moe_two_lin_silu_kernel(
@@ -58,7 +57,7 @@ def tile_moe_two_lin_silu_kernel(
         raw = {}
         for i in range(len(PASSES)):
             for c0, c1 in LOADS[i]:
-                raw[i, c0] = keep.tile([P, PACK, c1 - c0], F32, name=f"raw{i}_{c0}")
+                raw[i, c0] = keep.tile([P, PACK, c1 - c0], F32, name=f"raw{i}_{c0}", align_bytes=64)
         all_codes = keep.tile([P, len(PASSES) * T + SPARE], U32, name="all_codes", align_bytes=64)
         codes = [all_codes[:, (LAST - i) * T : (LAST - i + 1) * T] for i in range(len(PASSES))]
         windows = [all_codes[:, (LAST - i) * T : (LAST - i + 1) * T + SPARE] for i in range(len(PASSES))]
@@ -66,17 +65,16 @@ def tile_moe_two_lin_silu_kernel(
         slot_codes = [keep.tile([P, S], U32, name=f"slot_codes{i}", align_bytes=64) for i in range(len(PASSES))]
         slot_planes = [keep.tile([P, S], U8, name=f"slot_planes{i}", align_bytes=64) for i in range(2)]
         moved_plane = keep.tile([P, S], U8, name="moved_plane", align_bytes=64)
-        w8_sb = [keep.tile([P, (e1 - e0) * A8, 4 * N], U8, name=f"w8_sb{e0}", align_bytes=64) for e0, e1 in W8_LOADS]
-        w4_sb = [keep.tile([P, (e1 - e0) * A4, 2 * N], U8, name=f"w4_sb{e0}", align_bytes=64) for e0, e1 in W4_LOADS]
+        first_words = keep.tile([P, W4_BYTES + W8_BYTES], U8, name="first_words", align_bytes=64)
+        pair_words = [first_words[:]]
         gate_sb = keep.tile([P, S], F32, name="gate_sb")
         ident = keep.tile([P, P], F32, name="ident")
         gate_row = keep.tile([P, S // P], F32, name="gate_row")
-        w8_plane = keep.tile([P, E * A8, N // 4], I32, name="w8_plane", align_bytes=64)
-        w4_plane = keep.tile([P, E * A4, N // 4], I32, name="w4_plane", align_bytes=64)
+        w_planes = keep.tile([P, E * (A4 + A8), N // 4], I32, name="w_planes", align_bytes=64)
+        w4_plane, w8_plane = w_planes[:, : E * A4, :], w_planes[:, E * A4 :, :]
 
         make_identity(nc, ident[:])
-        nc.vector.memset(w8_plane[:], 0)
-        nc.gpsimd.memset(w4_plane[:], 0)
+        nc.vector.memset(w_planes[:], 0)
         for plane in planes:
             nc.gpsimd.memset(plane[:].bitcast(I32), 0)
         nc.gpsimd.memset(moved_plane[:].bitcast(I32), 0)
@@ -101,24 +99,23 @@ def tile_moe_two_lin_silu_kernel(
             for c0, c1 in LOADS[i]:
                 nc.sync.dma_start(out=raw[i, c0][:], in_=src[:, :, c0:c1])
 
-        def load_scale_rows(plane, scales, first):
-            rows = scales.rearrange("e a q n -> q (e a) n").bitcast(I32)
-            for r in range(4):
-                nc.sync.dma_start(out=plane[first + r : P : 32], in_=rows[r:16:4])
+        def load_scale_rows(plane, scales):
+            nc.sync.dma_start(out=plane[0:P:8], in_=scales.rearrange("e a q n -> q (e a) n").bitcast(I32))
 
-        def load_w4(j):
-            e0, e1 = W4_LOADS[j]
-            rows = w4_words[e0:e1].rearrange("e a p n -> p (e a) n")
-            nc.sync.dma_start(out=w4_sb[j][:].bitcast(I32), in_=rows.bitcast(I32))
+        def place_scale_rows():
+            for r in range(1, 4):
+                nc.sync.dma_start(out=w_planes[r:P:32], in_=w_planes[8 * r : P : 32])
 
-        def load_w8(j):
-            e0, e1 = W8_LOADS[j]
-            rows = w8_words[e0:e1].rearrange("e a p n r -> p (e a) (n r)")
-            nc.sync.dma_start(out=w8_sb[j][:].bitcast(I32), in_=rows.bitcast(I32))
+        def load_words(g):
+            rows4 = w4_words[2 * g : 2 * g + 2].rearrange("e a p n -> p (e a) n")
+            into4 = pair_words[g][:, :W4_BYTES].rearrange("p (j n) -> p j n", n=2 * N)
+            nc.sync.dma_start(out=into4.bitcast(I32), in_=rows4.bitcast(I32))
+            rows8 = w8_words[2 * g : 2 * g + 2].rearrange("e a p n r -> p (e a) (n r)")
+            into8 = pair_words[g][:, W4_BYTES:].rearrange("p (j n) -> p j n", n=4 * N)
+            nc.sync.dma_start(out=into8.bitcast(I32), in_=rows8.bitcast(I32))
 
-        def words_of(tiles, loads, passes, e, a):
-            j = [e0 <= e < e1 for e0, e1 in loads].index(True)
-            return tiles[j][:, passes * (e - loads[j][0]) + a, :]
+        def words_of(e, first, width):
+            return pair_words[e // 2][:, first : first + width]
 
         def pair_views(i, grouped, l0, c0, c1):
             return (
@@ -163,9 +160,9 @@ def tile_moe_two_lin_silu_kernel(
             fmt, a, tile_no, first = PASSES[i]
             cols = slice(e * C, (e + 1) * C)
             if fmt == "e4m3":
-                words, plane = words_of(w8_sb, W8_LOADS, A8, e, a).bitcast(FP8X4), w8_plane[W8_FIRST:P, A8 * e + a, :]
+                words, plane = words_of(e, W4_BYTES + (A8 * (e % 2) + a) * 4 * N, 4 * N).bitcast(FP8X4), w8_plane[:, A8 * e + a, :]
             else:
-                words, plane = words_of(w4_sb, W4_LOADS, A4, e, a).bitcast(FP4X4), w4_plane[:, A4 * e + a, :]
+                words, plane = words_of(e, (A4 * (e % 2) + a) * 2 * N, 2 * N).bitcast(FP4X4), w4_plane[:, A4 * e + a, :]
             nc.tensor.matmul_mx(
                 out=acc[e][:],
                 lhsT=words,
@@ -178,18 +175,16 @@ def tile_moe_two_lin_silu_kernel(
 
         load_pass(0)
         nc.sync.dma_start(offs_sb[:], offs)
-        for i in range(1, len(PASSES)):
+        for i in range(1, LAST):
             load_pass(i)
+        load_scale_rows(w4_plane, w4_scales)
+        load_scale_rows(w8_plane, w8_scales)
+        load_pass(LAST)
         nc.sync.dma_start(out=gate_row[:], in_=gate[0:1, :].rearrange("o (p i) -> (o p) i", i=S // P))
-        load_w4(0)
-        load_scale_rows(w4_plane, w4_scales, 0)
-        load_w8(0)
-        load_scale_rows(w8_plane, w8_scales, W8_FIRST)
+        load_words(0)
         nc.sync.dma_start(out=b_sb[:], in_=b)
         nc.sync.dma_start(dst_sb[:], dst)
-        for g in range(1, PAIRS):
-            load_w4(g)
-            load_w8(g)
+        place_scale_rows()
 
         for i in range(len(PASSES)):
             grouped = stage.tile([P, T, PACK], BF16, name="grouped", align_bytes=64)
@@ -200,6 +195,12 @@ def tile_moe_two_lin_silu_kernel(
                 move_plane()
             if i < LAST:
                 gather_codes(i, 0, S)
+            if i == LAST - 1:
+                width = W4_BYTES + W8_BYTES
+                later = keep.tile([P, (PAIRS - 1) * width], U8, name="later", tag=f"raw{i}_{LOADS[i][-1][0]}", align_bytes=64)
+                for g in range(1, PAIRS):
+                    pair_words.append(later[:, (g - 1) * width : g * width])
+                    load_words(g)
 
         spread_gate()
         acc = [psum.tile([P, C], F32, name=f"acc{e}", tag=f"bank{e}") for e in range(E)]
@@ -214,7 +215,8 @@ def tile_moe_two_lin_silu_kernel(
                 for i in E4M3_PASSES:
                     multiply(i, e)
                 nc.scalar.activation(y_sb[:, e * C : (e + 1) * C], acc[e][:], ACT.Silu, bias=b_sb[:, e : e + 1])
-            cols = slice(2 * g * C, 2 * (g + 1) * C)
+        for e0, e1 in SCATTERS:
+            cols = slice(e0 * C, e1 * C)
             places = out_sb[:].indirect(dst_sb[:, cols.start // 16 : cols.stop // 16])
             nc.vector.tensor_tensor(places, y_sb[:, cols], gate_sb[:, cols], MULT)
         nc.sync.dma_start(out=out, in_=out_sb[:])

@@ -28,15 +28,13 @@ SPARE = 256
 
 PASSES = (("e2m1", 0, 0, 0), ("e2m1", 1, 0, 4), ("e4m3", 0, 1, 4), ("e4m3", 1, 1, 8), ("e2m1", 2, 1, 0))
 MOVED, LAST = 1, 4
-E2M1_PASSES, E4M3_PASSES = (0, 1, 4), (2, 3)
 
 QUANT = ((0, 512), (512, 1024), (1024, T))
 HALVES = ((0, T // 2), (T // 2, T))
 LOADS = (((0, T),), ((0, T),), HALVES, HALVES, QUANT)
 
-VECTOR_SHARE = ((640,), (576,), (0, 0), (0, 128), (0, 128, 128))
+VECTOR_SHARE = ((768,), (640,), (0, 0), (0, 128), (0, 128, 128))
 
-SCATTERS = ((0, 2), (2, 5), (5, 8))
 W4_BYTES, W8_BYTES = 2 * A4 * 2 * N, 2 * A8 * 4 * N
 
 
@@ -51,11 +49,11 @@ def tile_moe_two_lin_silu_kernel(
 
         offs_sb = keep.tile([P, S // 16], U16, name="offs_sb")
         dst_sb = keep.tile([P, S // 16], U16, name="dst_sb")
-        b_sb = keep.tile([P, E], F32, name="b_sb")
         y_sb = keep.tile([P, S], F32, name="y_sb")
         out_sb = keep.tile([P, T], F32, name="out_sb")
         raw = {}
-        for i in range(len(PASSES)):
+        first_rows = [keep.tile([P, 2, T], F32, name=f"first_rows{u}") for u in range(2)]
+        for i in range(1, LAST):
             for c0, c1 in LOADS[i]:
                 raw[i, c0] = keep.tile([P, PACK, c1 - c0], F32, name=f"raw{i}_{c0}", align_bytes=64)
         all_codes = keep.tile([P, len(PASSES) * T + SPARE], U32, name="all_codes", align_bytes=64)
@@ -65,11 +63,9 @@ def tile_moe_two_lin_silu_kernel(
         slot_codes = [keep.tile([P, S], U32, name=f"slot_codes{i}", align_bytes=64) for i in range(len(PASSES))]
         slot_planes = [keep.tile([P, S], U8, name=f"slot_planes{i}", align_bytes=64) for i in range(2)]
         moved_plane = keep.tile([P, S], U8, name="moved_plane", align_bytes=64)
-        first_words = keep.tile([P, W4_BYTES + W8_BYTES], U8, name="first_words", align_bytes=64)
-        pair_words = [first_words[:]]
+        pair_words = []
         gate_sb = keep.tile([P, S], F32, name="gate_sb")
         ident = keep.tile([P, P], F32, name="ident")
-        gate_row = keep.tile([P, S // P], F32, name="gate_row")
         w_planes = keep.tile([P, E * (A4 + A8), N // 4], I32, name="w_planes", align_bytes=64)
         w4_plane, w8_plane = w_planes[:, : E * A4, :], w_planes[:, E * A4 :, :]
 
@@ -81,7 +77,7 @@ def tile_moe_two_lin_silu_kernel(
         nc.vector.memset(out_sb[:], 0.0)
         nc.vector.memset(all_codes[:, len(PASSES) * T :].bitcast(I32), 0)
 
-        def spread_gate():
+        def spread_gate(gate_row):
             for half in range(2):
                 spread = psum.tile([P, 4, P], F32, name="spread", tag=f"bank{E - 2 + half}")
                 for q in range(4):
@@ -96,8 +92,12 @@ def tile_moe_two_lin_silu_kernel(
             fmt, a, tile_no, first = PASSES[i]
             row = K_PASS * a + (0 if fmt == "e4m3" else K8)
             src = xT[row : row + K_PASS, :].rearrange("(p t) c -> p t c", t=PACK)
+            if i == 0:
+                for u in range(2):
+                    nc.sync.dma_start(out=first_rows[u][:], in_=src[:, 2 * u : 2 * u + 2, :])
+                return
             for c0, c1 in LOADS[i]:
-                nc.sync.dma_start(out=raw[i, c0][:], in_=src[:, :, c0:c1])
+                nc.sync.dma_start(out=raw[i, c0][:, :, :], in_=src[:, :, c0:c1])
 
         def load_scale_rows(plane, scales):
             nc.sync.dma_start(out=plane[0:P:8], in_=scales.rearrange("e a q n -> q (e a) n").bitcast(I32))
@@ -132,6 +132,21 @@ def tile_moe_two_lin_silu_kernel(
                 for c0, c1 in zip(cuts, cuts[1:]):
                     nc.scalar.activation(*pair_views(i, grouped, l0, c0, c1), ACT.Copy)
 
+        def interleave_first(grouped):
+            split = T - VECTOR_SHARE[0][0]
+            for u in range(2):
+                for c0, c1 in ((split, T), (0, QUANT[0][1]), (QUANT[0][1], split)):
+                    if c1 <= c0:
+                        continue
+                    views = (
+                        grouped[:, c0:c1, 2 * u : 2 * u + 2].rearrange("p (c i) t -> p c t i", i=4),
+                        first_rows[u][:, :, c0:c1].rearrange("p t (c i) -> p c t i", i=4),
+                    )
+                    if c0 == split:
+                        nc.vector.tensor_copy(*views)
+                    else:
+                        nc.scalar.activation(*views, ACT.Copy)
+
         def quantize(i, grouped):
             fmt, a, tile_no, first = PASSES[i]
             for c0, c1 in QUANT:
@@ -151,7 +166,7 @@ def tile_moe_two_lin_silu_kernel(
         def move_plane():
             fmt, a, tile_no, first = PASSES[MOVED]
             for r in range(4):
-                nc.gpsimd.dma_start(
+                nc.sync.dma_start(
                     out=moved_plane[32 * r : 32 * r + 4, :].bitcast(I32),
                     in_=slot_planes[tile_no][32 * r + first : 32 * r + first + 4, :].bitcast(I32),
                 )
@@ -169,53 +184,61 @@ def tile_moe_two_lin_silu_kernel(
                 lhsT_scale=plane.bitcast(U8),
                 rhs=slot_codes[i][:, cols].bitcast(FP8X4),
                 rhs_scale=moved_plane[:, cols] if i == MOVED else slot_planes[tile_no][first:P, cols],
-                start=(i == E2M1_PASSES[0]),
-                stop=(i == E4M3_PASSES[-1]),
+                start=(i == 0),
+                stop=(i == LAST),
             )
 
         load_pass(0)
         nc.sync.dma_start(offs_sb[:], offs)
-        for i in range(1, LAST):
+        load_pass(1)
+        nc.sync.dma_start(dst_sb[:], dst)
+        for i in range(2, LAST):
             load_pass(i)
         load_scale_rows(w4_plane, w4_scales)
         load_scale_rows(w8_plane, w8_scales)
-        load_pass(LAST)
-        nc.sync.dma_start(out=gate_row[:], in_=gate[0:1, :].rearrange("o (p i) -> (o p) i", i=S // P))
-        load_words(0)
-        nc.sync.dma_start(out=b_sb[:], in_=b)
-        nc.sync.dma_start(dst_sb[:], dst)
-        place_scale_rows()
 
         for i in range(len(PASSES)):
             grouped = stage.tile([P, T, PACK], BF16, name="grouped", align_bytes=64)
-            interleave(i, grouped)
+            if i == 0:
+                interleave_first(grouped)
+            else:
+                interleave(i, grouped)
             quantize(i, grouped)
             if i == MOVED:
                 gather_planes(PASSES[MOVED][2], 0, S)
                 move_plane()
             if i < LAST:
                 gather_codes(i, 0, S)
+            if i == LAST - 2:
+                last = keep.tile([P, PACK * T], F32, name="last", tag=f"raw{i}_{LOADS[i][-1][0]}", align_bytes=64)
+                for c0, c1 in LOADS[LAST]:
+                    raw[LAST, c0] = last[:, PACK * c0 : PACK * c1].rearrange("p (t c) -> p t c", t=PACK)
+                load_pass(LAST)
             if i == LAST - 1:
+                small = keep.tile([P, 2 * E], F32, name="small", tag=f"raw{i}_0", align_bytes=64)
+                gate_row, b_sb = small[:, :E], small[:, E:]
+                nc.sync.dma_start(out=gate_row, in_=gate[0:1, :].rearrange("o (p i) -> (o p) i", i=S // P))
+                nc.sync.dma_start(out=b_sb, in_=b)
+                place_scale_rows()
                 width = W4_BYTES + W8_BYTES
-                later = keep.tile([P, (PAIRS - 1) * width], U8, name="later", tag=f"raw{i}_{LOADS[i][-1][0]}", align_bytes=64)
-                for g in range(1, PAIRS):
-                    pair_words.append(later[:, (g - 1) * width : g * width])
+                later = keep.tile([P, PAIRS * width], U8, name="later", tag=f"raw{i}_{LOADS[i][-1][0]}", align_bytes=64)
+                for g in range(PAIRS):
+                    pair_words.append(later[:, g * width : (g + 1) * width])
                     load_words(g)
 
-        spread_gate()
+        spread_gate(gate_row)
         acc = [psum.tile([P, C], F32, name=f"acc{e}", tag=f"bank{e}") for e in range(E)]
         for s0 in (0, S // 2):
-            gather_codes(LAST, s0, s0 + S // 2)
             gather_planes(PASSES[LAST][2], s0, s0 + S // 2)
-        for g in range(PAIRS):
-            for e in (2 * g, 2 * g + 1):
-                for i in E2M1_PASSES:
-                    multiply(i, e)
-            for e in (2 * g, 2 * g + 1):
-                for i in E4M3_PASSES:
-                    multiply(i, e)
-                nc.scalar.activation(y_sb[:, e * C : (e + 1) * C], acc[e][:], ACT.Silu, bias=b_sb[:, e : e + 1])
-        for e0, e1 in SCATTERS:
+            gather_codes(LAST, s0, s0 + S // 2)
+        for e0, e1 in ((0, E // 2), (E // 2, E)):
+            for pair in range(e0, e1, 2):
+                for passes in ((0, MOVED), (2, 3), (LAST,)):
+                    for e in (pair, pair + 1):
+                        for i in passes:
+                            multiply(i, e)
+                for e in (pair, pair + 1):
+                    nc.scalar.activation(y_sb[:, e * C : (e + 1) * C], acc[e][:], ACT.Silu, bias=b_sb[:, e : e + 1])
             cols = slice(e0 * C, e1 * C)
             places = out_sb[:].indirect(dst_sb[:, cols.start // 16 : cols.stop // 16])
             nc.vector.tensor_tensor(places, y_sb[:, cols], gate_sb[:, cols], MULT)

@@ -167,8 +167,8 @@ def tile_moe_two_lin_silu_kernel(
             fmt, a, tile_no, first = PASSES[MOVED]
             for r in range(4):
                 nc.sync.dma_start(
-                    out=moved_plane[32 * r : 32 * r + 4, :].bitcast(I32),
-                    in_=slot_planes[tile_no][32 * r + first : 32 * r + first + 4, :].bitcast(I32),
+                    out=moved_plane[r:P:32, :].bitcast(I32),
+                    in_=slot_planes[tile_no][first + r : P : 32, :].bitcast(I32),
                 )
 
         def multiply(i, e):
@@ -231,7 +231,7 @@ def tile_moe_two_lin_silu_kernel(
         for s0 in (0, S // 2):
             gather_planes(PASSES[LAST][2], s0, s0 + S // 2)
             gather_codes(LAST, s0, s0 + S // 2)
-        for e0, e1 in ((0, E // 2), (E // 2, E)):
+        for e0, e1 in ((0, 2), (2, 4), (4, E)):
             for pair in range(e0, e1, 2):
                 for passes in ((0, MOVED), (2, 3), (LAST,)):
                     for e in (pair, pair + 1):

@@ -35,6 +35,8 @@ LOADS = (((0, T),), ((0, T),), HALVES, HALVES, QUANT)
 
 VECTOR_SHARE = ((768,), (640,), (0, 0), (0, 128), (0, 128, 128))
 
+HALF = E // 2
+HALF_PLANES = HALF * (A4 + A8)
 W4_BYTES, W8_BYTES = 2 * A4 * 2 * N, 2 * A8 * 4 * N
 
 
@@ -66,11 +68,11 @@ def tile_moe_two_lin_silu_kernel(
         pair_words = []
         gate_sb = keep.tile([P, S], F32, name="gate_sb")
         ident = keep.tile([P, P], F32, name="ident")
-        w_planes = keep.tile([P, E * (A4 + A8), N // 4], I32, name="w_planes", align_bytes=64)
-        w4_plane, w8_plane = w_planes[:, : E * A4, :], w_planes[:, E * A4 :, :]
+        w_planes = [keep.tile([P, HALF_PLANES, N // 4], I32, name=f"w_planes{h}", align_bytes=64) for h in range(2)]
 
         make_identity(nc, ident[:])
-        nc.vector.memset(w_planes[:], 0)
+        for plane in w_planes:
+            nc.vector.memset(plane[:], 0)
         for plane in planes:
             nc.gpsimd.memset(plane[:].bitcast(I32), 0)
         nc.gpsimd.memset(moved_plane[:].bitcast(I32), 0)
@@ -99,12 +101,15 @@ def tile_moe_two_lin_silu_kernel(
             for c0, c1 in LOADS[i]:
                 nc.sync.dma_start(out=raw[i, c0][:, :, :], in_=src[:, :, c0:c1])
 
-        def load_scale_rows(plane, scales):
-            nc.sync.dma_start(out=plane[0:P:8], in_=scales.rearrange("e a q n -> q (e a) n").bitcast(I32))
+        def load_scale_rows(h, into):
+            experts = slice(h * HALF, (h + 1) * HALF)
+            for scales, j0, j1 in ((w4_scales, 0, HALF * A4), (w8_scales, HALF * A4, HALF_PLANES)):
+                rows = scales[experts].rearrange("e a q n -> q (e a) n")
+                nc.sync.dma_start(out=into[0:P:8, j0:j1, :], in_=rows.bitcast(I32))
 
-        def place_scale_rows():
-            for r in range(1, 4):
-                nc.sync.dma_start(out=w_planes[r:P:32], in_=w_planes[8 * r : P : 32])
+        def place_scale_rows(h, staged, first_row):
+            for r in range(first_row, 4):
+                nc.sync.dma_start(out=w_planes[h][r:P:32], in_=staged[8 * r : P : 32])
 
         def load_words(g):
             rows4 = w4_words[2 * g : 2 * g + 2].rearrange("e a p n -> p (e a) n")
@@ -175,9 +180,9 @@ def tile_moe_two_lin_silu_kernel(
             fmt, a, tile_no, first = PASSES[i]
             cols = slice(e * C, (e + 1) * C)
             if fmt == "e4m3":
-                words, plane = words_of(e, W4_BYTES + (A8 * (e % 2) + a) * 4 * N, 4 * N).bitcast(FP8X4), w8_plane[:, A8 * e + a, :]
+                words, plane = words_of(e, W4_BYTES + (A8 * (e % 2) + a) * 4 * N, 4 * N).bitcast(FP8X4), w_planes[e // HALF][:, HALF * A4 + A8 * (e % HALF) + a, :]
             else:
-                words, plane = words_of(e, (A4 * (e % 2) + a) * 2 * N, 2 * N).bitcast(FP4X4), w4_plane[:, A4 * e + a, :]
+                words, plane = words_of(e, (A4 * (e % 2) + a) * 2 * N, 2 * N).bitcast(FP4X4), w_planes[e // HALF][:, A4 * (e % HALF) + a, :]
             nc.tensor.matmul_mx(
                 out=acc[e][:],
                 lhsT=words,
@@ -194,8 +199,7 @@ def tile_moe_two_lin_silu_kernel(
         nc.sync.dma_start(dst_sb[:], dst)
         for i in range(2, LAST):
             load_pass(i)
-        load_scale_rows(w4_plane, w4_scales)
-        load_scale_rows(w8_plane, w8_scales)
+        load_scale_rows(0, w_planes[0])
 
         for i in range(len(PASSES)):
             grouped = stage.tile([P, T, PACK], BF16, name="grouped", align_bytes=64)
@@ -219,12 +223,21 @@ def tile_moe_two_lin_silu_kernel(
                 gate_row, b_sb = small[:, :E], small[:, E:]
                 nc.sync.dma_start(out=gate_row, in_=gate[0:1, :].rearrange("o (p i) -> (o p) i", i=S // P))
                 nc.sync.dma_start(out=b_sb, in_=b)
-                place_scale_rows()
+                place_scale_rows(0, w_planes[0], 1)
                 width = W4_BYTES + W8_BYTES
-                later = keep.tile([P, PAIRS * width], U8, name="later", tag=f"raw{i}_{LOADS[i][-1][0]}", align_bytes=64)
-                for g in range(PAIRS):
+                words_end = (PAIRS - 1) * width
+                later = keep.tile([P, words_end + HALF_PLANES * N], U8, name="later", tag=f"raw{i}_{LOADS[i][-1][0]}", align_bytes=64)
+                staged = later[:, words_end:].bitcast(I32).rearrange("p (j n) -> p j n", n=N // 4)
+                for g in range(PAIRS - 1):
                     pair_words.append(later[:, g * width : (g + 1) * width])
                     load_words(g)
+                    if g == 0:
+                        load_scale_rows(1, staged)
+                place_scale_rows(1, staged, 0)
+            if i == LAST:
+                final = keep.tile([P, width], U8, name="final", tag=f"raw{LAST - 2}_{LOADS[LAST - 2][-1][0]}", align_bytes=64)
+                pair_words.append(final[:, :])
+                load_words(PAIRS - 1)
 
         spread_gate(gate_row)
         acc = [psum.tile([P, C], F32, name=f"acc{e}", tag=f"bank{e}") for e in range(E)]

@@ -244,7 +244,7 @@ def tile_moe_two_lin_silu_kernel(
         for s0 in (0, S // 2):
             gather_planes(PASSES[LAST][2], s0, s0 + S // 2)
             gather_codes(LAST, s0, s0 + S // 2)
-        for e0, e1 in ((0, 2), (2, 4), (4, E)):
+        for e0, e1 in ((0, HALF), (HALF, E)):
             for pair in range(e0, e1, 2):
                 for passes in ((0, MOVED), (2, 3), (LAST,)):
                     for e in (pair, pair + 1):

@@ -33,8 +33,9 @@ QUANT = ((0, 512), (512, 1024), (1024, T))
 HALVES = ((0, T // 2), (T // 2, T))
 LOADS = (((0, T),), ((0, T),), HALVES, HALVES, QUANT)
 
-VECTOR_SHARE = ((768,), (640,), (0, 0), (0, 128), (0, 128, 128))
+VECTOR_SHARE = ((768,), (704,), (0, 0), (0, 128), (0, 128, 128))
 
+SCATTERS = ((0, 3), (3, 5), (5, E))
 HALF = E // 2
 HALF_PLANES = HALF * (A4 + A8)
 W4_BYTES, W8_BYTES = 2 * A4 * 2 * N, 2 * A8 * 4 * N
@@ -130,10 +131,15 @@ def tile_moe_two_lin_silu_kernel(
 
         def interleave(i, grouped):
             for (l0, l1), share in zip(LOADS[i], VECTOR_SHARE[i]):
-                split = l1 - share
-                if share:
-                    nc.vector.tensor_copy(*pair_views(i, grouped, l0, split, l1))
-                cuts = [l0] + [c1 for c0, c1 in QUANT if l0 < c1 < split] + [split]
+                if l1 - l0 == T:
+                    v0, v1, s0, s1 = l0, l0 + share, l0 + share, l1
+                else:
+                    v0, v1, s0, s1 = l1 - share, l1, l0, l1 - share
+                cuts = [v0] + [c1 for c0, c1 in QUANT if v0 < c1 < v1] + [v1]
+                for c0, c1 in zip(cuts, cuts[1:]):
+                    if c1 > c0:
+                        nc.vector.tensor_copy(*pair_views(i, grouped, l0, c0, c1))
+                cuts = [s0] + [c1 for c0, c1 in QUANT if s0 < c1 < s1] + [s1]
                 for c0, c1 in zip(cuts, cuts[1:]):
                     nc.scalar.activation(*pair_views(i, grouped, l0, c0, c1), ACT.Copy)
 
@@ -244,14 +250,14 @@ def tile_moe_two_lin_silu_kernel(
         for s0 in (0, S // 2):
             gather_planes(PASSES[LAST][2], s0, s0 + S // 2)
             gather_codes(LAST, s0, s0 + S // 2)
-        for e0, e1 in ((0, HALF), (HALF, E)):
-            for pair in range(e0, e1, 2):
-                for passes in ((0, MOVED), (2, 3), (LAST,)):
-                    for e in (pair, pair + 1):
-                        for i in passes:
-                            multiply(i, e)
+        for pair in range(0, E, 2):
+            for passes in ((0, MOVED), (2, 3), (LAST,)):
                 for e in (pair, pair + 1):
-                    nc.scalar.activation(y_sb[:, e * C : (e + 1) * C], acc[e][:], ACT.Silu, bias=b_sb[:, e : e + 1])
+                    for i in passes:
+                        multiply(i, e)
+            for e in (pair, pair + 1):
+                nc.scalar.activation(y_sb[:, e * C : (e + 1) * C], acc[e][:], ACT.Silu, bias=b_sb[:, e : e + 1])
+        for e0, e1 in SCATTERS:
             cols = slice(e0 * C, e1 * C)
             places = out_sb[:].indirect(dst_sb[:, cols.start // 16 : cols.stop // 16])
             nc.vector.tensor_tensor(places, y_sb[:, cols], gate_sb[:, cols], MULT)

@@ -18,12 +18,13 @@ FP8X4 = mybir.dt.float8_e4m3fn_x4
 FP4X4 = mybir.dt.float4_e2m1fn_x4
 ACT = mybir.ActivationFunctionType
 MULT = mybir.AluOpType.mult
+ADD = mybir.AluOpType.add
 
 P = 128
 PACK = 4
 K_PASS = P * PACK
 A8, A4 = 2, 3
-PAIRS = E // 2
+PAIR = 2 * C
 SPARE = 256
 
 PASSES = (("e2m1", 0, 0, 0), ("e2m1", 1, 0, 4), ("e4m3", 0, 1, 4), ("e4m3", 1, 1, 8), ("e2m1", 2, 1, 0))
@@ -32,13 +33,11 @@ MOVED, LAST = 1, 4
 QUANT = ((0, 512), (512, 1024), (1024, T))
 HALVES = ((0, T // 2), (T // 2, T))
 LOADS = (((0, T),), ((0, T),), HALVES, HALVES, QUANT)
-
 VECTOR_SHARE = ((768,), (704,), (0, 0), (0, 128), (0, 128, 128))
 
-SCATTERS = ((0, 3), (3, 5), (5, E))
-HALF = E // 2
-HALF_PLANES = HALF * (A4 + A8)
-W4_BYTES, W8_BYTES = 2 * A4 * 2 * N, 2 * A8 * 4 * N
+SCALAR_LATE = (448, 736)
+OUT_CHUNKS = ((0, 384), (384, 896), (896, T))
+W4_BYTES, W8_BYTES = A4 * 2 * N, A8 * 4 * N
 
 
 def tile_moe_two_lin_silu_kernel(
@@ -50,113 +49,77 @@ def tile_moe_two_lin_silu_kernel(
         stage = ctx.enter_context(tc.tile_pool(name="stage", bufs=4))
         psum = ctx.enter_context(tc.psum_pool(name="psum", bufs=1))
 
+        def tile(name, shape, dtype, on=None):
+            return keep.tile(shape, dtype, name=name, tag=on or name, align_bytes=64)
+
         offs_sb = keep.tile([P, S // 16], U16, name="offs_sb")
         dst_sb = keep.tile([P, S // 16], U16, name="dst_sb")
-        y_sb = keep.tile([P, S], F32, name="y_sb")
-        out_sb = keep.tile([P, T], F32, name="out_sb")
-        raw = {}
-        first_rows = [keep.tile([P, 2, T], F32, name=f"first_rows{u}") for u in range(2)]
-        for i in range(1, LAST):
-            for c0, c1 in LOADS[i]:
-                raw[i, c0] = keep.tile([P, PACK, c1 - c0], F32, name=f"raw{i}_{c0}", align_bytes=64)
-        all_codes = keep.tile([P, len(PASSES) * T + SPARE], U32, name="all_codes", align_bytes=64)
+        ident = tile("ident", [P, P], F32)
+        gate_row = tile("gate_row", [P, S // P], F32)
+        gate_first = tile("gate_first", [P, PAIR], F32)
+        gate_rest = tile("gate_rest", [P, S - PAIR], F32)
+        scalar_window = tile("scalar_window", [P, T + E], F32)
+        b_sb = scalar_window[:, T:]
+        vector_window = tile("vector_window", [P, T], F32)
+        all_codes = tile("all_codes", [P, len(PASSES) * T + SPARE], U32)
         codes = [all_codes[:, (LAST - i) * T : (LAST - i + 1) * T] for i in range(len(PASSES))]
         windows = [all_codes[:, (LAST - i) * T : (LAST - i + 1) * T + SPARE] for i in range(len(PASSES))]
-        planes = [keep.tile([P, T + SPARE], U8, name=f"planes{i}", align_bytes=64) for i in range(2)]
-        slot_codes = [keep.tile([P, S], U32, name=f"slot_codes{i}", align_bytes=64) for i in range(len(PASSES))]
-        slot_planes = [keep.tile([P, S], U8, name=f"slot_planes{i}", align_bytes=64) for i in range(2)]
-        moved_plane = keep.tile([P, S], U8, name="moved_plane", align_bytes=64)
-        pair_words = []
-        gate_sb = keep.tile([P, S], F32, name="gate_sb")
-        ident = keep.tile([P, P], F32, name="ident")
-        w_planes = [keep.tile([P, HALF_PLANES, N // 4], I32, name=f"w_planes{h}", align_bytes=64) for h in range(2)]
+        planes = [tile(f"planes{i}", [P, T + SPARE], U8) for i in range(2)]
+        slot_codes = [tile(f"slot_codes{i}", [P, S], U32) for i in range(LAST)]
+        early_plane = tile("early_plane", [P, S], U8)
+        moved_plane = tile("moved_plane", [P, S], U8)
+        w_planes = tile("w_planes", [P, E * (A4 + A8), N // 4], I32)
 
         make_identity(nc, ident[:])
-        for plane in w_planes:
-            nc.vector.memset(plane[:], 0)
+        nc.vector.memset(w_planes[:], 0)
         for plane in planes:
             nc.gpsimd.memset(plane[:].bitcast(I32), 0)
         nc.gpsimd.memset(moved_plane[:].bitcast(I32), 0)
-        nc.vector.memset(out_sb[:], 0.0)
+        nc.vector.memset(scalar_window[:, :T], 0.0)
+        nc.vector.memset(vector_window[:], 0.0)
         nc.vector.memset(all_codes[:, len(PASSES) * T :].bitcast(I32), 0)
 
-        def spread_gate(gate_row):
-            for half in range(2):
-                spread = psum.tile([P, 4, P], F32, name="spread", tag=f"bank{E - 2 + half}")
-                for q in range(4):
-                    i = 4 * half + q
-                    nc.tensor.transpose(spread[:, q, :], gate_row[:, i : i + 1].to_broadcast([P, P]), ident[:])
-                nc.scalar.copy(
-                    gate_sb[:].rearrange("m (p i) -> m p i", i=S // P)[:, :, 4 * half : 4 * half + 4],
-                    spread[:].rearrange("m q p -> m p q"),
-                )
-
-        def load_pass(i):
+        def pass_rows(i):
             fmt, a, tile_no, first = PASSES[i]
             row = K_PASS * a + (0 if fmt == "e4m3" else K8)
-            src = xT[row : row + K_PASS, :].rearrange("(p t) c -> p t c", t=PACK)
-            if i == 0:
-                for u in range(2):
-                    nc.sync.dma_start(out=first_rows[u][:], in_=src[:, 2 * u : 2 * u + 2, :])
-                return
+            return xT[row : row + K_PASS, :].rearrange("(p t) c -> p t c", t=PACK)
+
+        raw = {}
+
+        def load_pass(i, into):
             for c0, c1 in LOADS[i]:
-                nc.sync.dma_start(out=raw[i, c0][:, :, :], in_=src[:, :, c0:c1])
+                raw[i, c0] = into(c0, c1).rearrange("p (t c) -> p t c", t=PACK)
+                nc.sync.dma_start(out=raw[i, c0], in_=pass_rows(i)[:, :, c0:c1])
 
-        def load_scale_rows(h, into):
-            experts = slice(h * HALF, (h + 1) * HALF)
-            for scales, j0, j1 in ((w4_scales, 0, HALF * A4), (w8_scales, HALF * A4, HALF_PLANES)):
-                rows = scales[experts].rearrange("e a q n -> q (e a) n")
-                nc.sync.dma_start(out=into[0:P:8, j0:j1, :], in_=rows.bitcast(I32))
+        def slices_of(whole):
+            return lambda c0, c1: whole[:, PACK * c0 : PACK * c1]
 
-        def place_scale_rows(h, staged, first_row):
-            for r in range(first_row, 4):
-                nc.sync.dma_start(out=w_planes[h][r:P:32], in_=staged[8 * r : P : 32])
+        def round_and_group(engine, into, rows):
+            views = (into.rearrange("p (c i) t -> p c t i", i=4), rows.rearrange("p t (c i) -> p c t i", i=4))
+            if engine == "vector":
+                nc.vector.tensor_copy(*views)
+            else:
+                nc.scalar.activation(*views, ACT.Copy)
 
-        def load_words(g):
-            rows4 = w4_words[2 * g : 2 * g + 2].rearrange("e a p n -> p (e a) n")
-            into4 = pair_words[g][:, :W4_BYTES].rearrange("p (j n) -> p j n", n=2 * N)
-            nc.sync.dma_start(out=into4.bitcast(I32), in_=rows4.bitcast(I32))
-            rows8 = w8_words[2 * g : 2 * g + 2].rearrange("e a p n r -> p (e a) (n r)")
-            into8 = pair_words[g][:, W4_BYTES:].rearrange("p (j n) -> p j n", n=4 * N)
-            nc.sync.dma_start(out=into8.bitcast(I32), in_=rows8.bitcast(I32))
-
-        def words_of(e, first, width):
-            return pair_words[e // 2][:, first : first + width]
-
-        def pair_views(i, grouped, l0, c0, c1):
-            return (
-                grouped[:, c0:c1, :].rearrange("p (c i) t -> p c t i", i=4),
-                raw[i, l0][:, :, c0 - l0 : c1 - l0].rearrange("p t (c i) -> p c t i", i=4),
-            )
+        def cut(c0, c1):
+            ends = [c0] + [end for start, end in QUANT if c0 < end < c1] + [c1]
+            return [(a, z) for a, z in zip(ends, ends[1:]) if z > a]
 
         def interleave(i, grouped):
+            if i == 0:
+                split = T - VECTOR_SHARE[0][0]
+                for u in range(2):
+                    for engine, c0, c1 in (("vector", split, T), ("scalar", 0, split)):
+                        round_and_group(engine, grouped[:, c0:c1, 2 * u : 2 * u + 2], first_rows[u][:, :, c0:c1])
+                return
             for (l0, l1), share in zip(LOADS[i], VECTOR_SHARE[i]):
                 if l1 - l0 == T:
-                    v0, v1, s0, s1 = l0, l0 + share, l0 + share, l1
+                    parts = (("vector", l0, l0 + share), ("scalar", l0 + share, l1))
                 else:
-                    v0, v1, s0, s1 = l1 - share, l1, l0, l1 - share
-                cuts = [v0] + [c1 for c0, c1 in QUANT if v0 < c1 < v1] + [v1]
-                for c0, c1 in zip(cuts, cuts[1:]):
-                    if c1 > c0:
-                        nc.vector.tensor_copy(*pair_views(i, grouped, l0, c0, c1))
-                cuts = [s0] + [c1 for c0, c1 in QUANT if s0 < c1 < s1] + [s1]
-                for c0, c1 in zip(cuts, cuts[1:]):
-                    nc.scalar.activation(*pair_views(i, grouped, l0, c0, c1), ACT.Copy)
-
-        def interleave_first(grouped):
-            split = T - VECTOR_SHARE[0][0]
-            for u in range(2):
-                for c0, c1 in ((split, T), (0, QUANT[0][1]), (QUANT[0][1], split)):
-                    if c1 <= c0:
-                        continue
-                    views = (
-                        grouped[:, c0:c1, 2 * u : 2 * u + 2].rearrange("p (c i) t -> p c t i", i=4),
-                        first_rows[u][:, :, c0:c1].rearrange("p t (c i) -> p c t i", i=4),
-                    )
-                    if c0 == split:
-                        nc.vector.tensor_copy(*views)
-                    else:
-                        nc.scalar.activation(*views, ACT.Copy)
+                    parts = (("vector", l1 - share, l1), ("scalar", l0, l1 - share))
+                for engine, s0, s1 in parts:
+                    for c0, c1 in cut(s0, s1):
+                        round_and_group(engine, grouped[:, c0:c1, :], raw[i, l0][:, :, c0 - l0 : c1 - l0])
 
         def quantize(i, grouped):
             fmt, a, tile_no, first = PASSES[i]
@@ -167,98 +130,129 @@ def tile_moe_two_lin_silu_kernel(
                     in_=grouped[:, c0:c1, :].rearrange("p c t -> p (c t)"),
                 )
 
-        def gather_codes(i, s0, s1):
-            nc.vector.tensor_copy(slot_codes[i][:, s0:s1], windows[i].indirect(offs_sb[:, s0 // 16 : s1 // 16]))
+        def gather(into, window, s0, s1):
+            nc.vector.tensor_copy(into, window.indirect(offs_sb[:, s0 // 16 : s1 // 16]))
 
-        def gather_planes(tile_no, s0, s1):
-            window = planes[tile_no][:].indirect(offs_sb[:, s0 // 16 : s1 // 16])
-            nc.vector.tensor_copy(slot_planes[tile_no][:, s0:s1], window)
+        def spread_gate():
+            for half in range(2):
+                spread = psum.tile([P, 4, P], F32, name="spread", tag=f"bank{E - 2 + half}")
+                for q in range(4):
+                    i = 4 * half + q
+                    nc.tensor.transpose(spread[:, q, :], gate_row[:, i : i + 1].to_broadcast([P, P]), ident[:])
+                for into, p0, p1 in ((gate_first, 0, PAIR // E), (gate_rest, PAIR // E, P)):
+                    nc.scalar.copy(
+                        into[:].rearrange("m (p i) -> m p i", i=S // P)[:, :, 4 * half : 4 * half + 4],
+                        spread[:, :, p0:p1].rearrange("m q p -> m p q"),
+                    )
 
-        def move_plane():
-            fmt, a, tile_no, first = PASSES[MOVED]
-            for r in range(4):
-                nc.sync.dma_start(
-                    out=moved_plane[r:P:32, :].bitcast(I32),
-                    in_=slot_planes[tile_no][first + r : P : 32, :].bitcast(I32),
-                )
+        first_rows = [tile(f"first_rows{u}", [P, 2, T], F32) for u in range(2)]
+        for u in range(2):
+            nc.sync.dma_start(out=first_rows[u][:], in_=pass_rows(0)[:, 2 * u : 2 * u + 2, :])
+        nc.sync.dma_start(offs_sb[:], offs)
+        nc.sync.dma_start(out=gate_row[:], in_=gate[0:1, :].rearrange("o (p i) -> (o p) i", i=S // P))
+        load_pass(1, slices_of(tile("raw1", [P, PACK * T], F32)))
+        nc.sync.dma_start(out=b_sb, in_=b)
+        nc.sync.dma_start(dst_sb[:], dst)
+        load_pass(2, lambda c0, c1: tile(f"raw2_{c0}", [P, PACK * (c1 - c0)], F32)[:, :])
+        for scales, j0, j1 in ((w4_scales, 0, E * A4), (w8_scales, E * A4, E * (A4 + A8))):
+            rows = scales.rearrange("e a q n -> q (e a) n")
+            nc.sync.dma_start(out=w_planes[0:P:8, j0:j1, :], in_=rows.bitcast(I32))
+
+        for i in range(len(PASSES)):
+            grouped = stage.tile([P, T, PACK], BF16, name="grouped", align_bytes=64)
+            interleave(i, grouped)
+            quantize(i, grouped)
+            if i == MOVED:
+                load_pass(3, slices_of(tile("raw3", [P, PACK * T], F32, on="raw1")))
+                gather(early_plane[:], planes[0][:], 0, S)
+                for r in range(4):
+                    nc.sync.dma_start(
+                        out=moved_plane[r:P:32, :].bitcast(I32),
+                        in_=early_plane[PASSES[MOVED][3] + r : P : 32, :].bitcast(I32),
+                    )
+            if i < LAST:
+                gather(slot_codes[i][:], windows[i], 0, S)
+            if i == 2:
+                load_pass(LAST, slices_of(tile("raw4", [P, PACK * T], F32, on="raw2_0")))
+                for r in range(1, 4):
+                    nc.sync.dma_start(out=w_planes[r:P:32], in_=w_planes[8 * r : P : 32])
+                words = tile("words", [P, E * (W4_BYTES + W8_BYTES)], U8, on=f"raw2_{T // 2}")
+                words4 = words[:, : E * W4_BYTES].rearrange("p (j n) -> p j n", n=2 * N)
+                words8 = words[:, E * W4_BYTES :].rearrange("p (j n) -> p j n", n=4 * N)
+                for e in range(0, E, 2):
+                    rows4 = w4_words[e : e + 2].rearrange("e a p n -> p (e a) n")
+                    nc.sync.dma_start(out=words4[:, A4 * e : A4 * (e + 2), :].bitcast(I32), in_=rows4.bitcast(I32))
+                    rows8 = w8_words[e : e + 2].rearrange("e a p n r -> p (e a) (n r)")
+                    nc.sync.dma_start(out=words8[:, A8 * e : A8 * (e + 2), :].bitcast(I32), in_=rows8.bitcast(I32))
+        spread_gate()
+
+        acc = [psum.tile([P, C], F32, name=f"acc{e}", tag=f"bank{e}") for e in range(E)]
+        last_codes, last_planes = {}, {}
 
         def multiply(i, e):
             fmt, a, tile_no, first = PASSES[i]
             cols = slice(e * C, (e + 1) * C)
+            half, in_half = e // 4, slice(e % 4 * C, (e % 4 + 1) * C)
             if fmt == "e4m3":
-                words, plane = words_of(e, W4_BYTES + (A8 * (e % 2) + a) * 4 * N, 4 * N).bitcast(FP8X4), w_planes[e // HALF][:, HALF * A4 + A8 * (e % HALF) + a, :]
+                w, j = words8[:, A8 * e + a, :].bitcast(FP8X4), E * A4 + A8 * e + a
             else:
-                words, plane = words_of(e, (A4 * (e % 2) + a) * 2 * N, 2 * N).bitcast(FP4X4), w_planes[e // HALF][:, A4 * (e % HALF) + a, :]
+                w, j = words4[:, A4 * e + a, :].bitcast(FP4X4), A4 * e + a
+            if tile_no == 1:
+                plane = last_planes[half][first:P, in_half]
+            else:
+                plane = moved_plane[:, cols] if i == MOVED else early_plane[:, cols]
             nc.tensor.matmul_mx(
                 out=acc[e][:],
-                lhsT=words,
-                lhsT_scale=plane.bitcast(U8),
-                rhs=slot_codes[i][:, cols].bitcast(FP8X4),
-                rhs_scale=moved_plane[:, cols] if i == MOVED else slot_planes[tile_no][first:P, cols],
+                lhsT=w,
+                lhsT_scale=w_planes[:, j, :].bitcast(U8),
+                rhs=(last_codes[half][:, in_half] if i == LAST else slot_codes[i][:, cols]).bitcast(FP8X4),
+                rhs_scale=plane,
                 start=(i == 0),
                 stop=(i == LAST),
             )
 
-        load_pass(0)
-        nc.sync.dma_start(offs_sb[:], offs)
-        load_pass(1)
-        nc.sync.dma_start(dst_sb[:], dst)
-        for i in range(2, LAST):
-            load_pass(i)
-        load_scale_rows(0, w_planes[0])
-
-        for i in range(len(PASSES)):
-            grouped = stage.tile([P, T, PACK], BF16, name="grouped", align_bytes=64)
-            if i == 0:
-                interleave_first(grouped)
-            else:
-                interleave(i, grouped)
-            quantize(i, grouped)
-            if i == MOVED:
-                gather_planes(PASSES[MOVED][2], 0, S)
-                move_plane()
-            if i < LAST:
-                gather_codes(i, 0, S)
-            if i == LAST - 2:
-                last = keep.tile([P, PACK * T], F32, name="last", tag=f"raw{i}_{LOADS[i][-1][0]}", align_bytes=64)
-                for c0, c1 in LOADS[LAST]:
-                    raw[LAST, c0] = last[:, PACK * c0 : PACK * c1].rearrange("p (t c) -> p t c", t=PACK)
-                load_pass(LAST)
-            if i == LAST - 1:
-                small = keep.tile([P, 2 * E], F32, name="small", tag=f"raw{i}_0", align_bytes=64)
-                gate_row, b_sb = small[:, :E], small[:, E:]
-                nc.sync.dma_start(out=gate_row, in_=gate[0:1, :].rearrange("o (p i) -> (o p) i", i=S // P))
-                nc.sync.dma_start(out=b_sb, in_=b)
-                place_scale_rows(0, w_planes[0], 1)
-                width = W4_BYTES + W8_BYTES
-                words_end = (PAIRS - 1) * width
-                later = keep.tile([P, words_end + HALF_PLANES * N], U8, name="later", tag=f"raw{i}_{LOADS[i][-1][0]}", align_bytes=64)
-                staged = later[:, words_end:].bitcast(I32).rearrange("p (j n) -> p j n", n=N // 4)
-                for g in range(PAIRS - 1):
-                    pair_words.append(later[:, g * width : (g + 1) * width])
-                    load_words(g)
-                    if g == 0:
-                        load_scale_rows(1, staged)
-                place_scale_rows(1, staged, 0)
-            if i == LAST:
-                final = keep.tile([P, width], U8, name="final", tag=f"raw{LAST - 2}_{LOADS[LAST - 2][-1][0]}", align_bytes=64)
-                pair_words.append(final[:, :])
-                load_words(PAIRS - 1)
-
-        spread_gate(gate_row)
-        acc = [psum.tile([P, C], F32, name=f"acc{e}", tag=f"bank{e}") for e in range(E)]
-        for s0 in (0, S // 2):
-            gather_planes(PASSES[LAST][2], s0, s0 + S // 2)
-            gather_codes(LAST, s0, s0 + S // 2)
-        for pair in range(0, E, 2):
+        def experts(pair, y):
             for passes in ((0, MOVED), (2, 3), (LAST,)):
-                for e in (pair, pair + 1):
+                for e in (2 * pair, 2 * pair + 1):
                     for i in passes:
                         multiply(i, e)
-            for e in (pair, pair + 1):
-                nc.scalar.activation(y_sb[:, e * C : (e + 1) * C], acc[e][:], ACT.Silu, bias=b_sb[:, e : e + 1])
-        for e0, e1 in SCATTERS:
-            cols = slice(e0 * C, e1 * C)
-            places = out_sb[:].indirect(dst_sb[:, cols.start // 16 : cols.stop // 16])
-            nc.vector.tensor_tensor(places, y_sb[:, cols], gate_sb[:, cols], MULT)
-        nc.sync.dma_start(out=out, in_=out_sb[:])
+            for q in range(2):
+                e = 2 * pair + q
+                nc.scalar.activation(y[:, q * C : (q + 1) * C], acc[e][:], ACT.Silu, bias=b_sb[:, e : e + 1])
+
+        def places(window, s0, s1):
+            return window[:].indirect(dst_sb[:, s0 // 16 : s1 // 16])
+
+        last_codes[0] = tile("last_codes0", [P, 2 * PAIR], U32)
+        last_planes[0] = tile("last_planes0", [P, 2 * PAIR], U8)
+        gather(last_planes[0][:, :PAIR], planes[1][:], 0, PAIR)
+        gather(last_codes[0][:, :PAIR], windows[LAST], 0, PAIR)
+        gather(last_codes[0][:, PAIR:], windows[LAST], PAIR, 2 * PAIR)
+        gather(last_planes[0][:, PAIR:], planes[1][:], PAIR, 2 * PAIR)
+        y_first = tile("y_first", [P, PAIR], F32)
+        experts(0, y_first)
+        gated_first = tile("gated_first", [P, PAIR], F32)
+        nc.vector.tensor_tensor(gated_first[:], y_first[:], gate_first[:], MULT)
+        nc.scalar.activation(places(scalar_window, 0, PAIR), gated_first[:], ACT.Copy)
+
+        last_codes[1] = tile("last_codes1", [P, 2 * PAIR], U32, on="y_first")
+        last_planes[1] = tile("last_planes1", [P, 2 * PAIR], U8, on="gate_first")
+        gather(last_planes[1][:], planes[1][:], 2 * PAIR, S)
+        gather(last_codes[1][:, :PAIR], windows[LAST], 2 * PAIR, 3 * PAIR)
+        gather(last_codes[1][:, PAIR:], windows[LAST], 3 * PAIR, S)
+        y_rest = tile("y_rest", [P, S - PAIR], F32)
+        for pair in range(1, E // 2):
+            experts(pair, y_rest[:, (pair - 1) * PAIR : pair * PAIR])
+        s0, s1 = SCALAR_LATE
+
+        def times_gate(into, j0, j1):
+            nc.vector.tensor_tensor(into, y_rest[:, j0 - PAIR : j1 - PAIR], gate_rest[:, j0 - PAIR : j1 - PAIR], MULT)
+
+        times_gate(places(vector_window, PAIR, s0), PAIR, s0)
+        gated_late = tile("gated_late", [P, s1 - s0], F32)
+        times_gate(gated_late[:], s0, s1)
+        nc.scalar.activation(places(scalar_window, s0, s1), gated_late[:], ACT.Copy)
+        times_gate(places(vector_window, s1, S), s1, S)
+        for c0, c1 in OUT_CHUNKS:
+            nc.vector.tensor_tensor(vector_window[:, c0:c1], vector_window[:, c0:c1], scalar_window[:, c0:c1], ADD)
+            nc.sync.dma_start(out=out[:, c0:c1], in_=vector_window[:, c0:c1])

@@ -36,6 +36,8 @@ LOADS = (((0, T),), ((0, T),), HALVES, HALVES, QUANT)
 VECTOR_SHARE = ((768,), (704,), (0, 0), (0, 128), (0, 128, 128))
 
 SCALAR_LATE = (448, 736)
+WORD_LOADS = [(fmt, e, e + 2) for e in (0, 2, 4) for fmt in ("e2m1", "e4m3")]
+WORD_LOADS = WORD_LOADS + [("e4m3", 6, 8), ("e2m1", 6, 7), ("e2m1", 7, 8)]
 OUT_CHUNKS = ((0, 384), (384, 896), (896, T))
 W4_BYTES, W8_BYTES = A4 * 2 * N, A8 * 4 * N
 
@@ -179,17 +181,19 @@ def tile_moe_two_lin_silu_kernel(
                 words = tile("words", [P, E * (W4_BYTES + W8_BYTES)], U8, on=f"raw2_{T // 2}")
                 words4 = words[:, : E * W4_BYTES].rearrange("p (j n) -> p j n", n=2 * N)
                 words8 = words[:, E * W4_BYTES :].rearrange("p (j n) -> p j n", n=4 * N)
-                for e in range(0, E, 2):
-                    rows4 = w4_words[e : e + 2].rearrange("e a p n -> p (e a) n")
-                    nc.sync.dma_start(out=words4[:, A4 * e : A4 * (e + 2), :].bitcast(I32), in_=rows4.bitcast(I32))
-                    rows8 = w8_words[e : e + 2].rearrange("e a p n r -> p (e a) (n r)")
-                    nc.sync.dma_start(out=words8[:, A8 * e : A8 * (e + 2), :].bitcast(I32), in_=rows8.bitcast(I32))
+                rows4 = w4_words.rearrange("e a p n -> p (e a) n")
+                rows8 = w8_words.rearrange("e a p n r -> p (e a) (n r)")
+                for fmt, e0, e1 in WORD_LOADS:
+                    into, rows, a = (words4, rows4, A4) if fmt == "e2m1" else (words8, rows8, A8)
+                    nc.sync.dma_start(
+                        out=into[:, a * e0 : a * e1, :].bitcast(I32), in_=rows[:, a * e0 : a * e1, :].bitcast(I32)
+                    )
         spread_gate()
 
         acc = [psum.tile([P, C], F32, name=f"acc{e}", tag=f"bank{e}") for e in range(E)]
         last_codes, last_planes = {}, {}
 
-        def multiply(i, e):
+        def multiply(i, e, opens):
             fmt, a, tile_no, first = PASSES[i]
             cols = slice(e * C, (e + 1) * C)
             half, in_half = e // 4, slice(e % 4 * C, (e % 4 + 1) * C)
@@ -207,15 +211,16 @@ def tile_moe_two_lin_silu_kernel(
                 lhsT_scale=w_planes[:, j, :].bitcast(U8),
                 rhs=(last_codes[half][:, in_half] if i == LAST else slot_codes[i][:, cols]).bitcast(FP8X4),
                 rhs_scale=plane,
-                start=(i == 0),
+                start=opens,
                 stop=(i == LAST),
             )
 
         def experts(pair, y):
-            for passes in ((0, MOVED), (2, 3), (LAST,)):
+            order = ((0, MOVED), (2, 3), (LAST,)) if pair < 3 else ((2, 3), (0, MOVED, LAST))
+            for passes in order:
                 for e in (2 * pair, 2 * pair + 1):
                     for i in passes:
-                        multiply(i, e)
+                        multiply(i, e, i == order[0][0])
             for q in range(2):
                 e = 2 * pair + q
                 nc.scalar.activation(y[:, q * C : (q + 1) * C], acc[e][:], ACT.Silu, bias=b_sb[:, e : e + 1])

@@ -36,10 +36,17 @@ LOADS = (((0, T),), ((0, T),), HALVES, HALVES, QUANT)
 VECTOR_SHARE = ((768,), (704,), (0, 0), (0, 128), (0, 128, 128))
 
 SCALAR_LATE = (448, 736)
-WORD_LOADS = [(fmt, e, e + 2) for e in (0, 2, 4) for fmt in ("e2m1", "e4m3")]
-WORD_LOADS = WORD_LOADS + [("e4m3", 6, 8), ("e2m1", 6, 7), ("e2m1", 7, 8)]
+WORD_LOADS = (
+    (("e2m1", 0, 2), ("e4m3", 0, 2)),
+    (("e4m3", 2, 4), ("e2m1", 2, 4)),
+    (("e4m3", 4, 6), ("e2m1", 4, 6)),
+    (("e4m3", 6, 8), ("e2m1", 6, 7), ("e2m1", 7, 8)),
+)
+HALF = E // 2
+HALF_PLANES = HALF * (A4 + A8)
 OUT_CHUNKS = ((0, 384), (384, 896), (896, T))
 W4_BYTES, W8_BYTES = A4 * 2 * N, A8 * 4 * N
+PAIR_BYTES = 2 * (W4_BYTES + W8_BYTES)
 
 
 def tile_moe_two_lin_silu_kernel(
@@ -57,7 +64,6 @@ def tile_moe_two_lin_silu_kernel(
         offs_sb = keep.tile([P, S // 16], U16, name="offs_sb")
         dst_sb = keep.tile([P, S // 16], U16, name="dst_sb")
         ident = tile("ident", [P, P], F32)
-        gate_row = tile("gate_row", [P, S // P], F32)
         gate_first = tile("gate_first", [P, PAIR], F32)
         gate_rest = tile("gate_rest", [P, S - PAIR], F32)
         scalar_window = tile("scalar_window", [P, T + E], F32)
@@ -70,10 +76,11 @@ def tile_moe_two_lin_silu_kernel(
         slot_codes = [tile(f"slot_codes{i}", [P, S], U32) for i in range(LAST)]
         early_plane = tile("early_plane", [P, S], U8)
         moved_plane = tile("moved_plane", [P, S], U8)
-        w_planes = tile("w_planes", [P, E * (A4 + A8), N // 4], I32)
+        w_planes = [tile(f"w_planes{h}", [P, HALF_PLANES, N // 4], I32) for h in range(2)]
 
         make_identity(nc, ident[:])
-        nc.vector.memset(w_planes[:], 0)
+        for plane in w_planes:
+            nc.vector.memset(plane[:], 0)
         for plane in planes:
             nc.gpsimd.memset(plane[:].bitcast(I32), 0)
         nc.gpsimd.memset(moved_plane[:].bitcast(I32), 0)
@@ -135,6 +142,34 @@ def tile_moe_two_lin_silu_kernel(
         def gather(into, window, s0, s1):
             nc.vector.tensor_copy(into, window.indirect(offs_sb[:, s0 // 16 : s1 // 16]))
 
+        def load_scale_rows(h, into):
+            for scales, j0, j1 in ((w4_scales, 0, HALF * A4), (w8_scales, HALF * A4, HALF_PLANES)):
+                rows = scales[h * HALF : (h + 1) * HALF].rearrange("e a q n -> q (e a) n")
+                nc.sync.dma_start(out=into[0:P:8, j0:j1, :], in_=rows.bitcast(I32))
+
+        def place_scale_rows(h, staged, first_row):
+            for r in range(first_row, 4):
+                nc.sync.dma_start(out=w_planes[h][r:P:32], in_=staged[8 * r : P : 32])
+
+        words = {}
+
+        def load_words(fmt, e0, e1, into):
+            if fmt == "e2m1":
+                rows, a, width = w4_words.rearrange("e a p n -> p (e a) n"), A4, 2 * N
+            else:
+                rows, a, width = w8_words.rearrange("e a p n r -> p (e a) (n r)"), A8, 4 * N
+            by_pass = into.rearrange("p (j n) -> p j n", n=width)
+            nc.sync.dma_start(out=by_pass.bitcast(I32), in_=rows[:, a * e0 : a * e1, :].bitcast(I32))
+            for j in range(a * (e1 - e0)):
+                words[fmt, e0 + j // a, j % a] = into[:, j * width : (j + 1) * width]
+
+        def load_pair(pair, into):
+            at = 0
+            for fmt, e0, e1 in WORD_LOADS[pair]:
+                width = (e1 - e0) * (W4_BYTES if fmt == "e2m1" else W8_BYTES)
+                load_words(fmt, e0, e1, into[:, at : at + width])
+                at = at + width
+
         def spread_gate():
             for half in range(2):
                 spread = psum.tile([P, 4, P], F32, name="spread", tag=f"bank{E - 2 + half}")
@@ -151,21 +186,18 @@ def tile_moe_two_lin_silu_kernel(
         for u in range(2):
             nc.sync.dma_start(out=first_rows[u][:], in_=pass_rows(0)[:, 2 * u : 2 * u + 2, :])
         nc.sync.dma_start(offs_sb[:], offs)
-        nc.sync.dma_start(out=gate_row[:], in_=gate[0:1, :].rearrange("o (p i) -> (o p) i", i=S // P))
         load_pass(1, slices_of(tile("raw1", [P, PACK * T], F32)))
-        nc.sync.dma_start(out=b_sb, in_=b)
         nc.sync.dma_start(dst_sb[:], dst)
-        load_pass(2, lambda c0, c1: tile(f"raw2_{c0}", [P, PACK * (c1 - c0)], F32)[:, :])
-        for scales, j0, j1 in ((w4_scales, 0, E * A4), (w8_scales, E * A4, E * (A4 + A8))):
-            rows = scales.rearrange("e a q n -> q (e a) n")
-            nc.sync.dma_start(out=w_planes[0:P:8, j0:j1, :], in_=rows.bitcast(I32))
+        nc.sync.dma_start(out=b_sb, in_=b)
+        for i in (2, 3):
+            load_pass(i, lambda c0, c1: tile(f"raw{i}_{c0}", [P, PACK * (c1 - c0)], F32)[:, :])
+        load_scale_rows(0, w_planes[0])
 
         for i in range(len(PASSES)):
             grouped = stage.tile([P, T, PACK], BF16, name="grouped", align_bytes=64)
             interleave(i, grouped)
             quantize(i, grouped)
             if i == MOVED:
-                load_pass(3, slices_of(tile("raw3", [P, PACK * T], F32, on="raw1")))
                 gather(early_plane[:], planes[0][:], 0, S)
                 for r in range(4):
                     nc.sync.dma_start(
@@ -175,22 +207,22 @@ def tile_moe_two_lin_silu_kernel(
             if i < LAST:
                 gather(slot_codes[i][:], windows[i], 0, S)
             if i == 2:
-                load_pass(LAST, slices_of(tile("raw4", [P, PACK * T], F32, on="raw2_0")))
-                for r in range(1, 4):
-                    nc.sync.dma_start(out=w_planes[r:P:32], in_=w_planes[8 * r : P : 32])
-                words = tile("words", [P, E * (W4_BYTES + W8_BYTES)], U8, on=f"raw2_{T // 2}")
-                words4 = words[:, : E * W4_BYTES].rearrange("p (j n) -> p j n", n=2 * N)
-                words8 = words[:, E * W4_BYTES :].rearrange("p (j n) -> p j n", n=4 * N)
-                rows4 = w4_words.rearrange("e a p n -> p (e a) n")
-                rows8 = w8_words.rearrange("e a p n r -> p (e a) (n r)")
-                for fmt, e0, e1 in WORD_LOADS:
-                    into, rows, a = (words4, rows4, A4) if fmt == "e2m1" else (words8, rows8, A8)
-                    nc.sync.dma_start(
-                        out=into[:, a * e0 : a * e1, :].bitcast(I32), in_=rows[:, a * e0 : a * e1, :].bitcast(I32)
-                    )
+                load_pass(LAST, slices_of(tile("raw4", [P, PACK * T], F32, on=f"raw2_{T // 2}")))
+            if i == 3:
+                gate_row = tile("gate_row", [P, S // P], F32, on="raw3_0")[:, :]
+                nc.sync.dma_start(out=gate_row, in_=gate[0:1, :].rearrange("o (p i) -> (o p) i", i=S // P))
+                place_scale_rows(0, w_planes[0], 1)
+                later = tile("later", [P, 3 * PAIR_BYTES + HALF_PLANES * N], U8, on=f"raw3_{T // 2}")
+                staged = later[:, 3 * PAIR_BYTES :].bitcast(I32).rearrange("p (j n) -> p j n", n=N // 4)
+                for pair in range(3):
+                    load_pair(pair, later[:, pair * PAIR_BYTES : (pair + 1) * PAIR_BYTES])
+                    if pair == 0:
+                        load_scale_rows(1, staged)
+                place_scale_rows(1, staged, 0)
+        load_pair(3, tile("final", [P, PAIR_BYTES], U8, on=f"raw2_{T // 2}")[:, :])
         spread_gate()
 
-        acc = [psum.tile([P, C], F32, name=f"acc{e}", tag=f"bank{e}") for e in range(E)]
+        acc = {}
         last_codes, last_planes = {}, {}
 
         def multiply(i, e, opens):
@@ -198,17 +230,17 @@ def tile_moe_two_lin_silu_kernel(
             cols = slice(e * C, (e + 1) * C)
             half, in_half = e // 4, slice(e % 4 * C, (e % 4 + 1) * C)
             if fmt == "e4m3":
-                w, j = words8[:, A8 * e + a, :].bitcast(FP8X4), E * A4 + A8 * e + a
+                view, j = FP8X4, HALF * A4 + A8 * (e % HALF) + a
             else:
-                w, j = words4[:, A4 * e + a, :].bitcast(FP4X4), A4 * e + a
+                view, j = FP4X4, A4 * (e % HALF) + a
             if tile_no == 1:
                 plane = last_planes[half][first:P, in_half]
             else:
                 plane = moved_plane[:, cols] if i == MOVED else early_plane[:, cols]
             nc.tensor.matmul_mx(
                 out=acc[e][:],
-                lhsT=w,
-                lhsT_scale=w_planes[:, j, :].bitcast(U8),
+                lhsT=words[fmt, e, a].bitcast(view),
+                lhsT_scale=w_planes[half][:, j, :].bitcast(U8),
                 rhs=(last_codes[half][:, in_half] if i == LAST else slot_codes[i][:, cols]).bitcast(FP8X4),
                 rhs_scale=plane,
                 start=opens,
@@ -216,7 +248,9 @@ def tile_moe_two_lin_silu_kernel(
             )
 
         def experts(pair, y):
-            order = ((0, MOVED), (2, 3), (LAST,)) if pair < 3 else ((2, 3), (0, MOVED, LAST))
+            order = ((0, MOVED), (2, 3), (LAST,)) if pair == 0 else ((2, 3), (0, MOVED, LAST))
+            for e in (2 * pair, 2 * pair + 1):
+                acc[e] = psum.tile([P, C], F32, name=f"acc{e}", tag=f"bank{e % 2 if pair < 2 else e}")
             for passes in order:
                 for e in (2 * pair, 2 * pair + 1):
                     for i in passes:

@@ -18,7 +18,6 @@ FP8X4 = mybir.dt.float8_e4m3fn_x4
 FP4X4 = mybir.dt.float4_e2m1fn_x4
 ACT = mybir.ActivationFunctionType
 MULT = mybir.AluOpType.mult
-ADD = mybir.AluOpType.add
 
 P = 128
 PACK = 4
@@ -35,7 +34,6 @@ HALVES = ((0, T // 2), (T // 2, T))
 LOADS = (((0, T),), ((0, T),), HALVES, HALVES, QUANT)
 VECTOR_SHARE = ((768,), (704,), (0, 0), (0, 128), (0, 128, 128))
 
-SCALAR_LATE = (448, 736)
 WORD_LOADS = (
     (("e2m1", 0, 2), ("e4m3", 0, 2)),
     (("e4m3", 2, 4), ("e2m1", 2, 4)),
@@ -44,7 +42,6 @@ WORD_LOADS = (
 )
 HALF = E // 2
 HALF_PLANES = HALF * (A4 + A8)
-OUT_CHUNKS = ((0, 384), (384, 896), (896, T))
 W4_BYTES, W8_BYTES = A4 * 2 * N, A8 * 4 * N
 PAIR_BYTES = 2 * (W4_BYTES + W8_BYTES)
 
@@ -66,9 +63,8 @@ def tile_moe_two_lin_silu_kernel(
         ident = tile("ident", [P, P], F32)
         gate_first = tile("gate_first", [P, PAIR], F32)
         gate_rest = tile("gate_rest", [P, S - PAIR], F32)
-        scalar_window = tile("scalar_window", [P, T + E], F32)
-        b_sb = scalar_window[:, T:]
-        vector_window = tile("vector_window", [P, T], F32)
+        window = tile("window", [P, T], F32)
+        b_sb = tile("b_sb", [P, E], F32)
         all_codes = tile("all_codes", [P, len(PASSES) * T + SPARE], U32)
         codes = [all_codes[:, (LAST - i) * T : (LAST - i + 1) * T] for i in range(len(PASSES))]
         windows = [all_codes[:, (LAST - i) * T : (LAST - i + 1) * T + SPARE] for i in range(len(PASSES))]
@@ -84,8 +80,7 @@ def tile_moe_two_lin_silu_kernel(
         for plane in planes:
             nc.gpsimd.memset(plane[:].bitcast(I32), 0)
         nc.gpsimd.memset(moved_plane[:].bitcast(I32), 0)
-        nc.vector.memset(scalar_window[:, :T], 0.0)
-        nc.vector.memset(vector_window[:], 0.0)
+        nc.vector.memset(window[:], 0.0)
         nc.vector.memset(all_codes[:, len(PASSES) * T :].bitcast(I32), 0)
 
         def pass_rows(i):
@@ -188,7 +183,7 @@ def tile_moe_two_lin_silu_kernel(
         nc.sync.dma_start(offs_sb[:], offs)
         load_pass(1, slices_of(tile("raw1", [P, PACK * T], F32)))
         nc.sync.dma_start(dst_sb[:], dst)
-        nc.sync.dma_start(out=b_sb, in_=b)
+        nc.sync.dma_start(out=b_sb[:], in_=b)
         for i in (2, 3):
             load_pass(i, lambda c0, c1: tile(f"raw{i}_{c0}", [P, PACK * (c1 - c0)], F32)[:, :])
         load_scale_rows(0, w_planes[0])
@@ -272,7 +267,7 @@ def tile_moe_two_lin_silu_kernel(
         experts(0, y_first)
         gated_first = tile("gated_first", [P, PAIR], F32)
         nc.vector.tensor_tensor(gated_first[:], y_first[:], gate_first[:], MULT)
-        nc.scalar.activation(places(scalar_window, 0, PAIR), gated_first[:], ACT.Copy)
+        nc.scalar.activation(places(window, 0, PAIR), gated_first[:], ACT.Copy)
 
         last_codes[1] = tile("last_codes1", [P, 2 * PAIR], U32, on="y_first")
         last_planes[1] = tile("last_planes1", [P, 2 * PAIR], U8, on="gate_first")
@@ -282,16 +277,7 @@ def tile_moe_two_lin_silu_kernel(
         y_rest = tile("y_rest", [P, S - PAIR], F32)
         for pair in range(1, E // 2):
             experts(pair, y_rest[:, (pair - 1) * PAIR : pair * PAIR])
-        s0, s1 = SCALAR_LATE
-
-        def times_gate(into, j0, j1):
-            nc.vector.tensor_tensor(into, y_rest[:, j0 - PAIR : j1 - PAIR], gate_rest[:, j0 - PAIR : j1 - PAIR], MULT)
-
-        times_gate(places(vector_window, PAIR, s0), PAIR, s0)
-        gated_late = tile("gated_late", [P, s1 - s0], F32)
-        times_gate(gated_late[:], s0, s1)
-        nc.scalar.activation(places(scalar_window, s0, s1), gated_late[:], ACT.Copy)
-        times_gate(places(vector_window, s1, S), s1, S)
-        for c0, c1 in OUT_CHUNKS:
-            nc.vector.tensor_tensor(vector_window[:, c0:c1], vector_window[:, c0:c1], scalar_window[:, c0:c1], ADD)
-            nc.sync.dma_start(out=out[:, c0:c1], in_=vector_window[:, c0:c1])
+        for j0, j1 in ((PAIR, 2 * PAIR), (2 * PAIR, S)):
+            cols = slice(j0 - PAIR, j1 - PAIR)
+            nc.vector.tensor_tensor(places(window, j0, j1), y_rest[:, cols], gate_rest[:, cols], MULT)
+        nc.sync.dma_start(out=out, in_=window[:])

@@ -40,8 +40,10 @@ WORD_LOADS = (
     (("e4m3", 4, 6), ("e2m1", 4, 6)),
     (("e4m3", 6, 8), ("e2m1", 6, 7), ("e2m1", 7, 8)),
 )
-HALF = E // 2
-HALF_PLANES = HALF * (A4 + A8)
+GROUPS = ((0, 4), (4, E))
+PLANES = [(e1 - e0) * (A4 + A8) for e0, e1 in GROUPS]
+ON = ("raw2_640", "first_rows1", "grouped3")
+VECTOR_SCATTERS = ((256, 512), (512, 1024))
 W4_BYTES, W8_BYTES = A4 * 2 * N, A8 * 4 * N
 PAIR_BYTES = 2 * (W4_BYTES + W8_BYTES)
 
@@ -52,7 +54,6 @@ def tile_moe_two_lin_silu_kernel(
     nc = tc.nc
     with ExitStack() as ctx:
         keep = ctx.enter_context(tc.tile_pool(name="keep", bufs=1))
-        stage = ctx.enter_context(tc.tile_pool(name="stage", bufs=4))
         psum = ctx.enter_context(tc.psum_pool(name="psum", bufs=1))
 
         def tile(name, shape, dtype, on=None):
@@ -64,7 +65,6 @@ def tile_moe_two_lin_silu_kernel(
         gate_first = tile("gate_first", [P, PAIR], F32)
         gate_rest = tile("gate_rest", [P, S - PAIR], F32)
         window = tile("window", [P, T], F32)
-        b_sb = tile("b_sb", [P, E], F32)
         all_codes = tile("all_codes", [P, len(PASSES) * T + SPARE], U32)
         codes = [all_codes[:, (LAST - i) * T : (LAST - i + 1) * T] for i in range(len(PASSES))]
         windows = [all_codes[:, (LAST - i) * T : (LAST - i + 1) * T + SPARE] for i in range(len(PASSES))]
@@ -72,7 +72,7 @@ def tile_moe_two_lin_silu_kernel(
         slot_codes = [tile(f"slot_codes{i}", [P, S], U32) for i in range(LAST)]
         early_plane = tile("early_plane", [P, S], U8)
         moved_plane = tile("moved_plane", [P, S], U8)
-        w_planes = [tile(f"w_planes{h}", [P, HALF_PLANES, N // 4], I32) for h in range(2)]
+        w_planes = [tile(f"w_planes{h}", [P, PLANES[h], N // 4], I32) for h in range(2)]
 
         make_identity(nc, ident[:])
         for plane in w_planes:
@@ -138,8 +138,9 @@ def tile_moe_two_lin_silu_kernel(
             nc.vector.tensor_copy(into, window.indirect(offs_sb[:, s0 // 16 : s1 // 16]))
 
         def load_scale_rows(h, into):
-            for scales, j0, j1 in ((w4_scales, 0, HALF * A4), (w8_scales, HALF * A4, HALF_PLANES)):
-                rows = scales[h * HALF : (h + 1) * HALF].rearrange("e a q n -> q (e a) n")
+            e0, e1 = GROUPS[h]
+            for scales, j0, j1 in ((w4_scales, 0, (e1 - e0) * A4), (w8_scales, (e1 - e0) * A4, PLANES[h])):
+                rows = scales[e0:e1].rearrange("e a q n -> q (e a) n")
                 nc.sync.dma_start(out=into[0:P:8, j0:j1, :], in_=rows.bitcast(I32))
 
         def place_scale_rows(h, staged, first_row):
@@ -181,17 +182,19 @@ def tile_moe_two_lin_silu_kernel(
         for u in range(2):
             nc.sync.dma_start(out=first_rows[u][:], in_=pass_rows(0)[:, 2 * u : 2 * u + 2, :])
         nc.sync.dma_start(offs_sb[:], offs)
+        gate_row = tile("gate_row", [P, S // P], F32)
+        nc.sync.dma_start(out=gate_row[:], in_=gate[0:1, :].rearrange("o (p i) -> (o p) i", i=S // P))
         load_pass(1, slices_of(tile("raw1", [P, PACK * T], F32)))
         nc.sync.dma_start(dst_sb[:], dst)
-        nc.sync.dma_start(out=b_sb[:], in_=b)
-        for i in (2, 3):
-            load_pass(i, lambda c0, c1: tile(f"raw{i}_{c0}", [P, PACK * (c1 - c0)], F32)[:, :])
+        load_pass(2, lambda c0, c1: tile(f"raw2_{c0}", [P, PACK * (c1 - c0)], F32)[:, :])
         load_scale_rows(0, w_planes[0])
 
         for i in range(len(PASSES)):
-            grouped = stage.tile([P, T, PACK], BF16, name="grouped", align_bytes=64)
+            grouped = tile(f"grouped{i}", [P, T, PACK], BF16)
             interleave(i, grouped)
             quantize(i, grouped)
+            if i == 0:
+                load_pass(3, lambda c0, c1: tile(f"raw3_{c0}", [P, PACK * (c1 - c0)], F32, on=f"first_rows{c1 // T}")[:, :])
             if i == MOVED:
                 gather(early_plane[:], planes[0][:], 0, S)
                 for r in range(4):
@@ -199,22 +202,22 @@ def tile_moe_two_lin_silu_kernel(
                         out=moved_plane[r:P:32, :].bitcast(I32),
                         in_=early_plane[PASSES[MOVED][3] + r : P : 32, :].bitcast(I32),
                     )
+                load_pass(LAST, slices_of(tile("raw4", [P, PACK * T], F32, on="planes0")))
             if i < LAST:
                 gather(slot_codes[i][:], windows[i], 0, S)
             if i == 2:
-                load_pass(LAST, slices_of(tile("raw4", [P, PACK * T], F32, on=f"raw2_{T // 2}")))
-            if i == 3:
-                gate_row = tile("gate_row", [P, S // P], F32, on="raw3_0")[:, :]
-                nc.sync.dma_start(out=gate_row, in_=gate[0:1, :].rearrange("o (p i) -> (o p) i", i=S // P))
+                staged = tile("staged", [P, PLANES[1], N // 4], I32, on="raw2_0")
+                load_scale_rows(1, staged)
                 place_scale_rows(0, w_planes[0], 1)
-                later = tile("later", [P, 3 * PAIR_BYTES + HALF_PLANES * N], U8, on=f"raw3_{T // 2}")
-                staged = later[:, 3 * PAIR_BYTES :].bitcast(I32).rearrange("p (j n) -> p j n", n=N // 4)
-                for pair in range(3):
-                    load_pair(pair, later[:, pair * PAIR_BYTES : (pair + 1) * PAIR_BYTES])
-                    if pair == 0:
-                        load_scale_rows(1, staged)
+                load_pair(0, tile("words0", [P, PAIR_BYTES], U8, on=ON[0])[:, :])
+            if i == 3:
+                b_sb = tile("b_sb", [P, E], F32, on=ON[1])
+                nc.sync.dma_start(out=b_sb[:], in_=b)
+                load_pair(1, tile("words1", [P, PAIR_BYTES], U8, on=ON[2])[:, :])
                 place_scale_rows(1, staged, 0)
-        load_pair(3, tile("final", [P, PAIR_BYTES], U8, on=f"raw2_{T // 2}")[:, :])
+        late_words = tile("late_words", [P, 2 * PAIR_BYTES], U8, on="planes0")
+        for pair in (2, 3):
+            load_pair(pair, late_words[:, (pair - 2) * PAIR_BYTES : (pair - 1) * PAIR_BYTES])
         spread_gate()
 
         acc = {}
@@ -224,10 +227,12 @@ def tile_moe_two_lin_silu_kernel(
             fmt, a, tile_no, first = PASSES[i]
             cols = slice(e * C, (e + 1) * C)
             half, in_half = e // 4, slice(e % 4 * C, (e % 4 + 1) * C)
+            group = int(e >= GROUPS[1][0])
+            e0, e1 = GROUPS[group]
             if fmt == "e4m3":
-                view, j = FP8X4, HALF * A4 + A8 * (e % HALF) + a
+                view, j = FP8X4, (e1 - e0) * A4 + A8 * (e - e0) + a
             else:
-                view, j = FP4X4, A4 * (e % HALF) + a
+                view, j = FP4X4, A4 * (e - e0) + a
             if tile_no == 1:
                 plane = last_planes[half][first:P, in_half]
             else:
@@ -235,7 +240,7 @@ def tile_moe_two_lin_silu_kernel(
             nc.tensor.matmul_mx(
                 out=acc[e][:],
                 lhsT=words[fmt, e, a].bitcast(view),
-                lhsT_scale=w_planes[half][:, j, :].bitcast(U8),
+                lhsT_scale=w_planes[group][:, j, :].bitcast(U8),
                 rhs=(last_codes[half][:, in_half] if i == LAST else slot_codes[i][:, cols]).bitcast(FP8X4),
                 rhs_scale=plane,
                 start=opens,
@@ -271,13 +276,14 @@ def tile_moe_two_lin_silu_kernel(
 
         last_codes[1] = tile("last_codes1", [P, 2 * PAIR], U32, on="y_first")
         last_planes[1] = tile("last_planes1", [P, 2 * PAIR], U8, on="gate_first")
-        gather(last_planes[1][:], planes[1][:], 2 * PAIR, S)
-        gather(last_codes[1][:, :PAIR], windows[LAST], 2 * PAIR, 3 * PAIR)
-        gather(last_codes[1][:, PAIR:], windows[LAST], 3 * PAIR, S)
+        for q in range(2):
+            cols = slice(q * PAIR, (q + 1) * PAIR)
+            gather(last_planes[1][:, cols], planes[1][:], (2 + q) * PAIR, (3 + q) * PAIR)
+            gather(last_codes[1][:, cols], windows[LAST], (2 + q) * PAIR, (3 + q) * PAIR)
         y_rest = tile("y_rest", [P, S - PAIR], F32)
         for pair in range(1, E // 2):
             experts(pair, y_rest[:, (pair - 1) * PAIR : pair * PAIR])
-        for j0, j1 in ((PAIR, 2 * PAIR), (2 * PAIR, S)):
+        for j0, j1 in VECTOR_SCATTERS:
             cols = slice(j0 - PAIR, j1 - PAIR)
             nc.vector.tensor_tensor(places(window, j0, j1), y_rest[:, cols], gate_rest[:, cols], MULT)
         nc.sync.dma_start(out=out, in_=window[:])

@@ -32,7 +32,7 @@ MOVED, LAST = 1, 4
 QUANT = ((0, 512), (512, 1024), (1024, T))
 HALVES = ((0, T // 2), (T // 2, T))
 LOADS = (((0, T),), ((0, T),), HALVES, HALVES, QUANT)
-VECTOR_SHARE = ((768,), (704,), (0, 0), (0, 128), (0, 128, 128))
+VECTOR_SHARE = ((768,), (704,), (0, 0), (0, 256), (0, 192, 128))
 
 WORD_LOADS = (
     (("e2m1", 0, 2), ("e4m3", 0, 2)),
@@ -40,7 +40,7 @@ WORD_LOADS = (
     (("e4m3", 4, 6), ("e2m1", 4, 6)),
     (("e4m3", 6, 8), ("e2m1", 6, 7), ("e2m1", 7, 8)),
 )
-GROUPS = ((0, 4), (4, E))
+GROUPS = ((0, 2), (2, E))
 PLANES = [(e1 - e0) * (A4 + A8) for e0, e1 in GROUPS]
 ON = ("raw2_640", "first_rows1", "grouped3")
 VECTOR_SCATTERS = ((256, 512), (512, 1024))
@@ -185,8 +185,8 @@ def tile_moe_two_lin_silu_kernel(
         gate_row = tile("gate_row", [P, S // P], F32)
         nc.sync.dma_start(out=gate_row[:], in_=gate[0:1, :].rearrange("o (p i) -> (o p) i", i=S // P))
         load_pass(1, slices_of(tile("raw1", [P, PACK * T], F32)))
-        nc.sync.dma_start(dst_sb[:], dst)
         load_pass(2, lambda c0, c1: tile(f"raw2_{c0}", [P, PACK * (c1 - c0)], F32)[:, :])
+        nc.sync.dma_start(dst_sb[:], dst)
         load_scale_rows(0, w_planes[0])
 
         for i in range(len(PASSES)):

@@ -31,8 +31,8 @@ MOVED, LAST = 1, 4
 
 QUANT = ((0, 512), (512, 1024), (1024, T))
 HALVES = ((0, T // 2), (T // 2, T))
-LOADS = (((0, T),), ((0, T),), HALVES, HALVES, QUANT)
-VECTOR_SHARE = ((768,), (704,), (0, 0), (0, 256), (0, 192, 128))
+LOADS = (((0, T),), ((0, T),), HALVES, ((0, T),), QUANT)
+VECTOR_SHARE = ((768,), (640,), (0, 0), (640,), (0, 192, 128))
 
 WORD_LOADS = (
     (("e2m1", 0, 2), ("e4m3", 0, 2)),
@@ -42,7 +42,9 @@ WORD_LOADS = (
 )
 GROUPS = ((0, 2), (2, E))
 PLANES = [(e1 - e0) * (A4 + A8) for e0, e1 in GROUPS]
-ON = ("raw2_640", "first_rows1", "grouped3")
+ON = ("grouped2", "first_rows1", "grouped3")
+LAST_LOAD = (None, "raw1", "raw2_640", "first_rows1", "planes0")
+GATE_AT, B_AT = P - 2, P - 1
 VECTOR_SCATTERS = ((256, 512), (512, 1024))
 W4_BYTES, W8_BYTES = A4 * 2 * N, A8 * 4 * N
 PAIR_BYTES = 2 * (W4_BYTES + W8_BYTES)
@@ -65,23 +67,28 @@ def tile_moe_two_lin_silu_kernel(
         gate_first = tile("gate_first", [P, PAIR], F32)
         gate_rest = tile("gate_rest", [P, S - PAIR], F32)
         window = tile("window", [P, T], F32)
-        all_codes = tile("all_codes", [P, len(PASSES) * T + SPARE], U32)
-        codes = [all_codes[:, (LAST - i) * T : (LAST - i + 1) * T] for i in range(len(PASSES))]
-        windows = [all_codes[:, (LAST - i) * T : (LAST - i + 1) * T + SPARE] for i in range(len(PASSES))]
+        codes = [tile(f"codes{i}", [P, T], U32) for i in range(len(PASSES))]
+        windows = [whole[:] for whole in codes]
         planes = [tile(f"planes{i}", [P, T + SPARE], U8) for i in range(2)]
-        slot_codes = [tile(f"slot_codes{i}", [P, S], U32) for i in range(LAST)]
+        slot_codes = [tile(f"slot_codes{i}", [P, S - C], U32) for i in range(LAST)]
+        held_codes = []
         early_plane = tile("early_plane", [P, S], U8)
         moved_plane = tile("moved_plane", [P, S], U8)
         w_planes = [tile(f"w_planes{h}", [P, PLANES[h], N // 4], I32) for h in range(2)]
 
+        flat = tile("flat", [P, S], F32)
+        gate_row = tile("gate_row", [P, E], F32)
+        b_sb = tile("b_sb", [P, E], F32)
+        b_first = tile("b_first", [P, 2], F32)
+
         make_identity(nc, ident[:])
+        nc.gpsimd.memset(flat[:GATE_AT, :], 0.0)
         for plane in w_planes:
             nc.vector.memset(plane[:], 0)
         for plane in planes:
             nc.gpsimd.memset(plane[:].bitcast(I32), 0)
         nc.gpsimd.memset(moved_plane[:].bitcast(I32), 0)
         nc.vector.memset(window[:], 0.0)
-        nc.vector.memset(all_codes[:, len(PASSES) * T :].bitcast(I32), 0)
 
         def pass_rows(i):
             fmt, a, tile_no, first = PASSES[i]
@@ -166,6 +173,16 @@ def tile_moe_two_lin_silu_kernel(
                 load_words(fmt, e0, e1, into[:, at : at + width])
                 at = at + width
 
+        def turn_rows():
+            by_eight = flat[:].rearrange("p (m i) -> p i m", i=E)
+            for half in range(2):
+                turned = psum.tile([P, 4, P], F32, name="turned", tag=f"bank{E - 4 + half}")
+                for q in range(4):
+                    nc.tensor.transpose(turned[:, q, :], by_eight[:, 4 * half + q, :], ident[:])
+                nc.scalar.copy(gate_row[:, 4 * half : 4 * half + 4], turned[:, :, GATE_AT])
+                nc.scalar.copy(b_sb[:, 4 * half : 4 * half + 4], turned[:, :, B_AT])
+            nc.scalar.copy(b_first[:], b_sb[:, :2])
+
         def spread_gate():
             for half in range(2):
                 spread = psum.tile([P, 4, P], F32, name="spread", tag=f"bank{E - 2 + half}")
@@ -181,9 +198,9 @@ def tile_moe_two_lin_silu_kernel(
         first_rows = [tile(f"first_rows{u}", [P, 2, T], F32) for u in range(2)]
         for u in range(2):
             nc.sync.dma_start(out=first_rows[u][:], in_=pass_rows(0)[:, 2 * u : 2 * u + 2, :])
+        nc.sync.dma_start(out=flat[GATE_AT : GATE_AT + 1, :], in_=gate[0:1, :])
+        nc.sync.dma_start(out=flat[B_AT : B_AT + 1, :], in_=b.rearrange("(o n) e -> o (n e)", o=1))
         nc.sync.dma_start(offs_sb[:], offs)
-        gate_row = tile("gate_row", [P, S // P], F32)
-        nc.sync.dma_start(out=gate_row[:], in_=gate[0:1, :].rearrange("o (p i) -> (o p) i", i=S // P))
         load_pass(1, slices_of(tile("raw1", [P, PACK * T], F32)))
         load_pass(2, lambda c0, c1: tile(f"raw2_{c0}", [P, PACK * (c1 - c0)], F32)[:, :])
         nc.sync.dma_start(dst_sb[:], dst)
@@ -193,6 +210,9 @@ def tile_moe_two_lin_silu_kernel(
             grouped = tile(f"grouped{i}", [P, T, PACK], BF16)
             interleave(i, grouped)
             quantize(i, grouped)
+            if i > 0:
+                held_codes.append(tile(f"held_codes{i - 1}", [P, C], U32, on=LAST_LOAD[i]))
+                gather(held_codes[i - 1][:], windows[i - 1], S - C, S)
             if i == 0:
                 load_pass(3, lambda c0, c1: tile(f"raw3_{c0}", [P, PACK * (c1 - c0)], F32, on=f"first_rows{c1 // T}")[:, :])
             if i == MOVED:
@@ -204,20 +224,19 @@ def tile_moe_two_lin_silu_kernel(
                     )
                 load_pass(LAST, slices_of(tile("raw4", [P, PACK * T], F32, on="planes0")))
             if i < LAST:
-                gather(slot_codes[i][:], windows[i], 0, S)
+                gather(slot_codes[i][:], windows[i], 0, S - C)
             if i == 2:
                 staged = tile("staged", [P, PLANES[1], N // 4], I32, on="raw2_0")
                 load_scale_rows(1, staged)
                 place_scale_rows(0, w_planes[0], 1)
                 load_pair(0, tile("words0", [P, PAIR_BYTES], U8, on=ON[0])[:, :])
             if i == 3:
-                b_sb = tile("b_sb", [P, E], F32, on=ON[1])
-                nc.sync.dma_start(out=b_sb[:], in_=b)
                 load_pair(1, tile("words1", [P, PAIR_BYTES], U8, on=ON[2])[:, :])
                 place_scale_rows(1, staged, 0)
-        late_words = tile("late_words", [P, 2 * PAIR_BYTES], U8, on="planes0")
+        late_words = tile("late_words", [P, 2 * PAIR_BYTES], U8, on="grouped4")
         for pair in (2, 3):
             load_pair(pair, late_words[:, (pair - 2) * PAIR_BYTES : (pair - 1) * PAIR_BYTES])
+        turn_rows()
         spread_gate()
 
         acc = {}
@@ -237,11 +256,15 @@ def tile_moe_two_lin_silu_kernel(
                 plane = last_planes[half][first:P, in_half]
             else:
                 plane = moved_plane[:, cols] if i == MOVED else early_plane[:, cols]
+            if i == LAST:
+                tokens = last_codes[half][:, in_half]
+            else:
+                tokens = held_codes[i][:] if e == E - 1 else slot_codes[i][:, cols]
             nc.tensor.matmul_mx(
                 out=acc[e][:],
                 lhsT=words[fmt, e, a].bitcast(view),
                 lhsT_scale=w_planes[group][:, j, :].bitcast(U8),
-                rhs=(last_codes[half][:, in_half] if i == LAST else slot_codes[i][:, cols]).bitcast(FP8X4),
+                rhs=tokens.bitcast(FP8X4),
                 rhs_scale=plane,
                 start=opens,
                 stop=(i == LAST),
@@ -257,7 +280,7 @@ def tile_moe_two_lin_silu_kernel(
                         multiply(i, e, i == order[0][0])
             for q in range(2):
                 e = 2 * pair + q
-                nc.scalar.activation(y[:, q * C : (q + 1) * C], acc[e][:], ACT.Silu, bias=b_sb[:, e : e + 1])
+                nc.scalar.activation(y[:, q * C : (q + 1) * C], acc[e][:], ACT.Silu, bias=(b_first if pair == 0 else b_sb)[:, e : e + 1])
 
         def places(window, s0, s1):
             return window[:].indirect(dst_sb[:, s0 // 16 : s1 // 16])
@@ -275,7 +298,7 @@ def tile_moe_two_lin_silu_kernel(
         nc.scalar.activation(places(window, 0, PAIR), gated_first[:], ACT.Copy)
 
         last_codes[1] = tile("last_codes1", [P, 2 * PAIR], U32, on="y_first")
-        last_planes[1] = tile("last_planes1", [P, 2 * PAIR], U8, on="gate_first")
+        last_planes[1] = tile("last_planes1", [P, 2 * PAIR], U8, on="b_first")
         for q in range(2):
             cols = slice(q * PAIR, (q + 1) * PAIR)
             gather(last_planes[1][:, cols], planes[1][:], (2 + q) * PAIR, (3 + q) * PAIR)

@@ -1,3 +1,4 @@
+import math
 from contextlib import ExitStack
 
 import concourse.mybir as mybir
@@ -16,6 +17,7 @@ U16 = mybir.dt.uint16
 U8 = mybir.dt.uint8
 FP8X4 = mybir.dt.float8_e4m3fn_x4
 FP4X4 = mybir.dt.float4_e2m1fn_x4
+BYTES_OF = {F32: 4, BF16: 2, I32: 4, U32: 4, U8: 1}
 ACT = mybir.ActivationFunctionType
 MULT = mybir.AluOpType.mult
 
@@ -30,9 +32,14 @@ PASSES = (("e2m1", 0, 0, 0), ("e2m1", 1, 0, 4), ("e4m3", 0, 1, 4), ("e4m3", 1, 1
 MOVED, LAST = 1, 4
 
 QUANT = ((0, 512), (512, 1024), (1024, T))
-HALVES = ((0, T // 2), (T // 2, T))
-LOADS = (((0, T),), ((0, T),), HALVES, ((0, T),), QUANT)
-VECTOR_SHARE = ((768,), (640,), (0, 0), (640,), (0, 192, 128))
+LOADS = (((0, T),), ((0, T),), ((0, T),), ((0, T),), QUANT)
+ROUNDING = (
+    (("vector", 512, T), ("scalar", 0, 512)),
+    (("vector", 0, 512), ("vector", 512, 640), ("scalar", 640, 1024), ("scalar", 1024, T)),
+    (("vector", 512, 736), ("scalar", 0, 512), ("scalar", 736, 1024), ("gpsimd", 1024, T)),
+    (("vector", 512, 832), ("scalar", 0, 512), ("scalar", 832, 1024), ("gpsimd", 1024, T)),
+    (("scalar", 0, 512), ("vector", 832, 1024), ("scalar", 512, 832), ("vector", 1152, T), ("scalar", 1024, 1152)),
+)
 
 WORD_LOADS = (
     (("e2m1", 0, 2), ("e4m3", 0, 2)),
@@ -42,8 +49,6 @@ WORD_LOADS = (
 )
 GROUPS = ((0, 2), (2, E))
 PLANES = [(e1 - e0) * (A4 + A8) for e0, e1 in GROUPS]
-ON = ("grouped2", "first_rows1", "grouped3")
-LAST_LOAD = (None, "raw1", "raw2_640", "first_rows1", "planes0")
 GATE_AT, B_AT = P - 2, P - 1
 VECTOR_SCATTERS = ((256, 512), (512, 1024))
 W4_BYTES, W8_BYTES = A4 * 2 * N, A8 * 4 * N
@@ -58,18 +63,30 @@ def tile_moe_two_lin_silu_kernel(
         keep = ctx.enter_context(tc.tile_pool(name="keep", bufs=1))
         psum = ctx.enter_context(tc.psum_pool(name="psum", bufs=1))
 
-        def tile(name, shape, dtype, on=None):
-            return keep.tile(shape, dtype, name=name, tag=on or name, align_bytes=64)
+        lists = ctx.enter_context(tc.tile_pool(name="lists", bufs=1))
+        place = {"free": 0}
 
-        offs_sb = keep.tile([P, S // 16], U16, name="offs_sb")
-        dst_sb = keep.tile([P, S // 16], U16, name="dst_sb")
+        def tile(name, shape, dtype, on=None, at=0, room=0):
+            size = math.prod(shape[1:]) * BYTES_OF[dtype]
+            if on is None:
+                place[name] = place["free"]
+                place["free"] = place["free"] + 64 * -(-max(size, room) // 64)
+            else:
+                place[name] = place[on] + at
+            return keep.tile(shape, dtype, name=name, align_bytes=64, offset=place[name])
+
+        offs_sb = lists.tile([P, S // 16], U16, name="offs_sb")
+        dst_sb = lists.tile([P, S // 16], U16, name="dst_sb")
         ident = tile("ident", [P, P], F32)
         gate_first = tile("gate_first", [P, PAIR], F32)
         gate_rest = tile("gate_rest", [P, S - PAIR], F32)
         window = tile("window", [P, T], F32)
         codes = [tile(f"codes{i}", [P, T], U32) for i in range(len(PASSES))]
         windows = [whole[:] for whole in codes]
-        planes = [tile(f"planes{i}", [P, T + SPARE], U8) for i in range(2)]
+        tile_room = 2048 + 4 * PACK * T
+        place["around_planes0"] = place["free"]
+        place["free"] = place["free"] + tile_room
+        planes = [tile("planes0", [P, T + SPARE], U8, on="around_planes0", at=1280), tile("planes1", [P, T + SPARE], U8)]
         slot_codes = [tile(f"slot_codes{i}", [P, S - C], U32) for i in range(LAST)]
         held_codes = []
         early_plane = tile("early_plane", [P, S], U8)
@@ -79,7 +96,7 @@ def tile_moe_two_lin_silu_kernel(
         flat = tile("flat", [P, S], F32)
         gate_row = tile("gate_row", [P, E], F32)
         b_sb = tile("b_sb", [P, E], F32)
-        b_first = tile("b_first", [P, 2], F32)
+        b_first = tile("b_first", [P, 2], F32, room=2 * PAIR)
 
         make_identity(nc, ident[:])
         nc.gpsimd.memset(flat[:GATE_AT, :], 0.0)
@@ -109,28 +126,24 @@ def tile_moe_two_lin_silu_kernel(
             views = (into.rearrange("p (c i) t -> p c t i", i=4), rows.rearrange("p t (c i) -> p c t i", i=4))
             if engine == "vector":
                 nc.vector.tensor_copy(*views)
+            elif engine == "gpsimd":
+                nc.gpsimd.tensor_copy(into, rows.rearrange("p t c -> p c t"))
             else:
                 nc.scalar.activation(*views, ACT.Copy)
 
-        def cut(c0, c1):
-            ends = [c0] + [end for start, end in QUANT if c0 < end < c1] + [c1]
-            return [(a, z) for a, z in zip(ends, ends[1:]) if z > a]
+        def columns(grouped, c0, c1):
+            start = max(at for at in grouped if at <= c0)
+            return grouped[start][:, c0 - start : c1 - start, :]
 
         def interleave(i, grouped):
             if i == 0:
-                split = T - VECTOR_SHARE[0][0]
                 for u in range(2):
-                    for engine, c0, c1 in (("vector", split, T), ("scalar", 0, split)):
-                        round_and_group(engine, grouped[:, c0:c1, 2 * u : 2 * u + 2], first_rows[u][:, :, c0:c1])
+                    for engine, c0, c1 in ROUNDING[0]:
+                        round_and_group(engine, grouped[0][:, c0:c1, 2 * u : 2 * u + 2], first_rows[u][:, :, c0:c1])
                 return
-            for (l0, l1), share in zip(LOADS[i], VECTOR_SHARE[i]):
-                if l1 - l0 == T:
-                    parts = (("vector", l0, l0 + share), ("scalar", l0 + share, l1))
-                else:
-                    parts = (("vector", l1 - share, l1), ("scalar", l0, l1 - share))
-                for engine, s0, s1 in parts:
-                    for c0, c1 in cut(s0, s1):
-                        round_and_group(engine, grouped[:, c0:c1, :], raw[i, l0][:, :, c0 - l0 : c1 - l0])
+            for engine, c0, c1 in ROUNDING[i]:
+                l0 = max(start for start, end in LOADS[i] if start <= c0)
+                round_and_group(engine, columns(grouped, c0, c1), raw[i, l0][:, :, c0 - l0 : c1 - l0])
 
         def quantize(i, grouped):
             fmt, a, tile_no, first = PASSES[i]
@@ -138,7 +151,7 @@ def tile_moe_two_lin_silu_kernel(
                 nc.vector.quantize_mx(
                     out=codes[i][:, c0:c1].bitcast(FP8X4),
                     scales=planes[tile_no][first:P, c0:c1],
-                    in_=grouped[:, c0:c1, :].rearrange("p c t -> p (c t)"),
+                    in_=columns(grouped, c0, c1).rearrange("p c t -> p (c t)"),
                 )
 
         def gather(into, window, s0, s1):
@@ -195,26 +208,40 @@ def tile_moe_two_lin_silu_kernel(
                         spread[:, :, p0:p1].rearrange("m q p -> m p q"),
                     )
 
-        first_rows = [tile(f"first_rows{u}", [P, 2, T], F32) for u in range(2)]
+        first_rows = [tile(f"first_rows{u}", [P, 2, T], F32, room=u * 4 * PACK * T) for u in range(2)]
         for u in range(2):
             nc.sync.dma_start(out=first_rows[u][:], in_=pass_rows(0)[:, 2 * u : 2 * u + 2, :])
         nc.sync.dma_start(out=flat[GATE_AT : GATE_AT + 1, :], in_=gate[0:1, :])
         nc.sync.dma_start(out=flat[B_AT : B_AT + 1, :], in_=b.rearrange("(o n) e -> o (n e)", o=1))
         nc.sync.dma_start(offs_sb[:], offs)
         load_pass(1, slices_of(tile("raw1", [P, PACK * T], F32)))
-        load_pass(2, lambda c0, c1: tile(f"raw2_{c0}", [P, PACK * (c1 - c0)], F32)[:, :])
+        load_pass(2, slices_of(tile("raw2", [P, PACK * T], F32)))
         nc.sync.dma_start(dst_sb[:], dst)
         load_scale_rows(0, w_planes[0])
 
+        def grouped_tiles(i):
+            if i == 2:
+                return {
+                    0: tile("grouped2_0", [P, 512, PACK], BF16),
+                    512: tile("grouped2_512", [P, 512, PACK], BF16, room=2048 + PAIR_BYTES),
+                    1024: tile("grouped2_1024", [P, 256, PACK], BF16, on="around_planes0"),
+                }
+            if i == 3:
+                return {
+                    0: tile("grouped3_0", [P, 1024, PACK], BF16),
+                    1024: tile("grouped3_1024", [P, 256, PACK], BF16, on="grouped2_512"),
+                }
+            return {0: tile(f"grouped{i}_0", [P, T, PACK], BF16)}
+
         for i in range(len(PASSES)):
-            grouped = tile(f"grouped{i}", [P, T, PACK], BF16)
+            grouped = grouped_tiles(i)
             interleave(i, grouped)
             quantize(i, grouped)
             if i > 0:
-                held_codes.append(tile(f"held_codes{i - 1}", [P, C], U32, on=LAST_LOAD[i]))
+                held_codes.append(tile(f"held_codes{i - 1}", [P, C], U32, on=f"raw{i}"))
                 gather(held_codes[i - 1][:], windows[i - 1], S - C, S)
             if i == 0:
-                load_pass(3, lambda c0, c1: tile(f"raw3_{c0}", [P, PACK * (c1 - c0)], F32, on=f"first_rows{c1 // T}")[:, :])
+                load_pass(3, slices_of(tile("raw3", [P, PACK * T], F32, on="first_rows1")))
             if i == MOVED:
                 gather(early_plane[:], planes[0][:], 0, S)
                 for r in range(4):
@@ -222,18 +249,18 @@ def tile_moe_two_lin_silu_kernel(
                         out=moved_plane[r:P:32, :].bitcast(I32),
                         in_=early_plane[PASSES[MOVED][3] + r : P : 32, :].bitcast(I32),
                     )
-                load_pass(LAST, slices_of(tile("raw4", [P, PACK * T], F32, on="planes0")))
+                load_pass(LAST, slices_of(tile("raw4", [P, PACK * T], F32, on="around_planes0", at=2048)))
             if i < LAST:
                 gather(slot_codes[i][:], windows[i], 0, S - C)
             if i == 2:
-                staged = tile("staged", [P, PLANES[1], N // 4], I32, on="raw2_0")
+                staged = tile("staged", [P, PLANES[1], N // 4], I32, on="raw2", at=1024)
                 load_scale_rows(1, staged)
                 place_scale_rows(0, w_planes[0], 1)
-                load_pair(0, tile("words0", [P, PAIR_BYTES], U8, on=ON[0])[:, :])
+                load_pair(0, tile("words0", [P, PAIR_BYTES], U8, on="grouped2_512", at=2048)[:, :])
             if i == 3:
-                load_pair(1, tile("words1", [P, PAIR_BYTES], U8, on=ON[2])[:, :])
+                load_pair(1, tile("words1", [P, PAIR_BYTES], U8, on="grouped3_0")[:, :])
                 place_scale_rows(1, staged, 0)
-        late_words = tile("late_words", [P, 2 * PAIR_BYTES], U8, on="grouped4")
+        late_words = tile("late_words", [P, 2 * PAIR_BYTES], U8, on="grouped4_0")
         for pair in (2, 3):
             load_pair(pair, late_words[:, (pair - 2) * PAIR_BYTES : (pair - 1) * PAIR_BYTES])
         turn_rows()
@@ -291,7 +318,7 @@ def tile_moe_two_lin_silu_kernel(
         gather(last_codes[0][:, :PAIR], windows[LAST], 0, PAIR)
         gather(last_codes[0][:, PAIR:], windows[LAST], PAIR, 2 * PAIR)
         gather(last_planes[0][:, PAIR:], planes[1][:], PAIR, 2 * PAIR)
-        y_first = tile("y_first", [P, PAIR], F32)
+        y_first = tile("y_first", [P, PAIR], F32, room=8 * PAIR)
         experts(0, y_first)
         gated_first = tile("gated_first", [P, PAIR], F32)
         nc.vector.tensor_tensor(gated_first[:], y_first[:], gate_first[:], MULT)

@@ -32,12 +32,12 @@ PASSES = (("e2m1", 0, 0, 0), ("e2m1", 1, 0, 4), ("e4m3", 0, 1, 4), ("e4m3", 1, 1
 MOVED, LAST = 1, 4
 
 QUANT = ((0, 512), (512, 1024), (1024, T))
-LOADS = (((0, T),), ((0, T),), ((0, T),), ((0, T),), QUANT)
+LOADS = (((0, T),), ((0, T),), ((0, 640), (640, T)), ((0, T),), QUANT)
 ROUNDING = (
     (("vector", 512, T), ("scalar", 0, 512)),
     (("vector", 0, 512), ("vector", 512, 640), ("scalar", 640, 1024), ("scalar", 1024, T)),
-    (("vector", 512, 736), ("scalar", 0, 512), ("scalar", 736, 1024), ("gpsimd", 1024, T)),
-    (("vector", 512, 832), ("scalar", 0, 512), ("scalar", 832, 1024), ("gpsimd", 1024, T)),
+    (("scalar", 0, 512), ("scalar", 512, 640), ("scalar", 640, 1024), ("scalar", 1024, T)),
+    (("vector", 0, 512), ("vector", 512, 640), ("scalar", 640, 1024), ("scalar", 1024, T)),
     (("scalar", 0, 512), ("vector", 832, 1024), ("scalar", 512, 832), ("vector", 1152, T), ("scalar", 1024, 1152)),
 )
 
@@ -49,8 +49,10 @@ WORD_LOADS = (
 )
 GROUPS = ((0, 2), (2, E))
 PLANES = [(e1 - e0) * (A4 + A8) for e0, e1 in GROUPS]
+LAST_LOAD = (None, "raw1", "raw2_640", "raw3", "raw4")
 GATE_AT, B_AT = P - 2, P - 1
-VECTOR_SCATTERS = ((256, 512), (512, 1024))
+FIRST = 160
+VECTOR_SCATTERS = ((FIRST, 512), (512, 1024))
 W4_BYTES, W8_BYTES = A4 * 2 * N, A8 * 4 * N
 PAIR_BYTES = 2 * (W4_BYTES + W8_BYTES)
 
@@ -78,15 +80,12 @@ def tile_moe_two_lin_silu_kernel(
         offs_sb = lists.tile([P, S // 16], U16, name="offs_sb")
         dst_sb = lists.tile([P, S // 16], U16, name="dst_sb")
         ident = tile("ident", [P, P], F32)
-        gate_first = tile("gate_first", [P, PAIR], F32)
-        gate_rest = tile("gate_rest", [P, S - PAIR], F32)
+        gate_first = tile("gate_first", [P, FIRST], F32, room=8 * PAIR)
+        gate_rest = tile("gate_rest", [P, S - FIRST], F32)
         window = tile("window", [P, T], F32)
         codes = [tile(f"codes{i}", [P, T], U32) for i in range(len(PASSES))]
         windows = [whole[:] for whole in codes]
-        tile_room = 2048 + 4 * PACK * T
-        place["around_planes0"] = place["free"]
-        place["free"] = place["free"] + tile_room
-        planes = [tile("planes0", [P, T + SPARE], U8, on="around_planes0", at=1280), tile("planes1", [P, T + SPARE], U8)]
+        planes = [tile("planes0", [P, T + SPARE], U8, room=4 * PACK * T), tile("planes1", [P, T + SPARE], U8)]
         slot_codes = [tile(f"slot_codes{i}", [P, S - C], U32) for i in range(LAST)]
         held_codes = []
         early_plane = tile("early_plane", [P, S], U8)
@@ -126,8 +125,6 @@ def tile_moe_two_lin_silu_kernel(
             views = (into.rearrange("p (c i) t -> p c t i", i=4), rows.rearrange("p t (c i) -> p c t i", i=4))
             if engine == "vector":
                 nc.vector.tensor_copy(*views)
-            elif engine == "gpsimd":
-                nc.gpsimd.tensor_copy(into, rows.rearrange("p t c -> p c t"))
             else:
                 nc.scalar.activation(*views, ACT.Copy)
 
@@ -202,7 +199,7 @@ def tile_moe_two_lin_silu_kernel(
                 for q in range(4):
                     i = 4 * half + q
                     nc.tensor.transpose(spread[:, q, :], gate_row[:, i : i + 1].to_broadcast([P, P]), ident[:])
-                for into, p0, p1 in ((gate_first, 0, PAIR // E), (gate_rest, PAIR // E, P)):
+                for into, p0, p1 in ((gate_first, 0, FIRST // E), (gate_rest, FIRST // E, P)):
                     nc.scalar.copy(
                         into[:].rearrange("m (p i) -> m p i", i=S // P)[:, :, 4 * half : 4 * half + 4],
                         spread[:, :, p0:p1].rearrange("m q p -> m p q"),
@@ -215,30 +212,16 @@ def tile_moe_two_lin_silu_kernel(
         nc.sync.dma_start(out=flat[B_AT : B_AT + 1, :], in_=b.rearrange("(o n) e -> o (n e)", o=1))
         nc.sync.dma_start(offs_sb[:], offs)
         load_pass(1, slices_of(tile("raw1", [P, PACK * T], F32)))
-        load_pass(2, slices_of(tile("raw2", [P, PACK * T], F32)))
+        load_pass(2, lambda c0, c1: tile(f"raw2_{c0}", [P, PACK * (c1 - c0)], F32)[:, :])
         nc.sync.dma_start(dst_sb[:], dst)
         load_scale_rows(0, w_planes[0])
 
-        def grouped_tiles(i):
-            if i == 2:
-                return {
-                    0: tile("grouped2_0", [P, 512, PACK], BF16),
-                    512: tile("grouped2_512", [P, 512, PACK], BF16, room=2048 + PAIR_BYTES),
-                    1024: tile("grouped2_1024", [P, 256, PACK], BF16, on="around_planes0"),
-                }
-            if i == 3:
-                return {
-                    0: tile("grouped3_0", [P, 1024, PACK], BF16),
-                    1024: tile("grouped3_1024", [P, 256, PACK], BF16, on="grouped2_512"),
-                }
-            return {0: tile(f"grouped{i}_0", [P, T, PACK], BF16)}
-
         for i in range(len(PASSES)):
-            grouped = grouped_tiles(i)
+            grouped = {0: tile(f"grouped{i}_0", [P, T, PACK], BF16)}
             interleave(i, grouped)
             quantize(i, grouped)
             if i > 0:
-                held_codes.append(tile(f"held_codes{i - 1}", [P, C], U32, on=f"raw{i}"))
+                held_codes.append(tile(f"held_codes{i - 1}", [P, C], U32, on=LAST_LOAD[i]))
                 gather(held_codes[i - 1][:], windows[i - 1], S - C, S)
             if i == 0:
                 load_pass(3, slices_of(tile("raw3", [P, PACK * T], F32, on="first_rows1")))
@@ -249,14 +232,14 @@ def tile_moe_two_lin_silu_kernel(
                         out=moved_plane[r:P:32, :].bitcast(I32),
                         in_=early_plane[PASSES[MOVED][3] + r : P : 32, :].bitcast(I32),
                     )
-                load_pass(LAST, slices_of(tile("raw4", [P, PACK * T], F32, on="around_planes0", at=2048)))
+                load_pass(LAST, slices_of(tile("raw4", [P, PACK * T], F32, on="planes0")))
             if i < LAST:
                 gather(slot_codes[i][:], windows[i], 0, S - C)
             if i == 2:
-                staged = tile("staged", [P, PLANES[1], N // 4], I32, on="raw2", at=1024)
+                staged = tile("staged", [P, PLANES[1], N // 4], I32, on="raw2_0")
                 load_scale_rows(1, staged)
                 place_scale_rows(0, w_planes[0], 1)
-                load_pair(0, tile("words0", [P, PAIR_BYTES], U8, on="grouped2_512", at=2048)[:, :])
+                load_pair(0, tile("words0", [P, PAIR_BYTES], U8, on="grouped2_0")[:, :])
             if i == 3:
                 load_pair(1, tile("words1", [P, PAIR_BYTES], U8, on="grouped3_0")[:, :])
                 place_scale_rows(1, staged, 0)
@@ -318,22 +301,20 @@ def tile_moe_two_lin_silu_kernel(
         gather(last_codes[0][:, :PAIR], windows[LAST], 0, PAIR)
         gather(last_codes[0][:, PAIR:], windows[LAST], PAIR, 2 * PAIR)
         gather(last_planes[0][:, PAIR:], planes[1][:], PAIR, 2 * PAIR)
-        y_first = tile("y_first", [P, PAIR], F32, room=8 * PAIR)
-        experts(0, y_first)
-        gated_first = tile("gated_first", [P, PAIR], F32)
-        nc.vector.tensor_tensor(gated_first[:], y_first[:], gate_first[:], MULT)
-        nc.scalar.activation(places(window, 0, PAIR), gated_first[:], ACT.Copy)
+        y = tile("y", [P, S], F32)
+        experts(0, y[:, :PAIR])
+        gated_first = tile("gated_first", [P, FIRST], F32)
+        nc.vector.tensor_tensor(gated_first[:], y[:, :FIRST], gate_first[:], MULT)
+        nc.scalar.activation(places(window, 0, FIRST), gated_first[:], ACT.Copy)
 
-        last_codes[1] = tile("last_codes1", [P, 2 * PAIR], U32, on="y_first")
+        last_codes[1] = tile("last_codes1", [P, 2 * PAIR], U32, on="gate_first")
         last_planes[1] = tile("last_planes1", [P, 2 * PAIR], U8, on="b_first")
         for q in range(2):
             cols = slice(q * PAIR, (q + 1) * PAIR)
             gather(last_planes[1][:, cols], planes[1][:], (2 + q) * PAIR, (3 + q) * PAIR)
             gather(last_codes[1][:, cols], windows[LAST], (2 + q) * PAIR, (3 + q) * PAIR)
-        y_rest = tile("y_rest", [P, S - PAIR], F32)
         for pair in range(1, E // 2):
-            experts(pair, y_rest[:, (pair - 1) * PAIR : pair * PAIR])
+            experts(pair, y[:, pair * PAIR : (pair + 1) * PAIR])
         for j0, j1 in VECTOR_SCATTERS:
-            cols = slice(j0 - PAIR, j1 - PAIR)
-            nc.vector.tensor_tensor(places(window, j0, j1), y_rest[:, cols], gate_rest[:, cols], MULT)
+            nc.vector.tensor_tensor(places(window, j0, j1), y[:, j0:j1], gate_rest[:, j0 - FIRST : j1 - FIRST], MULT)
         nc.sync.dma_start(out=out, in_=window[:])

@@ -51,8 +51,7 @@ GROUPS = ((0, 2), (2, E))
 PLANES = [(e1 - e0) * (A4 + A8) for e0, e1 in GROUPS]
 LAST_LOAD = (None, "raw1", "raw2_640", "raw3", "raw4")
 GATE_AT, B_AT = P - 2, P - 1
-FIRST = 160
-VECTOR_SCATTERS = ((FIRST, 512), (512, 1024))
+VECTOR_SCATTERS = ((256, 512), (512, 1024))
 W4_BYTES, W8_BYTES = A4 * 2 * N, A8 * 4 * N
 PAIR_BYTES = 2 * (W4_BYTES + W8_BYTES)
 
@@ -80,8 +79,8 @@ def tile_moe_two_lin_silu_kernel(
         offs_sb = lists.tile([P, S // 16], U16, name="offs_sb")
         dst_sb = lists.tile([P, S // 16], U16, name="dst_sb")
         ident = tile("ident", [P, P], F32)
-        gate_first = tile("gate_first", [P, FIRST], F32, room=8 * PAIR)
-        gate_rest = tile("gate_rest", [P, S - FIRST], F32)
+        gate_first = tile("gate_first", [P, PAIR], F32)
+        gate_rest = tile("gate_rest", [P, S - PAIR], F32)
         window = tile("window", [P, T], F32)
         codes = [tile(f"codes{i}", [P, T], U32) for i in range(len(PASSES))]
         windows = [whole[:] for whole in codes]
@@ -122,7 +121,7 @@ def tile_moe_two_lin_silu_kernel(
             return lambda c0, c1: whole[:, PACK * c0 : PACK * c1]
 
         def round_and_group(engine, into, rows):
-            views = (into.rearrange("p (c i) t -> p c t i", i=4), rows.rearrange("p t (c i) -> p c t i", i=4))
+            views = (into.rearrange("p (c i) t -> p c t i", i=2), rows.rearrange("p t (c i) -> p c t i", i=2))
             if engine == "vector":
                 nc.vector.tensor_copy(*views)
             else:
@@ -199,7 +198,7 @@ def tile_moe_two_lin_silu_kernel(
                 for q in range(4):
                     i = 4 * half + q
                     nc.tensor.transpose(spread[:, q, :], gate_row[:, i : i + 1].to_broadcast([P, P]), ident[:])
-                for into, p0, p1 in ((gate_first, 0, FIRST // E), (gate_rest, FIRST // E, P)):
+                for into, p0, p1 in ((gate_first, 0, PAIR // E), (gate_rest, PAIR // E, P)):
                     nc.scalar.copy(
                         into[:].rearrange("m (p i) -> m p i", i=S // P)[:, :, 4 * half : 4 * half + 4],
                         spread[:, :, p0:p1].rearrange("m q p -> m p q"),
@@ -301,20 +300,22 @@ def tile_moe_two_lin_silu_kernel(
         gather(last_codes[0][:, :PAIR], windows[LAST], 0, PAIR)
         gather(last_codes[0][:, PAIR:], windows[LAST], PAIR, 2 * PAIR)
         gather(last_planes[0][:, PAIR:], planes[1][:], PAIR, 2 * PAIR)
-        y = tile("y", [P, S], F32)
-        experts(0, y[:, :PAIR])
-        gated_first = tile("gated_first", [P, FIRST], F32)
-        nc.vector.tensor_tensor(gated_first[:], y[:, :FIRST], gate_first[:], MULT)
-        nc.scalar.activation(places(window, 0, FIRST), gated_first[:], ACT.Copy)
+        y_first = tile("y_first", [P, PAIR], F32, room=8 * PAIR)
+        experts(0, y_first)
+        gated_first = tile("gated_first", [P, PAIR], F32)
+        nc.vector.tensor_tensor(gated_first[:], y_first[:], gate_first[:], MULT)
+        nc.scalar.activation(places(window, 0, PAIR), gated_first[:], ACT.Copy)
 
-        last_codes[1] = tile("last_codes1", [P, 2 * PAIR], U32, on="gate_first")
+        last_codes[1] = tile("last_codes1", [P, 2 * PAIR], U32, on="y_first")
         last_planes[1] = tile("last_planes1", [P, 2 * PAIR], U8, on="b_first")
         for q in range(2):
             cols = slice(q * PAIR, (q + 1) * PAIR)
             gather(last_planes[1][:, cols], planes[1][:], (2 + q) * PAIR, (3 + q) * PAIR)
             gather(last_codes[1][:, cols], windows[LAST], (2 + q) * PAIR, (3 + q) * PAIR)
+        y_rest = tile("y_rest", [P, S - PAIR], F32)
         for pair in range(1, E // 2):
-            experts(pair, y[:, pair * PAIR : (pair + 1) * PAIR])
+            experts(pair, y_rest[:, (pair - 1) * PAIR : pair * PAIR])
         for j0, j1 in VECTOR_SCATTERS:
-            nc.vector.tensor_tensor(places(window, j0, j1), y[:, j0:j1], gate_rest[:, j0 - FIRST : j1 - FIRST], MULT)
+            cols = slice(j0 - PAIR, j1 - PAIR)
+            nc.vector.tensor_tensor(places(window, j0, j1), y_rest[:, cols], gate_rest[:, cols], MULT)
         nc.sync.dma_start(out=out, in_=window[:])

@@ -34,7 +34,7 @@ MOVED, LAST = 1, 4
 QUANT = ((0, 512), (512, 1024), (1024, T))
 LOADS = (((0, T),), ((0, T),), ((0, 640), (640, T)), ((0, T),), QUANT)
 ROUNDING = (
-    (("vector", 512, T), ("scalar", 0, 512)),
+    (("vector", 512, 1024), ("vector", 1024, T), ("scalar", 0, 512)),
     (("vector", 0, 512), ("vector", 512, 640), ("scalar", 640, 1024), ("scalar", 1024, T)),
     (("scalar", 0, 512), ("scalar", 512, 640), ("scalar", 640, 1024), ("scalar", 1024, T)),
     (("vector", 0, 512), ("vector", 512, 640), ("scalar", 640, 1024), ("scalar", 1024, T)),
@@ -121,7 +121,7 @@ def tile_moe_two_lin_silu_kernel(
             return lambda c0, c1: whole[:, PACK * c0 : PACK * c1]
 
         def round_and_group(engine, into, rows):
-            views = (into.rearrange("p (c i) t -> p c t i", i=2), rows.rearrange("p t (c i) -> p c t i", i=2))
+            views = (into.rearrange("p (c i) t -> p c t i", i=4), rows.rearrange("p t (c i) -> p c t i", i=4))
             if engine == "vector":
                 nc.vector.tensor_copy(*views)
             else:
@@ -132,11 +132,6 @@ def tile_moe_two_lin_silu_kernel(
             return grouped[start][:, c0 - start : c1 - start, :]
 
         def interleave(i, grouped):
-            if i == 0:
-                for u in range(2):
-                    for engine, c0, c1 in ROUNDING[0]:
-                        round_and_group(engine, grouped[0][:, c0:c1, 2 * u : 2 * u + 2], first_rows[u][:, :, c0:c1])
-                return
             for engine, c0, c1 in ROUNDING[i]:
                 l0 = max(start for start, end in LOADS[i] if start <= c0)
                 round_and_group(engine, columns(grouped, c0, c1), raw[i, l0][:, :, c0 - l0 : c1 - l0])
@@ -204,9 +199,7 @@ def tile_moe_two_lin_silu_kernel(
                         spread[:, :, p0:p1].rearrange("m q p -> m p q"),
                     )
 
-        first_rows = [tile(f"first_rows{u}", [P, 2, T], F32, room=u * 4 * PACK * T) for u in range(2)]
-        for u in range(2):
-            nc.sync.dma_start(out=first_rows[u][:], in_=pass_rows(0)[:, 2 * u : 2 * u + 2, :])
+        load_pass(0, slices_of(tile("raw0", [P, PACK * T], F32)))
         nc.sync.dma_start(out=flat[GATE_AT : GATE_AT + 1, :], in_=gate[0:1, :])
         nc.sync.dma_start(out=flat[B_AT : B_AT + 1, :], in_=b.rearrange("(o n) e -> o (n e)", o=1))
         nc.sync.dma_start(offs_sb[:], offs)
@@ -223,7 +216,7 @@ def tile_moe_two_lin_silu_kernel(
                 held_codes.append(tile(f"held_codes{i - 1}", [P, C], U32, on=LAST_LOAD[i]))
                 gather(held_codes[i - 1][:], windows[i - 1], S - C, S)
             if i == 0:
-                load_pass(3, slices_of(tile("raw3", [P, PACK * T], F32, on="first_rows1")))
+                load_pass(3, slices_of(tile("raw3", [P, PACK * T], F32, on="raw0")))
             if i == MOVED:
                 gather(early_plane[:], planes[0][:], 0, S)
                 for r in range(4):
@@ -308,10 +301,8 @@ def tile_moe_two_lin_silu_kernel(
 
         last_codes[1] = tile("last_codes1", [P, 2 * PAIR], U32, on="y_first")
         last_planes[1] = tile("last_planes1", [P, 2 * PAIR], U8, on="b_first")
-        for q in range(2):
-            cols = slice(q * PAIR, (q + 1) * PAIR)
-            gather(last_planes[1][:, cols], planes[1][:], (2 + q) * PAIR, (3 + q) * PAIR)
-            gather(last_codes[1][:, cols], windows[LAST], (2 + q) * PAIR, (3 + q) * PAIR)
+        gather(last_planes[1][:], planes[1][:], 2 * PAIR, S)
+        gather(last_codes[1][:], windows[LAST], 2 * PAIR, S)
         y_rest = tile("y_rest", [P, S - PAIR], F32)
         for pair in range(1, E // 2):
             experts(pair, y_rest[:, (pair - 1) * PAIR : pair * PAIR])

@@ -121,7 +121,7 @@ def tile_moe_two_lin_silu_kernel(
             return lambda c0, c1: whole[:, PACK * c0 : PACK * c1]
 
         def round_and_group(engine, into, rows):
-            views = (into.rearrange("p (c i) t -> p c t i", i=4), rows.rearrange("p t (c i) -> p c t i", i=4))
+            views = (into.rearrange("p (c i) t -> p c t i", i=8), rows.rearrange("p t (c i) -> p c t i", i=8))
             if engine == "vector":
                 nc.vector.tensor_copy(*views)
             else:

import math
from contextlib import ExitStack

import concourse.mybir as mybir
from concourse.masks import make_identity

K, T, E, C, N = 2560, 1280, 8, 128, 128
K8 = 1024
S = E * C
FLOPS = 2 * K * S * N

F32 = mybir.dt.float32
BF16 = mybir.dt.bfloat16
I32 = mybir.dt.int32
U32 = mybir.dt.uint32
U16 = mybir.dt.uint16
U8 = mybir.dt.uint8
FP8X4 = mybir.dt.float8_e4m3fn_x4
FP4X4 = mybir.dt.float4_e2m1fn_x4
BYTES_OF = {F32: 4, BF16: 2, I32: 4, U32: 4, U8: 1}
ACT = mybir.ActivationFunctionType
MULT = mybir.AluOpType.mult

P = 128
PACK = 4
K_PASS = P * PACK
A8, A4 = 2, 3
PAIR = 2 * C
SPARE = 256

PASSES = (("e2m1", 0, 0, 0), ("e2m1", 1, 0, 4), ("e4m3", 0, 1, 4), ("e4m3", 1, 1, 8), ("e2m1", 2, 1, 0))
MOVED, LAST = 1, 4

QUANT = ((0, 512), (512, 1024), (1024, T))
LOADS = (((0, T),), ((0, T),), ((0, 640), (640, T)), ((0, T),), QUANT)
ROUNDING = (
    (("vector", 512, 1024), ("vector", 1024, T), ("scalar", 0, 512)),
    (("vector", 0, 512), ("vector", 512, 640), ("scalar", 640, 1024), ("scalar", 1024, T)),
    (("scalar", 0, 512), ("scalar", 512, 640), ("scalar", 640, 1024), ("scalar", 1024, T)),
    (("vector", 0, 512), ("vector", 512, 640), ("scalar", 640, 1024), ("scalar", 1024, T)),
    (("scalar", 0, 512), ("vector", 832, 1024), ("scalar", 512, 832), ("vector", 1152, T), ("scalar", 1024, 1152)),
)

WORD_LOADS = (
    (("e2m1", 0, 2), ("e4m3", 0, 2)),
    (("e4m3", 2, 4), ("e2m1", 2, 4)),
    (("e4m3", 4, 6), ("e2m1", 4, 6)),
    (("e4m3", 6, 8), ("e2m1", 6, 7), ("e2m1", 7, 8)),
)
GROUPS = ((0, 2), (2, E))
PLANES = [(e1 - e0) * (A4 + A8) for e0, e1 in GROUPS]
LAST_LOAD = (None, "raw1", "raw2_640", "raw3", "raw4")
GATE_AT, B_AT = P - 2, P - 1
VECTOR_SCATTERS = ((256, 512), (512, 1024))
W4_BYTES, W8_BYTES = A4 * 2 * N, A8 * 4 * N
PAIR_BYTES = 2 * (W4_BYTES + W8_BYTES)


def tile_moe_two_lin_silu_kernel(
    tc, xT, w8_words, w8_scales, w4_words, w4_scales, b, gate, offs, dst, out
):
    nc = tc.nc
    with ExitStack() as ctx:
        keep = ctx.enter_context(tc.tile_pool(name="keep", bufs=1))
        psum = ctx.enter_context(tc.psum_pool(name="psum", bufs=1))

        lists = ctx.enter_context(tc.tile_pool(name="lists", bufs=1))
        place = {"free": 0}

        def tile(name, shape, dtype, on=None, at=0, room=0):
            size = math.prod(shape[1:]) * BYTES_OF[dtype]
            if on is None:
                place[name] = place["free"]
                place["free"] = place["free"] + 64 * -(-max(size, room) // 64)
            else:
                place[name] = place[on] + at
            return keep.tile(shape, dtype, name=name, align_bytes=64, offset=place[name])

        offs_sb = lists.tile([P, S // 16], U16, name="offs_sb")
        dst_sb = lists.tile([P, S // 16], U16, name="dst_sb")
        ident = tile("ident", [P, P], F32)
        gate_first = tile("gate_first", [P, PAIR], F32)
        gate_rest = tile("gate_rest", [P, S - PAIR], F32)
        window = tile("window", [P, T], F32)
        codes = [tile(f"codes{i}", [P, T], U32) for i in range(len(PASSES))]
        windows = [whole[:] for whole in codes]
        planes = [tile("planes0", [P, T + SPARE], U8, room=4 * PACK * T), tile("planes1", [P, T + SPARE], U8)]
        slot_codes = [tile(f"slot_codes{i}", [P, S - C], U32) for i in range(LAST)]
        held_codes = []
        early_plane = tile("early_plane", [P, S], U8)
        moved_plane = tile("moved_plane", [P, S], U8)
        w_planes = [tile(f"w_planes{h}", [P, PLANES[h], N // 4], I32) for h in range(2)]

        flat = tile("flat", [P, S], F32)
        gate_row = tile("gate_row", [P, E], F32)
        b_sb = tile("b_sb", [P, E], F32)
        b_first = tile("b_first", [P, 2], F32, room=2 * PAIR)

        make_identity(nc, ident[:])
        nc.gpsimd.memset(flat[:GATE_AT, :], 0.0)
        for plane in w_planes:
            nc.vector.memset(plane[:], 0)
        for plane in planes:
            nc.gpsimd.memset(plane[:].bitcast(I32), 0)
        nc.gpsimd.memset(moved_plane[:].bitcast(I32), 0)
        nc.vector.memset(window[:], 0.0)

        def pass_rows(i):
            fmt, a, tile_no, first = PASSES[i]
            row = K_PASS * a + (0 if fmt == "e4m3" else K8)
            return xT[row : row + K_PASS, :].rearrange("(p t) c -> p t c", t=PACK)

        raw = {}

        def load_pass(i, into):
            for c0, c1 in LOADS[i]:
                raw[i, c0] = into(c0, c1).rearrange("p (t c) -> p t c", t=PACK)
                nc.sync.dma_start(out=raw[i, c0], in_=pass_rows(i)[:, :, c0:c1])

        def slices_of(whole):
            return lambda c0, c1: whole[:, PACK * c0 : PACK * c1]

        def round_and_group(engine, into, rows):
            views = (into.rearrange("p (c i) t -> p c t i", i=8), rows.rearrange("p t (c i) -> p c t i", i=8))
            if engine == "vector":
                nc.vector.tensor_copy(*views)
            else:
                nc.scalar.activation(*views, ACT.Copy)

        def columns(grouped, c0, c1):
            start = max(at for at in grouped if at <= c0)
            return grouped[start][:, c0 - start : c1 - start, :]

        def interleave(i, grouped):
            for engine, c0, c1 in ROUNDING[i]:
                l0 = max(start for start, end in LOADS[i] if start <= c0)
                round_and_group(engine, columns(grouped, c0, c1), raw[i, l0][:, :, c0 - l0 : c1 - l0])

        def quantize(i, grouped):
            fmt, a, tile_no, first = PASSES[i]
            for c0, c1 in QUANT:
                nc.vector.quantize_mx(
                    out=codes[i][:, c0:c1].bitcast(FP8X4),
                    scales=planes[tile_no][first:P, c0:c1],
                    in_=columns(grouped, c0, c1).rearrange("p c t -> p (c t)"),
                )

        def gather(into, window, s0, s1):
            nc.vector.tensor_copy(into, window.indirect(offs_sb[:, s0 // 16 : s1 // 16]))

        def load_scale_rows(h, into):
            e0, e1 = GROUPS[h]
            for scales, j0, j1 in ((w4_scales, 0, (e1 - e0) * A4), (w8_scales, (e1 - e0) * A4, PLANES[h])):
                rows = scales[e0:e1].rearrange("e a q n -> q (e a) n")
                nc.sync.dma_start(out=into[0:P:8, j0:j1, :], in_=rows.bitcast(I32))

        def place_scale_rows(h, staged, first_row):
            for r in range(first_row, 4):
                nc.sync.dma_start(out=w_planes[h][r:P:32], in_=staged[8 * r : P : 32])

        words = {}

        def load_words(fmt, e0, e1, into):
            if fmt == "e2m1":
                rows, a, width = w4_words.rearrange("e a p n -> p (e a) n"), A4, 2 * N
            else:
                rows, a, width = w8_words.rearrange("e a p n r -> p (e a) (n r)"), A8, 4 * N
            by_pass = into.rearrange("p (j n) -> p j n", n=width)
            nc.sync.dma_start(out=by_pass.bitcast(I32), in_=rows[:, a * e0 : a * e1, :].bitcast(I32))
            for j in range(a * (e1 - e0)):
                words[fmt, e0 + j // a, j % a] = into[:, j * width : (j + 1) * width]

        def load_pair(pair, into):
            at = 0
            for fmt, e0, e1 in WORD_LOADS[pair]:
                width = (e1 - e0) * (W4_BYTES if fmt == "e2m1" else W8_BYTES)
                load_words(fmt, e0, e1, into[:, at : at + width])
                at = at + width

        def turn_rows():
            by_eight = flat[:].rearrange("p (m i) -> p i m", i=E)
            for half in range(2):
                turned = psum.tile([P, 4, P], F32, name="turned", tag=f"bank{E - 4 + half}")
                for q in range(4):
                    nc.tensor.transpose(turned[:, q, :], by_eight[:, 4 * half + q, :], ident[:])
                nc.scalar.copy(gate_row[:, 4 * half : 4 * half + 4], turned[:, :, GATE_AT])
                nc.scalar.copy(b_sb[:, 4 * half : 4 * half + 4], turned[:, :, B_AT])
            nc.scalar.copy(b_first[:], b_sb[:, :2])

        def spread_gate():
            for half in range(2):
                spread = psum.tile([P, 4, P], F32, name="spread", tag=f"bank{E - 2 + half}")
                for q in range(4):
                    i = 4 * half + q
                    nc.tensor.transpose(spread[:, q, :], gate_row[:, i : i + 1].to_broadcast([P, P]), ident[:])
                for into, p0, p1 in ((gate_first, 0, PAIR // E), (gate_rest, PAIR // E, P)):
                    nc.scalar.copy(
                        into[:].rearrange("m (p i) -> m p i", i=S // P)[:, :, 4 * half : 4 * half + 4],
                        spread[:, :, p0:p1].rearrange("m q p -> m p q"),
                    )

        load_pass(0, slices_of(tile("raw0", [P, PACK * T], F32)))
        nc.sync.dma_start(out=flat[GATE_AT : GATE_AT + 1, :], in_=gate[0:1, :])
        nc.sync.dma_start(out=flat[B_AT : B_AT + 1, :], in_=b.rearrange("(o n) e -> o (n e)", o=1))
        nc.sync.dma_start(offs_sb[:], offs)
        load_pass(1, slices_of(tile("raw1", [P, PACK * T], F32)))
        load_pass(2, lambda c0, c1: tile(f"raw2_{c0}", [P, PACK * (c1 - c0)], F32)[:, :])
        nc.sync.dma_start(dst_sb[:], dst)
        load_scale_rows(0, w_planes[0])

        for i in range(len(PASSES)):
            grouped = {0: tile(f"grouped{i}_0", [P, T, PACK], BF16)}
            interleave(i, grouped)
            quantize(i, grouped)
            if i > 0:
                held_codes.append(tile(f"held_codes{i - 1}", [P, C], U32, on=LAST_LOAD[i]))
                gather(held_codes[i - 1][:], windows[i - 1], S - C, S)
            if i == 0:
                load_pass(3, slices_of(tile("raw3", [P, PACK * T], F32, on="raw0")))
            if i == MOVED:
                gather(early_plane[:], planes[0][:], 0, S)
                for r in range(4):
                    nc.sync.dma_start(
                        out=moved_plane[r:P:32, :].bitcast(I32),
                        in_=early_plane[PASSES[MOVED][3] + r : P : 32, :].bitcast(I32),
                    )
                load_pass(LAST, slices_of(tile("raw4", [P, PACK * T], F32, on="planes0")))
            if i < LAST:
                gather(slot_codes[i][:], windows[i], 0, S - C)
            if i == 2:
                staged = tile("staged", [P, PLANES[1], N // 4], I32, on="raw2_0")
                load_scale_rows(1, staged)
                place_scale_rows(0, w_planes[0], 1)
                load_pair(0, tile("words0", [P, PAIR_BYTES], U8, on="grouped2_0")[:, :])
            if i == 3:
                load_pair(1, tile("words1", [P, PAIR_BYTES], U8, on="grouped3_0")[:, :])
                place_scale_rows(1, staged, 0)
        late_words = tile("late_words", [P, 2 * PAIR_BYTES], U8, on="grouped4_0")
        for pair in (2, 3):
            load_pair(pair, late_words[:, (pair - 2) * PAIR_BYTES : (pair - 1) * PAIR_BYTES])
        turn_rows()
        spread_gate()

        acc = {}
        last_codes, last_planes = {}, {}

        def multiply(i, e, opens):
            fmt, a, tile_no, first = PASSES[i]
            cols = slice(e * C, (e + 1) * C)
            half, in_half = e // 4, slice(e % 4 * C, (e % 4 + 1) * C)
            group = int(e >= GROUPS[1][0])
            e0, e1 = GROUPS[group]
            if fmt == "e4m3":
                view, j = FP8X4, (e1 - e0) * A4 + A8 * (e - e0) + a
            else:
                view, j = FP4X4, A4 * (e - e0) + a
            if tile_no == 1:
                plane = last_planes[half][first:P, in_half]
            else:
                plane = moved_plane[:, cols] if i == MOVED else early_plane[:, cols]
            if i == LAST:
                tokens = last_codes[half][:, in_half]
            else:
                tokens = held_codes[i][:] if e == E - 1 else slot_codes[i][:, cols]
            nc.tensor.matmul_mx(
                out=acc[e][:],
                lhsT=words[fmt, e, a].bitcast(view),
                lhsT_scale=w_planes[group][:, j, :].bitcast(U8),
                rhs=tokens.bitcast(FP8X4),
                rhs_scale=plane,
                start=opens,
                stop=(i == LAST),
            )

        def experts(pair, y):
            order = ((0, MOVED), (2, 3), (LAST,)) if pair == 0 else ((2, 3), (0, MOVED, LAST))
            for e in (2 * pair, 2 * pair + 1):
                acc[e] = psum.tile([P, C], F32, name=f"acc{e}", tag=f"bank{e % 2 if pair < 2 else e}")
            for passes in order:
                for e in (2 * pair, 2 * pair + 1):
                    for i in passes:
                        multiply(i, e, i == order[0][0])
            for q in range(2):
                e = 2 * pair + q
                nc.scalar.activation(y[:, q * C : (q + 1) * C], acc[e][:], ACT.Silu, bias=(b_first if pair == 0 else b_sb)[:, e : e + 1])

        def places(window, s0, s1):
            return window[:].indirect(dst_sb[:, s0 // 16 : s1 // 16])

        last_codes[0] = tile("last_codes0", [P, 2 * PAIR], U32)
        last_planes[0] = tile("last_planes0", [P, 2 * PAIR], U8)
        gather(last_planes[0][:, :PAIR], planes[1][:], 0, PAIR)
        gather(last_codes[0][:, :PAIR], windows[LAST], 0, PAIR)
        gather(last_codes[0][:, PAIR:], windows[LAST], PAIR, 2 * PAIR)
        gather(last_planes[0][:, PAIR:], planes[1][:], PAIR, 2 * PAIR)
        y_first = tile("y_first", [P, PAIR], F32, room=8 * PAIR)
        experts(0, y_first)
        gated_first = tile("gated_first", [P, PAIR], F32)
        nc.vector.tensor_tensor(gated_first[:], y_first[:], gate_first[:], MULT)
        nc.scalar.activation(places(window, 0, PAIR), gated_first[:], ACT.Copy)

        last_codes[1] = tile("last_codes1", [P, 2 * PAIR], U32, on="y_first")
        last_planes[1] = tile("last_planes1", [P, 2 * PAIR], U8, on="b_first")
        gather(last_planes[1][:], planes[1][:], 2 * PAIR, S)
        gather(last_codes[1][:], windows[LAST], 2 * PAIR, S)
        y_rest = tile("y_rest", [P, S - PAIR], F32)
        for pair in range(1, E // 2):
            experts(pair, y_rest[:, (pair - 1) * PAIR : pair * PAIR])
        for j0, j1 in VECTOR_SCATTERS:
            cols = slice(j0 - PAIR, j1 - PAIR)
            nc.vector.tensor_tensor(places(window, j0, j1), y_rest[:, cols], gate_rest[:, cols], MULT)
        nc.sync.dma_start(out=out, in_=window[:])
